import numpy as np
import ml_dtypes


def mxq(x, axis, fmt="e4m3"):
    dtype, down = {"e4m3": (ml_dtypes.float8_e4m3fn, 7), "e5m2": (ml_dtypes.float8_e5m2, 14)}[fmt]
    v = np.moveaxis(np.asarray(x, np.float32).astype(ml_dtypes.bfloat16).astype(np.float64), axis, -1)
    blocks = v.reshape(v.shape[:-1] + (-1, 32))
    amax = np.abs(blocks).max(-1, keepdims=True)
    byte = np.maximum(np.where(amax > 0, np.frexp(amax)[1] - 1 + 127, 0) - down, 1)
    scale = np.exp2(byte - 127.0)
    codes = (blocks / scale).astype(np.float32).astype(dtype).astype(np.float64)
    return np.moveaxis((codes * scale).reshape(v.shape), -1, axis)


WIDE = False


def mx_kscale(k):
    if not WIDE:
        return np.ones(k)
    levels = np.array([18, -18])
    if k % 512:
        return np.exp2(np.random.permutation(np.resize(levels, k // 32))).repeat(32)
    a = np.empty((k // 512, 16))
    for p in range(k // 512):
        a[p, :8] = np.random.permutation(np.resize(levels, 8))
        for g in range(8):
            far = levels[np.abs(levels - a[p, g]) >= 10]
            a[p, g + 8] = far[np.random.randint(len(far))]
    return np.exp2(a.ravel()).repeat(32)


def f64(x):
    return np.asarray(x).astype(np.float64)


def striped(idx):
    return np.tile(np.asarray(idx).reshape(-1, 16).T, (8, 1)).astype(np.uint16)


def unstriped(offs):
    return offs[:16].T.reshape(-1).astype(np.int64)

def planes(y):
    n, m = y.shape
    v = y.astype(np.float32).astype(ml_dtypes.bfloat16).astype(np.float64).reshape(n // 32, 32, m)
    top = np.abs(v).max(1)
    byte = np.clip(np.where(top > 0, np.frexp(top)[1] - 1 + 127 - 7, 1), 1, 254)
    codes = (v * np.exp2(127.0 - byte)[:, None, :]).reshape(n, m).astype(np.float32).astype(ml_dtypes.float8_e4m3fn).view(np.uint8)
    words = codes.reshape(n // 512, 128, 4, m).transpose(0, 1, 3, 2)
    return np.ascontiguousarray(words), np.ascontiguousarray(byte.astype(np.uint8).reshape(n // 512, 16, m))


B, N, T, D, R = 1, 512, 2048, 512, 1024


def setup_inputs():
    n = np.random.standard_normal
    idx = np.random.permutation(T)[:B * N]
    s = mx_kscale(D)[:, None]
    u = np.ones(T)
    u[idx] = mx_kscale(B * N)
    r = np.random.uniform(0.5, 2.0, T) * u
    x = n((B, D, R))
    return {
        "xT": (x * s).astype(np.float32),
        "wT": (n((D, T)) * (1.00 / np.sqrt(D)) / s / r).astype(np.float32),
        "y": (2 * np.random.randint(0, 2, (B, R, N)) - 1).astype(np.float32),
        "wt": (np.random.uniform(0.5, 1.5, (B, R, 1)) * 1.0 / np.sqrt(R)).astype(np.float32),
        "ts": np.tile(r, (128, 1)).astype(np.float32),
        "offs": striped(idx),
    }


def reference(xT, wT, y, wt, ts, offs):
    idx = unstriped(offs)
    pick = lambda x: x[:, idx].reshape(x.shape[0], B, N).transpose(1, 0, 2)
    w = pick(f64(wT))
    a = mxq(f64(xT), 1, "e4m3").transpose(0, 2, 1) @ mxq(w, 1, "e4m3")
    ts_ = pick(f64(ts))[:, :1, :]
    a = a * ts_
    g = -f64(wt) * f64(y) * np.maximum(1.0 - f64(y) * a, 0.0)
    g = g * ts_
    gx = mxq(g, 2, "e5m2") @ mxq(w, 2, "e4m3").transpose(0, 2, 1)
    out_0 = gx
    return (out_0,) + planes(out_0[0])

@@ -1,0 +1,191 @@
+from contextlib import ExitStack
+
+import concourse.mybir as mybir
+from concourse.masks import make_identity
+
+N, T, D, R = 512, 2048, 512, 1024
+FLOPS = 2 * 2 * R * N * D
+
+F32 = mybir.dt.float32
+BF16 = mybir.dt.bfloat16
+I32 = mybir.dt.int32
+U32 = mybir.dt.uint32
+U16 = mybir.dt.uint16
+U8 = mybir.dt.uint8
+E4M3 = mybir.dt.float8_e4m3fn_x4
+E5M2 = mybir.dt.float8_e5m2_x4
+ALU = mybir.AluOpType
+ACT = mybir.ActivationFunctionType
+
+P = 128
+PACK = 4
+PASS = P * PACK
+PASSES = R // PASS
+TILES = PASSES * PACK
+
+
+def tile_attend_gsqh_pl_x_ts_kernel(tc, xT, wT, y, wt, ts, offs, out_0, out_1, out_2):
+    nc = tc.nc
+    with ExitStack() as ctx:
+        keep = ctx.enter_context(tc.tile_pool(name="keep", bufs=1))
+        work = ctx.enter_context(tc.tile_pool(name="work", bufs=3))
+        psum = ctx.enter_context(tc.psum_pool(name="psum", bufs=1))
+
+        offsets = keep.tile([P, N // 16], U16, name="offsets")
+        nc.sync.dma_start(offsets[:], offs)
+
+        ts_row = keep.tile([P, T], F32, name="ts_row")
+        nc.vector.memset(ts_row[:], 0.0)
+        ident = keep.tile([P, P], F32, name="ident")
+        make_identity(nc, ident[:])
+
+        w_rows = wT.rearrange("(p j) c -> j p c", j=PACK)
+        w_plane = [keep.tile([P, T], F32, name=f"w_plane{j}") for j in range(PACK)]
+        for j in range(PACK):
+            nc.sync.dma_start(w_plane[j][:], w_rows[j])
+            if j == 0:
+                nc.sync.dma_start(ts_row[0:1, :], ts[0:1, :])
+
+        x_rows = xT[0].rearrange("(p j) r -> p j r", j=PACK)
+        y_rows = y[0].rearrange("(o p t) n -> o p t n", p=P, t=PACK)
+        x_raw = [keep.tile([P, PACK, PASS // 2], F32, name=f"x_raw{c}") for c in range(2 * PASSES)]
+        y_raw = [keep.tile([P, 2, N], F32, name=f"y_raw{k}") for k in range(TILES // 2)]
+        wt_raw = keep.tile([P, PASSES, PACK], F32, name="wt_raw")
+        nc.scalar.dma_start(wt_raw[:], wt[0].rearrange("(o p t) one -> p o (t one)", p=P, t=PACK))
+        for o in range(PASSES):
+            for c in range(2 * o, 2 * o + 2):
+                nc.sync.dma_start(x_raw[c][:], x_rows[:, :, c * PASS // 2 : (c + 1) * PASS // 2])
+            for half in range(2):
+                nc.sync.dma_start(y_raw[2 * o + half][:], y_rows[o, :, 2 * half : 2 * half + 2, :])
+
+        neg_wt = keep.tile([P, TILES], F32, name="neg_wt")
+        nc.vector.tensor_scalar(neg_wt[:], wt_raw[:].rearrange("p o t -> p (o t)"), -1.0, None, ALU.mult)
+
+        ts_listed = keep.tile([P, N], F32, name="ts_listed")
+        nc.vector.tensor_copy(ts_listed[:], ts_row[:].indirect(offsets[:]))
+        ts_turn = psum.tile([P, PACK, P], F32, name="ts_turn", tag="bank5")
+        for c in range(PACK):
+            nc.tensor.transpose(ts_turn[:, c, :], ts_listed[:, c * P : (c + 1) * P], ident[:])
+        ts_col = keep.tile([P, PACK], F32, name="ts_col")
+        nc.scalar.copy(ts_col[:], ts_turn[:, :, 0])
+        ts_all = psum.tile([P, N], F32, name="ts_all", tag="bank7")
+        for c in range(PACK):
+            nc.tensor.transpose(ts_all[:, c * P : (c + 1) * P], ts_col[:, c : c + 1].to_broadcast([P, P]), ident[:])
+
+        w_listed = keep.tile([P, N, PACK], BF16, name="w_listed", align_bytes=64)
+        w_words = w_listed[:].rearrange("p n j -> p (n j)").bitcast(F32).rearrange("p (a s e u) -> p u a e s", a=2, e=2, u=2)
+        w_turned = keep.tile([P, P, 2, 2, PACK], BF16, name="w_turned", align_bytes=64)
+        wd_codes = keep.tile([P, N], U32, name="wd_codes", align_bytes=64)
+        wd_scales = keep.tile([P, N], U8, name="wd_scales", align_bytes=64)
+        wn_codes = keep.tile([P, D], U32, name="wn_codes", align_bytes=64)
+        wn_scales = keep.tile([P, D], U8, name="wn_scales", align_bytes=64)
+
+        def gather_w(j):
+            nc.vector.tensor_copy(w_listed[:, :, j].rearrange("p (a s e) -> p s a e", a=2, e=2), w_plane[j][:].indirect(offsets[:]))
+
+        def turn_w(u):
+            bank = psum.tile([P, PACK * P], F32, name=f"w_turn{u}", tag=("bank6", "bank0")[u])
+            for t in range(PACK):
+                nc.tensor.transpose(bank[:, t * P : (t + 1) * P], w_words[:, u, t // 2, t % 2, :], ident[:])
+            nc.scalar.copy(w_turned[:, :, u, :, :], bank[:].bitcast(BF16).rearrange("s (t p e) -> s p e t", t=PACK, e=2))
+
+        x_dealt = [keep.tile([P, PACK, P, PACK], BF16, name=f"x_dealt{o}", align_bytes=64) for o in range(PASSES)]
+        x_codes = [keep.tile([P, PASS], U32, name=f"x_codes{o}", align_bytes=64) for o in range(PASSES)]
+        x_scales = [keep.tile([P, PASS], U8, name=f"x_scales{o}", align_bytes=64) for o in range(PASSES)]
+
+        def deal_x(c, copy):
+            o, half = divmod(c, 2)
+            copy(x_dealt[o][:, :, half * P // 2 : (half + 1) * P // 2, :].rearrange("p t m j -> p m t j"),
+                 x_raw[c][:].rearrange("p j (m t) -> p m t j", t=PACK))
+
+        def quantise_x(o):
+            nc.vector.quantize_mx(x_codes[o][:].bitcast(E4M3), x_scales[o][:], x_dealt[o][:].rearrange("p t m j -> p (t m j)"))
+
+        grad_rows = [keep.tile([P, PACK, D], F32, name=f"grad_rows{o}") for o in range(PASSES)]
+        out_rows = out_0[0].rearrange("(o p t) d -> o p t d", p=P, t=PACK)
+        signed, margin, h_words, h_ops = {}, {}, {}, {}
+
+        def sign_scales(k):
+            signed[k] = work.tile([P, N], F32, name="signed", tag="signed", bufs=4)
+            nc.vector.tensor_tensor(signed[k][:].rearrange("r (a s e) -> r s a e", a=2, e=2),
+                                    y_raw[k // 2][:, k % 2, :].rearrange("r (s a e) -> r s a e", a=2, e=2),
+                                    ts_all[:].rearrange("r (s a e) -> r s a e", a=2, e=2), ALU.mult)
+
+        def score(k):
+            o, t = divmod(k, PACK)
+            bank = psum.tile([P, N], F32, name="scores", tag=f"bank{k % 3}")
+            cols = slice(t * P, (t + 1) * P)
+            nc.tensor.matmul_mx(bank[:], lhsT=x_codes[o][:, cols].bitcast(E4M3), lhsT_scale=x_scales[o][:, cols],
+                                rhs=wd_codes[:].bitcast(E4M3), rhs_scale=wd_scales[:], start=True, stop=True)
+            ya = work.tile([P, N], F32, name="ya", tag="ya")
+            nc.vector.tensor_tensor(ya[:], bank[:], signed[k][:], ALU.mult)
+            margin[k] = work.tile([P, N], F32, name="margin", tag="margin")
+            nc.scalar.activation(margin[k][:], ya[:], ACT.Relu, bias=1.0, scale=-1.0)
+
+        def weigh(k):
+            h = work.tile([P, N], BF16, name="h", tag="h")
+            nc.vector.scalar_tensor_tensor(h[:], margin[k][:], neg_wt[:, k : k + 1], signed[k][:], ALU.mult, ALU.mult)
+            words = h[:].bitcast(F32).rearrange("r (u s) -> r u s", u=2)
+            bank = psum.tile([P, 2, P], F32, name="h_turn", tag=f"bank{3 + k % 2}")
+            for u in range(2):
+                nc.tensor.transpose(bank[:, u, :], words[:, u, :], ident[:])
+            h_words[k] = work.tile([P, P, 2], F32, name="h_words", tag="h_words", align_bytes=64)
+            nc.scalar.copy(h_words[k][:], bank[:].rearrange("s u r -> s r u"))
+
+        def gradient(k):
+            o, t = divmod(k, PACK)
+            codes = work.tile([P, P], U32, name="h_codes", tag="h_codes", align_bytes=64)
+            scales = work.tile([P, P], U8, name="h_scales", tag="h_scales", align_bytes=64)
+            nc.vector.quantize_mx(codes[:].bitcast(E5M2), scales[:], h_words[k][:].rearrange("s r u -> s (r u)").bitcast(BF16))
+            bank = psum.tile([P, D], F32, name="grad", tag=f"bank{5 + k % 2}")
+            nc.tensor.matmul_mx(bank[:], lhsT=codes[:].bitcast(E5M2), lhsT_scale=scales[:],
+                                rhs=wn_codes[:].bitcast(E4M3), rhs_scale=wn_scales[:], start=True, stop=True)
+            nc.scalar.copy(grad_rows[o][:, t, :], bank[:])
+            nc.sync.dma_start(out_rows[o, :, t, :], grad_rows[o][:, t, :])
+
+        def planes(o):
+            codes = keep.tile([P, D], U32, name=f"out_codes{o}", align_bytes=64)
+            scales = keep.tile([P, D], U8, name=f"out_scales{o}", align_bytes=64)
+            half = D // 2
+            for c in range(2):
+                cols = slice(c * half, (c + 1) * half)
+                woven = keep.tile([P, half, PACK], BF16, name=f"woven{o}{c}", align_bytes=64)
+                last = o == PASSES - 1
+                pieces = 1 if last else 2
+                copy = nc.vector.tensor_copy if last and c == 0 else nc.scalar.copy
+                width = half // pieces
+                for i in range(pieces):
+                    copy(woven[:, i * width : (i + 1) * width, :].rearrange("p (c i) t -> p c t i", i=4),
+                         grad_rows[o][:, :, c * half + i * width : c * half + (i + 1) * width].rearrange("p t (c i) -> p c t i", i=4))
+                nc.vector.quantize_mx(codes[:, cols].bitcast(E4M3), scales[:, cols], woven[:].rearrange("p d t -> p (d t)"))
+            nc.sync.dma_start(out_1[o].rearrange("p d l -> p (d l)").bitcast(I32), codes[:].bitcast(I32))
+            for q in range(4):
+                queue = nc.sync if q % 2 == 0 or not last else nc.scalar
+                queue.dma_start(out_2[o, 4 * q : 4 * q + 4, :].bitcast(I32), scales[32 * q : 32 * q + 4, :].bitcast(I32))
+
+        gather_w(0)
+        gather_w(1)
+        turn_w(0)
+        gather_w(2)
+        gather_w(3)
+        nc.vector.quantize_mx(wd_codes[:].bitcast(E4M3), wd_scales[:], w_listed[:].rearrange("p n j -> p (n j)"))
+        deal_x(0, nc.scalar.copy)
+        deal_x(1, nc.vector.tensor_copy)
+        quantise_x(0)
+        sign_scales(0)
+        for k in range(TILES):
+            score(k)
+            if k == 0:
+                turn_w(1)
+            if k + 1 < TILES:
+                sign_scales(k + 1)
+            weigh(k)
+            if k == 0:
+                nc.vector.quantize_mx(wn_codes[:].bitcast(E4M3), wn_scales[:], w_turned[:].rearrange("s p u e t -> s (p u e t)"))
+            gradient(k)
+            if k in (1, 2):
+                deal_x(k + 1, nc.scalar.copy)
+            if k == 2:
+                quantise_x(1)
+        for o in range(PASSES):
+            planes(o)

@@ -48,15 +48,28 @@ def tile_attend_gsqh_pl_x_ts_kernel(tc, xT, wT, y, wt, ts, offs, out_0, out_1, o
 
         x_rows = xT[0].rearrange("(p j) r -> p j r", j=PACK)
         y_rows = y[0].rearrange("(o p t) n -> o p t n", p=P, t=PACK)
-        x_raw = [keep.tile([P, PACK, PASS // 2], F32, name=f"x_raw{c}") for c in range(2 * PASSES)]
-        y_raw = [keep.tile([P, 2, N], F32, name=f"y_raw{k}") for k in range(TILES // 2)]
+        x_first = [keep.tile([P, PACK, PASS // 2], F32, name=f"x_first{c}") for c in range(2)]
+        x_second = keep.tile([P, PACK, PASS], F32, name="x_second")
+        x_halves = [x_first[0][:], x_first[1][:], x_second[:, :, : PASS // 2], x_second[:, :, PASS // 2 :]]
         wt_raw = keep.tile([P, PASSES, PACK], F32, name="wt_raw")
         nc.scalar.dma_start(wt_raw[:], wt[0].rearrange("(o p t) one -> p o (t one)", p=P, t=PACK))
-        for o in range(PASSES):
-            for c in range(2 * o, 2 * o + 2):
-                nc.sync.dma_start(x_raw[c][:], x_rows[:, :, c * PASS // 2 : (c + 1) * PASS // 2])
-            for half in range(2):
-                nc.sync.dma_start(y_raw[2 * o + half][:], y_rows[o, :, 2 * half : 2 * half + 2, :])
+        y_tile = {}
+
+        def load_y(k, count):
+            o, t = divmod(k, PACK)
+            rows = keep.tile([P, count, N], F32, name=f"y_rows{k}")
+            nc.sync.dma_start(rows[:], y_rows[o, :, t : t + count, :])
+            for i in range(count):
+                y_tile[k + i] = rows[:, i, :]
+
+        for c in range(2):
+            nc.sync.dma_start(x_first[c][:], x_rows[:, :, c * PASS // 2 : (c + 1) * PASS // 2])
+        load_y(0, 1)
+        load_y(1, 1)
+        load_y(2, 2)
+        nc.sync.dma_start(x_second[:], x_rows[:, :, PASS:])
+        load_y(4, 2)
+        load_y(6, 2)
 
         neg_wt = keep.tile([P, TILES], F32, name="neg_wt")
         nc.vector.tensor_scalar(neg_wt[:], wt_raw[:].rearrange("p o t -> p (o t)"), -1.0, None, ALU.mult)
@@ -96,10 +109,12 @@ def tile_attend_gsqh_pl_x_ts_kernel(tc, xT, wT, y, wt, ts, offs, out_0, out_1, o
         def deal_x(c, copy):
             o, half = divmod(c, 2)
             copy(x_dealt[o][:, :, half * P // 2 : (half + 1) * P // 2, :].rearrange("p t m j -> p m t j"),
-                 x_raw[c][:].rearrange("p j (m t) -> p m t j", t=PACK))
+                 x_halves[c].rearrange("p j (m t) -> p m t j", t=PACK))
 
-        def quantise_x(o):
-            nc.vector.quantize_mx(x_codes[o][:].bitcast(E4M3), x_scales[o][:], x_dealt[o][:].rearrange("p t m j -> p (t m j)"))
+        def quantise_x(o, t, count):
+            cols = slice(t * P, (t + count) * P)
+            nc.vector.quantize_mx(x_codes[o][:, cols].bitcast(E4M3), x_scales[o][:, cols],
+                                  x_dealt[o][:, t : t + count].rearrange("p t m j -> p (t m j)"))
 
         grad_rows = [keep.tile([P, PACK, D], F32, name=f"grad_rows{o}") for o in range(PASSES)]
         out_rows = out_0[0].rearrange("(o p t) d -> o p t d", p=P, t=PACK)
@@ -108,7 +123,7 @@ def tile_attend_gsqh_pl_x_ts_kernel(tc, xT, wT, y, wt, ts, offs, out_0, out_1, o
         def sign_scales(k):
             signed[k] = work.tile([P, N], F32, name="signed", tag="signed", bufs=4)
             nc.vector.tensor_tensor(signed[k][:].rearrange("r (a s e) -> r s a e", a=2, e=2),
-                                    y_raw[k // 2][:, k % 2, :].rearrange("r (s a e) -> r s a e", a=2, e=2),
+                                    y_tile[k].rearrange("r (s a e) -> r s a e", a=2, e=2),
                                     ts_all[:].rearrange("r (s a e) -> r s a e", a=2, e=2), ALU.mult)
 
         def score(k):
@@ -117,13 +132,13 @@ def tile_attend_gsqh_pl_x_ts_kernel(tc, xT, wT, y, wt, ts, offs, out_0, out_1, o
             cols = slice(t * P, (t + 1) * P)
             nc.tensor.matmul_mx(bank[:], lhsT=x_codes[o][:, cols].bitcast(E4M3), lhsT_scale=x_scales[o][:, cols],
                                 rhs=wd_codes[:].bitcast(E4M3), rhs_scale=wd_scales[:], start=True, stop=True)
-            ya = work.tile([P, N], F32, name="ya", tag="ya")
+            ya = work.tile([P, N], F32, name="ya", tag="ya") if k < TILES - 1 else keep.tile([P, N], F32, name="ya_last", tag="late0", align_bytes=64)
             nc.vector.tensor_tensor(ya[:], bank[:], signed[k][:], ALU.mult)
             margin[k] = work.tile([P, N], F32, name="margin", tag="margin")
             nc.scalar.activation(margin[k][:], ya[:], ACT.Relu, bias=1.0, scale=-1.0)
 
         def weigh(k):
-            h = work.tile([P, N], BF16, name="h", tag="h")
+            h = work.tile([P, N], BF16, name="h", tag="h") if k < TILES - 1 else keep.tile([P, N], BF16, name="h_last", tag="late1", align_bytes=64)
             nc.vector.scalar_tensor_tensor(h[:], margin[k][:], neg_wt[:, k : k + 1], signed[k][:], ALU.mult, ALU.mult)
             words = h[:].bitcast(F32).rearrange("r (u s) -> r u s", u=2)
             bank = psum.tile([P, 2, P], F32, name="h_turn", tag=f"bank{3 + k % 2}")
@@ -140,28 +155,42 @@ def tile_attend_gsqh_pl_x_ts_kernel(tc, xT, wT, y, wt, ts, offs, out_0, out_1, o
             bank = psum.tile([P, D], F32, name="grad", tag=f"bank{5 + k % 2}")
             nc.tensor.matmul_mx(bank[:], lhsT=codes[:].bitcast(E5M2), lhsT_scale=scales[:],
                                 rhs=wn_codes[:].bitcast(E4M3), rhs_scale=wn_scales[:], start=True, stop=True)
-            nc.scalar.copy(grad_rows[o][:, t, :], bank[:])
+            pieces = 2 if k == TILES - 1 else 1
+            for i in range(pieces):
+                cols = slice(i * D // pieces, (i + 1) * D // pieces)
+                nc.scalar.copy(grad_rows[o][:, t, cols], bank[:, cols])
             nc.sync.dma_start(out_rows[o, :, t, :], grad_rows[o][:, t, :])
+
+        out_scales = keep.tile([P, PASSES, D], U8, name="out_scales", align_bytes=64)
+
+        def weave(copy, woven, o, first, start, stop):
+            copy(woven[:, start - first : stop - first, :].rearrange("p (c i) t -> p c t i", i=4),
+                 grad_rows[o][:, :, start:stop].rearrange("p t (c i) -> p c t i", i=4))
 
         def planes(o):
             codes = keep.tile([P, D], U32, name=f"out_codes{o}", align_bytes=64)
-            scales = keep.tile([P, D], U8, name=f"out_scales{o}", align_bytes=64)
+            words_out = out_1[o].rearrange("p d l -> p (d l)").bitcast(I32)
             half = D // 2
+            last = o == PASSES - 1
+            woven = [keep.tile([P, half, PACK], BF16, name=f"woven{o}{c}", tag=f"woven{c}" if last else f"late{c}", align_bytes=64)
+                     for c in range(2)]
+            if last:
+                weave(nc.vector.tensor_copy, woven[0], o, 0, 0, half)
+                weave(nc.scalar.copy, woven[1], o, half, half + half // 2, D)
+                weave(nc.vector.tensor_copy, woven[1], o, half, half, half + half // 2)
+            else:
+                for c in range(2):
+                    weave(nc.scalar.copy, woven[c], o, c * half, c * half, (c + 1) * half)
             for c in range(2):
                 cols = slice(c * half, (c + 1) * half)
-                woven = keep.tile([P, half, PACK], BF16, name=f"woven{o}{c}", align_bytes=64)
-                last = o == PASSES - 1
-                pieces = 1 if last else 2
-                copy = nc.vector.tensor_copy if last and c == 0 else nc.scalar.copy
-                width = half // pieces
-                for i in range(pieces):
-                    copy(woven[:, i * width : (i + 1) * width, :].rearrange("p (c i) t -> p c t i", i=4),
-                         grad_rows[o][:, :, c * half + i * width : c * half + (i + 1) * width].rearrange("p t (c i) -> p c t i", i=4))
-                nc.vector.quantize_mx(codes[:, cols].bitcast(E4M3), scales[:, cols], woven[:].rearrange("p d t -> p (d t)"))
-            nc.sync.dma_start(out_1[o].rearrange("p d l -> p (d l)").bitcast(I32), codes[:].bitcast(I32))
+                nc.vector.quantize_mx(codes[:, cols].bitcast(E4M3), out_scales[:, o, cols], woven[c][:].rearrange("p d t -> p (d t)"))
+            nc.sync.dma_start(words_out, codes[:].bitcast(I32))
+
+        def store_scales():
             for q in range(4):
-                queue = nc.sync if q % 2 == 0 or not last else nc.scalar
-                queue.dma_start(out_2[o, 4 * q : 4 * q + 4, :].bitcast(I32), scales[32 * q : 32 * q + 4, :].bitcast(I32))
+                queue = nc.scalar if q % 2 == 0 else nc.sync
+                queue.dma_start(out_2[:, 4 * q : 4 * q + 4, :].rearrange("o i d -> i o d").bitcast(I32),
+                                out_scales[32 * q : 32 * q + 4].bitcast(I32))
 
         gather_w(0)
         gather_w(1)
@@ -171,12 +200,14 @@ def tile_attend_gsqh_pl_x_ts_kernel(tc, xT, wT, y, wt, ts, offs, out_0, out_1, o
         nc.vector.quantize_mx(wd_codes[:].bitcast(E4M3), wd_scales[:], w_listed[:].rearrange("p n j -> p (n j)"))
         deal_x(0, nc.scalar.copy)
         deal_x(1, nc.vector.tensor_copy)
-        quantise_x(0)
+        quantise_x(0, 0, 1)
         sign_scales(0)
         for k in range(TILES):
             score(k)
             if k == 0:
                 turn_w(1)
+            if k < 2:
+                quantise_x(0, k + 1, k + 1)
             if k + 1 < TILES:
                 sign_scales(k + 1)
             weigh(k)
@@ -186,6 +217,7 @@ def tile_attend_gsqh_pl_x_ts_kernel(tc, xT, wT, y, wt, ts, offs, out_0, out_1, o
             if k in (1, 2):
                 deal_x(k + 1, nc.scalar.copy)
             if k == 2:
-                quantise_x(1)
+                quantise_x(1, 0, PACK)
         for o in range(PASSES):
             planes(o)
+        store_scales()

@@ -32,7 +32,6 @@ def tile_attend_gsqh_pl_x_ts_kernel(tc, xT, wT, y, wt, ts, offs, out_0, out_1, o
         psum = ctx.enter_context(tc.psum_pool(name="psum", bufs=1))
 
         offsets = keep.tile([P, N // 16], U16, name="offsets")
-        nc.sync.dma_start(offsets[:], offs)
 
         ts_row = keep.tile([P, T], F32, name="ts_row")
         nc.vector.memset(ts_row[:], 0.0)
@@ -44,13 +43,13 @@ def tile_attend_gsqh_pl_x_ts_kernel(tc, xT, wT, y, wt, ts, offs, out_0, out_1, o
         for j in range(PACK):
             nc.sync.dma_start(w_plane[j][:], w_rows[j])
             if j == 0:
+                nc.sync.dma_start(offsets[:], offs)
                 nc.sync.dma_start(ts_row[0:1, :], ts[0:1, :])
 
         x_rows = xT[0].rearrange("(p j) r -> p j r", j=PACK)
         y_rows = y[0].rearrange("(o p t) n -> o p t n", p=P, t=PACK)
         x_first = [keep.tile([P, PACK, PASS // 2], F32, name=f"x_first{c}") for c in range(2)]
         x_second = keep.tile([P, PACK, PASS], F32, name="x_second")
-        x_halves = [x_first[0][:], x_first[1][:], x_second[:, :, : PASS // 2], x_second[:, :, PASS // 2 :]]
         wt_raw = keep.tile([P, PASSES, PACK], F32, name="wt_raw")
         nc.scalar.dma_start(wt_raw[:], wt[0].rearrange("(o p t) one -> p o (t one)", p=P, t=PACK))
         y_tile = {}
@@ -59,13 +58,11 @@ def tile_attend_gsqh_pl_x_ts_kernel(tc, xT, wT, y, wt, ts, offs, out_0, out_1, o
             o, t = divmod(k, PACK)
             rows = keep.tile([P, count, N], F32, name=f"y_rows{k}")
             nc.sync.dma_start(rows[:], y_rows[o, :, t : t + count, :])
-            for i in range(count):
-                y_tile[k + i] = rows[:, i, :]
+            y_tile[k] = rows
 
         for c in range(2):
             nc.sync.dma_start(x_first[c][:], x_rows[:, :, c * PASS // 2 : (c + 1) * PASS // 2])
-        load_y(0, 1)
-        load_y(1, 1)
+        load_y(0, 2)
         load_y(2, 2)
         nc.sync.dma_start(x_second[:], x_rows[:, :, PASS:])
         load_y(4, 2)
@@ -82,11 +79,14 @@ def tile_attend_gsqh_pl_x_ts_kernel(tc, xT, wT, y, wt, ts, offs, out_0, out_1, o
         ts_col = keep.tile([P, PACK], F32, name="ts_col")
         nc.scalar.copy(ts_col[:], ts_turn[:, :, 0])
         ts_all = psum.tile([P, N], F32, name="ts_all", tag="bank7")
+        ts_twice = keep.tile([P, 2, N], F32, name="ts_twice")
         for c in range(PACK):
             nc.tensor.transpose(ts_all[:, c * P : (c + 1) * P], ts_col[:, c : c + 1].to_broadcast([P, P]), ident[:])
+        for i in range(2):
+            nc.scalar.copy(ts_twice[:, i, :], ts_all[:])
 
         w_listed = keep.tile([P, N, PACK], BF16, name="w_listed", align_bytes=64)
-        w_words = w_listed[:].rearrange("p n j -> p (n j)").bitcast(F32).rearrange("p (a s e u) -> p u a e s", a=2, e=2, u=2)
+        w_words = w_listed[:].rearrange("p n j -> p (n j)").bitcast(F32).rearrange("p (s t u) -> p u t s", t=PACK, u=2)
         w_turned = keep.tile([P, P, 2, 2, PACK], BF16, name="w_turned", align_bytes=64)
         wd_codes = keep.tile([P, N], U32, name="wd_codes", align_bytes=64)
         wd_scales = keep.tile([P, N], U8, name="wd_scales", align_bytes=64)
@@ -94,22 +94,22 @@ def tile_attend_gsqh_pl_x_ts_kernel(tc, xT, wT, y, wt, ts, offs, out_0, out_1, o
         wn_scales = keep.tile([P, D], U8, name="wn_scales", align_bytes=64)
 
         def gather_w(j):
-            nc.vector.tensor_copy(w_listed[:, :, j].rearrange("p (a s e) -> p s a e", a=2, e=2), w_plane[j][:].indirect(offsets[:]))
+            nc.vector.tensor_copy(w_listed[:, :, j], w_plane[j][:].indirect(offsets[:]))
 
         def turn_w(u):
             bank = psum.tile([P, PACK * P], F32, name=f"w_turn{u}", tag=("bank6", "bank0")[u])
             for t in range(PACK):
-                nc.tensor.transpose(bank[:, t * P : (t + 1) * P], w_words[:, u, t // 2, t % 2, :], ident[:])
+                nc.tensor.transpose(bank[:, t * P : (t + 1) * P], w_words[:, u, t, :], ident[:])
             nc.scalar.copy(w_turned[:, :, u, :, :], bank[:].bitcast(BF16).rearrange("s (t p e) -> s p e t", t=PACK, e=2))
 
         x_dealt = [keep.tile([P, PACK, P, PACK], BF16, name=f"x_dealt{o}", align_bytes=64) for o in range(PASSES)]
         x_codes = [keep.tile([P, PASS], U32, name=f"x_codes{o}", align_bytes=64) for o in range(PASSES)]
         x_scales = [keep.tile([P, PASS], U8, name=f"x_scales{o}", align_bytes=64) for o in range(PASSES)]
 
-        def deal_x(c, copy):
-            o, half = divmod(c, 2)
-            copy(x_dealt[o][:, :, half * P // 2 : (half + 1) * P // 2, :].rearrange("p t m j -> p m t j"),
-                 x_halves[c].rearrange("p j (m t) -> p m t j", t=PACK))
+        def deal_x(o, rows, first, copy):
+            count = rows.shape[2] // PACK
+            copy(x_dealt[o][:, :, first : first + count, :].rearrange("p t m j -> p m t j"),
+                 rows.rearrange("p j (m t) -> p m t j", t=PACK))
 
         def quantise_x(o, t, count):
             cols = slice(t * P, (t + count) * P)
@@ -121,39 +121,45 @@ def tile_attend_gsqh_pl_x_ts_kernel(tc, xT, wT, y, wt, ts, offs, out_0, out_1, o
         signed, margin, h_words, h_ops = {}, {}, {}, {}
 
         def sign_scales(k):
-            signed[k] = work.tile([P, N], F32, name="signed", tag="signed", bufs=4)
-            nc.vector.tensor_tensor(signed[k][:].rearrange("r (a s e) -> r s a e", a=2, e=2),
-                                    y_tile[k].rearrange("r (s a e) -> r s a e", a=2, e=2),
-                                    ts_all[:].rearrange("r (s a e) -> r s a e", a=2, e=2), ALU.mult)
+            pair = work.tile([P, 2, N], F32, name="signed", tag="signed")
+            nc.vector.tensor_tensor(pair[:], y_tile[k][:], ts_twice[:], ALU.mult)
+            signed[k], signed[k + 1] = pair[:, 0, :], pair[:, 1, :]
 
         def score(k):
             o, t = divmod(k, PACK)
-            bank = psum.tile([P, N], F32, name="scores", tag=f"bank{k % 3}")
+            bank = psum.tile([P, N], F32, name="scores", tag=f"bank{(0, 1, 2, 7)[k % 4]}")
             cols = slice(t * P, (t + 1) * P)
             nc.tensor.matmul_mx(bank[:], lhsT=x_codes[o][:, cols].bitcast(E4M3), lhsT_scale=x_scales[o][:, cols],
                                 rhs=wd_codes[:].bitcast(E4M3), rhs_scale=wd_scales[:], start=True, stop=True)
             ya = work.tile([P, N], F32, name="ya", tag="ya") if k < TILES - 1 else keep.tile([P, N], F32, name="ya_last", tag="late0", align_bytes=64)
-            nc.vector.tensor_tensor(ya[:], bank[:], signed[k][:], ALU.mult)
+            nc.vector.tensor_tensor(ya[:], bank[:], signed[k], ALU.mult)
             margin[k] = work.tile([P, N], F32, name="margin", tag="margin")
             nc.scalar.activation(margin[k][:], ya[:], ACT.Relu, bias=1.0, scale=-1.0)
 
         def weigh(k):
             h = work.tile([P, N], BF16, name="h", tag="h") if k < TILES - 1 else keep.tile([P, N], BF16, name="h_last", tag="late1", align_bytes=64)
-            nc.vector.scalar_tensor_tensor(h[:], margin[k][:], neg_wt[:, k : k + 1], signed[k][:], ALU.mult, ALU.mult)
-            words = h[:].bitcast(F32).rearrange("r (u s) -> r u s", u=2)
+            nc.vector.scalar_tensor_tensor(h[:], margin[k][:], neg_wt[:, k : k + 1], signed[k], ALU.mult, ALU.mult)
+            words = h[:].bitcast(F32).rearrange("r (s u) -> r u s", u=2)
             bank = psum.tile([P, 2, P], F32, name="h_turn", tag=f"bank{3 + k % 2}")
             for u in range(2):
                 nc.tensor.transpose(bank[:, u, :], words[:, u, :], ident[:])
-            h_words[k] = work.tile([P, P, 2], F32, name="h_words", tag="h_words", align_bytes=64)
-            nc.scalar.copy(h_words[k][:], bank[:].rearrange("s u r -> s r u"))
+            if k % 2 == 0:
+                h_words[k // 2] = work.tile([P, 2, P, 2], F32, name="h_words", tag="h_words", bufs=2, align_bytes=64)
+            nc.scalar.copy(h_words[k // 2][:, k % 2], bank[:].rearrange("s u r -> s r u"))
+
+        def quantise_h(k, count):
+            codes = work.tile([P, count * P], U32, name="h_codes", tag="h_codes", bufs=2, align_bytes=64)
+            scales = work.tile([P, count * P], U8, name="h_scales", tag="h_scales", bufs=2, align_bytes=64)
+            words = h_words[k // 2][:, k % 2 : k % 2 + count].rearrange("s t r u -> s (t r u)")
+            nc.vector.quantize_mx(codes[:].bitcast(E5M2), scales[:], words.bitcast(BF16))
+            for i in range(count):
+                h_ops[k + i] = codes[:, i * P : (i + 1) * P], scales[:, i * P : (i + 1) * P]
 
         def gradient(k):
             o, t = divmod(k, PACK)
-            codes = work.tile([P, P], U32, name="h_codes", tag="h_codes", align_bytes=64)
-            scales = work.tile([P, P], U8, name="h_scales", tag="h_scales", align_bytes=64)
-            nc.vector.quantize_mx(codes[:].bitcast(E5M2), scales[:], h_words[k][:].rearrange("s r u -> s (r u)").bitcast(BF16))
+            codes, scales = h_ops[k]
             bank = psum.tile([P, D], F32, name="grad", tag=f"bank{5 + k % 2}")
-            nc.tensor.matmul_mx(bank[:], lhsT=codes[:].bitcast(E5M2), lhsT_scale=scales[:],
+            nc.tensor.matmul_mx(bank[:], lhsT=codes.bitcast(E5M2), lhsT_scale=scales,
                                 rhs=wn_codes[:].bitcast(E4M3), rhs_scale=wn_scales[:], start=True, stop=True)
             pieces = 2 if k == TILES - 1 else 1
             for i in range(pieces):
@@ -180,11 +186,14 @@ def tile_attend_gsqh_pl_x_ts_kernel(tc, xT, wT, y, wt, ts, offs, out_0, out_1, o
                 weave(nc.vector.tensor_copy, woven[1], o, half, half, half + half // 2)
             else:
                 for c in range(2):
-                    weave(nc.scalar.copy, woven[c], o, c * half, c * half, (c + 1) * half)
+                    weave(nc.vector.tensor_copy, woven[c], o, c * half, c * half, (c + 1) * half)
             for c in range(2):
                 cols = slice(c * half, (c + 1) * half)
                 nc.vector.quantize_mx(codes[:, cols].bitcast(E4M3), out_scales[:, o, cols], woven[c][:].rearrange("p d t -> p (d t)"))
-            nc.sync.dma_start(words_out, codes[:].bitcast(I32))
+                if last:
+                    nc.sync.dma_start(words_out[:, cols], codes[:, cols].bitcast(I32))
+            if not last:
+                nc.sync.dma_start(words_out, codes[:].bitcast(I32))
 
         def store_scales():
             for q in range(4):
@@ -198,24 +207,29 @@ def tile_attend_gsqh_pl_x_ts_kernel(tc, xT, wT, y, wt, ts, offs, out_0, out_1, o
         gather_w(2)
         gather_w(3)
         nc.vector.quantize_mx(wd_codes[:].bitcast(E4M3), wd_scales[:], w_listed[:].rearrange("p n j -> p (n j)"))
-        deal_x(0, nc.scalar.copy)
-        deal_x(1, nc.vector.tensor_copy)
-        quantise_x(0, 0, 1)
+        deal_x(0, x_first[0][:], 0, nc.scalar.copy)
+        deal_x(0, x_first[1][:, :, :P], P // 2, nc.vector.tensor_copy)
+        deal_x(0, x_first[1][:, :, P:], 3 * P // 4, nc.scalar.copy)
+        quantise_x(0, 0, PACK)
         sign_scales(0)
         for k in range(TILES):
             score(k)
             if k == 0:
                 turn_w(1)
-            if k < 2:
-                quantise_x(0, k + 1, k + 1)
-            if k + 1 < TILES:
+            if k % 2 == 1 and k + 1 < TILES:
                 sign_scales(k + 1)
             weigh(k)
-            if k == 0:
+            if k == 1:
                 nc.vector.quantize_mx(wn_codes[:].bitcast(E4M3), wn_scales[:], w_turned[:].rearrange("s p u e t -> s (p u e t)"))
-            gradient(k)
+            if k >= TILES - 2:
+                quantise_h(k, 1)
+                gradient(k)
+            elif k % 2 == 1:
+                quantise_h(k - 1, 2)
+                gradient(k - 1)
+                gradient(k)
             if k in (1, 2):
-                deal_x(k + 1, nc.scalar.copy)
+                deal_x(1, x_second[:, :, (k - 1) * PASS // 2 : k * PASS // 2], (k - 1) * P // 2, nc.scalar.copy)
             if k == 2:
                 quantise_x(1, 0, PACK)
         for o in range(PASSES):

@@ -22,6 +22,7 @@ PACK = 4
 PASS = P * PACK
 PASSES = R // PASS
 TILES = PASSES * PACK
+HALF = P // 2
 
 
 def tile_attend_gsqh_pl_x_ts_kernel(tc, xT, wT, y, wt, ts, offs, out_0, out_1, out_2):
@@ -32,139 +33,163 @@ def tile_attend_gsqh_pl_x_ts_kernel(tc, xT, wT, y, wt, ts, offs, out_0, out_1, o
         psum = ctx.enter_context(tc.psum_pool(name="psum", bufs=1))
 
         offsets = keep.tile([P, N // 16], U16, name="offsets")
-
-        ts_row = keep.tile([P, T], F32, name="ts_row")
+        ts_row = keep.tile([P, T], F32, name="ts_row", align_bytes=64)
         nc.vector.memset(ts_row[:], 0.0)
         ident = keep.tile([P, P], F32, name="ident")
         make_identity(nc, ident[:])
 
         w_rows = wT.rearrange("(p j) c -> j p c", j=PACK)
-        w_plane = [keep.tile([P, T], F32, name=f"w_plane{j}") for j in range(PACK)]
+        w_plane = [keep.tile([P, T], F32, name=f"w_plane{j}", align_bytes=64) for j in range(PACK)]
+        x_rows = xT[0].rearrange("(p j) r -> p j r", j=PACK)
+        y_first = y[0, :PASS].rearrange("(h m e) n -> h m e n", m=P, e=2)
+        y_second = y[0, PASS:].rearrange("(p c e) n -> c p e n", c=2, e=2)
+        x_raw = [keep.tile([P, PACK, 2 * P], F32, name=f"x_raw{i}", align_bytes=64) for i in range(TILES // 2)]
+        y_pair = [keep.tile([P, 2, N], F32, name=f"y_pair{i}") for i in range(TILES // 2)]
+        wt_first = keep.tile([P, 2, 2], F32, name="wt_first")
+        wt_second = keep.tile([P, PACK], F32, name="wt_second")
+
+        def load_x(i):
+            nc.sync.dma_start(x_raw[i][:], x_rows[:, :, i * 2 * P : (i + 1) * 2 * P])
+
+        def load_y(i):
+            nc.sync.dma_start(y_pair[i][:], y_first[i] if i < 2 else y_second[i - 2])
+
+        nc.scalar.dma_start(wt_first[:], wt[0, :PASS].rearrange("(h m e) one -> m h (e one)", m=P, e=2))
+        nc.scalar.dma_start(wt_second[:], wt[0, PASS:].rearrange("(p t) one -> p (t one)", t=PACK))
         for j in range(PACK):
             nc.sync.dma_start(w_plane[j][:], w_rows[j])
             if j == 0:
                 nc.sync.dma_start(offsets[:], offs)
                 nc.sync.dma_start(ts_row[0:1, :], ts[0:1, :])
-
-        x_rows = xT[0].rearrange("(p j) r -> p j r", j=PACK)
-        y_rows = y[0].rearrange("(o p t) n -> o p t n", p=P, t=PACK)
-        x_first = [keep.tile([P, PACK, PASS // 2], F32, name=f"x_first{c}") for c in range(2)]
-        x_second = keep.tile([P, PACK, PASS], F32, name="x_second")
-        wt_raw = keep.tile([P, PASSES, PACK], F32, name="wt_raw")
-        nc.scalar.dma_start(wt_raw[:], wt[0].rearrange("(o p t) one -> p o (t one)", p=P, t=PACK))
-        y_tile = {}
-
-        def load_y(k, count):
-            o, t = divmod(k, PACK)
-            rows = keep.tile([P, count, N], F32, name=f"y_rows{k}")
-            nc.sync.dma_start(rows[:], y_rows[o, :, t : t + count, :])
-            y_tile[k] = rows
-
-        for c in range(2):
-            nc.sync.dma_start(x_first[c][:], x_rows[:, :, c * PASS // 2 : (c + 1) * PASS // 2])
-        load_y(0, 2)
-        load_y(2, 2)
-        nc.sync.dma_start(x_second[:], x_rows[:, :, PASS:])
-        load_y(4, 2)
-        load_y(6, 2)
-
-        neg_wt = keep.tile([P, TILES], F32, name="neg_wt")
-        nc.vector.tensor_scalar(neg_wt[:], wt_raw[:].rearrange("p o t -> p (o t)"), -1.0, None, ALU.mult)
+        load_x(0)
+        load_x(1)
+        load_y(0)
+        load_y(1)
+        load_x(2)
+        load_x(3)
+        load_y(2)
+        load_y(3)
 
         ts_listed = keep.tile([P, N], F32, name="ts_listed")
         nc.vector.tensor_copy(ts_listed[:], ts_row[:].indirect(offsets[:]))
-        ts_turn = psum.tile([P, PACK, P], F32, name="ts_turn", tag="bank5")
+        ts_turn = psum.tile([P, PACK, P], F32, name="ts_turn", tag="bank4")
         for c in range(PACK):
             nc.tensor.transpose(ts_turn[:, c, :], ts_listed[:, c * P : (c + 1) * P], ident[:])
         ts_col = keep.tile([P, PACK], F32, name="ts_col")
         nc.scalar.copy(ts_col[:], ts_turn[:, :, 0])
         ts_all = psum.tile([P, N], F32, name="ts_all", tag="bank7")
-        ts_twice = keep.tile([P, 2, N], F32, name="ts_twice")
+        neg_ts = keep.tile([P, 1, N], F32, name="neg_ts")
         for c in range(PACK):
             nc.tensor.transpose(ts_all[:, c * P : (c + 1) * P], ts_col[:, c : c + 1].to_broadcast([P, P]), ident[:])
-        for i in range(2):
-            nc.scalar.copy(ts_twice[:, i, :], ts_all[:])
+        nc.scalar.activation(neg_ts[:, 0, :], ts_all[:], ACT.Copy, scale=-1.0)
 
-        w_listed = keep.tile([P, N, PACK], BF16, name="w_listed", align_bytes=64)
+        w_listed = keep.tile([P, N, PACK], BF16, name="w_listed", tag="ts_row", align_bytes=64)
         w_words = w_listed[:].rearrange("p n j -> p (n j)").bitcast(F32).rearrange("p (s t u) -> p u t s", t=PACK, u=2)
-        w_turned = keep.tile([P, P, 2, 2, PACK], BF16, name="w_turned", align_bytes=64)
         wd_codes = keep.tile([P, N], U32, name="wd_codes", align_bytes=64)
         wd_scales = keep.tile([P, N], U8, name="wd_scales", align_bytes=64)
-        wn_codes = keep.tile([P, D], U32, name="wn_codes", align_bytes=64)
+        turned, wn = {}, {}
         wn_scales = keep.tile([P, D], U8, name="wn_scales", align_bytes=64)
 
         def gather_w(j):
             nc.vector.tensor_copy(w_listed[:, :, j], w_plane[j][:].indirect(offsets[:]))
 
         def turn_w(u):
-            bank = psum.tile([P, PACK * P], F32, name=f"w_turn{u}", tag=("bank6", "bank0")[u])
+            bank = psum.tile([P, PACK * P], F32, name=f"w_turn{u}", tag=f"bank{6 - u}")
             for t in range(PACK):
                 nc.tensor.transpose(bank[:, t * P : (t + 1) * P], w_words[:, u, t, :], ident[:])
-            nc.scalar.copy(w_turned[:, :, u, :, :], bank[:].bitcast(BF16).rearrange("s (t p e) -> s p e t", t=PACK, e=2))
+            pairs = bank[:].bitcast(BF16).rearrange("s (t p e) -> s p e t", t=PACK, e=2)
+            turned[u] = keep.tile([P, P, 2, PACK], BF16, name=f"w_turned{u}", tag=("turned", "x_raw1")[u], align_bytes=64)
+            for i in range(2):
+                nc.scalar.copy(turned[u][:, i * HALF : (i + 1) * HALF], pairs[:, i * HALF : (i + 1) * HALF])
 
-        x_dealt = [keep.tile([P, PACK, P, PACK], BF16, name=f"x_dealt{o}", align_bytes=64) for o in range(PASSES)]
-        x_codes = [keep.tile([P, PASS], U32, name=f"x_codes{o}", align_bytes=64) for o in range(PASSES)]
-        x_scales = [keep.tile([P, PASS], U8, name=f"x_scales{o}", align_bytes=64) for o in range(PASSES)]
+        def quantise_turned():
+            wn["codes"] = keep.tile([P, D], U32, name="wn_codes", tag="after_ya1", align_bytes=64)
+            for u in range(2):
+                cols = slice(u * D // 2, (u + 1) * D // 2)
+                nc.vector.quantize_mx(wn["codes"][:, cols].bitcast(E4M3), wn_scales[:, cols], turned[u][:].rearrange("s p e t -> s (p e t)"))
 
-        def deal_x(o, rows, first, copy):
-            count = rows.shape[2] // PACK
-            copy(x_dealt[o][:, :, first : first + count, :].rearrange("p t m j -> p m t j"),
-                 rows.rearrange("p j (m t) -> p m t j", t=PACK))
+        x_ops, signed, margin, h_bank, h_words, h_ops = {}, {}, {}, {}, {}, {}
 
-        def quantise_x(o, t, count):
-            cols = slice(t * P, (t + count) * P)
-            nc.vector.quantize_mx(x_codes[o][:, cols].bitcast(E4M3), x_scales[o][:, cols],
-                                  x_dealt[o][:, t : t + count].rearrange("p t m j -> p (t m j)"))
+        def quantise_x(first, count, woven):
+            codes = keep.tile([P, count * P], U32, name=f"x_codes{first}", align_bytes=64)
+            scales = keep.tile([P, count * P], U8, name=f"x_scales{first}", align_bytes=64)
+            nc.vector.quantize_mx(codes[:].bitcast(E4M3), scales[:], woven)
+            for i in range(count):
+                x_ops[first + i] = codes[:, i * P : (i + 1) * P], scales[:, i * P : (i + 1) * P]
+
+        def first_x(h, copies):
+            woven = keep.tile([P, 2, P, PACK], BF16, name=f"x_half{h}", tag=("w_plane3", "x_raw0")[h], align_bytes=64)
+            for i, copy in enumerate(copies):
+                copy(woven[:, :, i * HALF : (i + 1) * HALF, :].rearrange("p e m j -> p m j e"),
+                     x_raw[h][:, :, i * P : (i + 1) * P].rearrange("p j (m e) -> p m j e", e=2))
+            quantise_x(2 * h, 2, woven[:].rearrange("p e m j -> p (e m j)"))
+
+        def second_x():
+            woven = keep.tile([P, PACK, P, PACK], BF16, name="x_dealt", tag="after_ya0", align_bytes=64)
+            for i in range(PACK):
+                (nc.scalar.copy, nc.scalar.copy, nc.scalar.copy, nc.scalar.copy)[i](woven[:, :, i * P // PACK : (i + 1) * P // PACK, :].rearrange("p t m j -> p m j t"),
+                               x_raw[2 + i // 2][:, :, i % 2 * P : (i % 2 + 1) * P].rearrange("p j (m t) -> p m j t", t=PACK))
+            quantise_x(PACK, PACK, woven[:].rearrange("p t m j -> p (t m j)"))
 
         grad_rows = [keep.tile([P, PACK, D], F32, name=f"grad_rows{o}") for o in range(PASSES)]
         out_rows = out_0[0].rearrange("(o p t) d -> o p t d", p=P, t=PACK)
-        signed, margin, h_words, h_ops = {}, {}, {}, {}
 
-        def sign_scales(k):
-            pair = work.tile([P, 2, N], F32, name="signed", tag="signed")
-            nc.vector.tensor_tensor(pair[:], y_tile[k][:], ts_twice[:], ALU.mult)
-            signed[k], signed[k + 1] = pair[:, 0, :], pair[:, 1, :]
+        def sign_scales(i):
+            tag = ("w_plane3", "x_raw0", "after_ya0", "h_words0")[i]
+            pair = keep.tile([P, 2, N], F32, name=f"signed{i}", tag=tag, align_bytes=64)
+            nc.vector.tensor_tensor(pair[:], y_pair[i][:], neg_ts[:].to_broadcast([P, 2, N]), ALU.mult)
+            signed[2 * i], signed[2 * i + 1] = pair[:, 0, :], pair[:, 1, :]
 
         def score(k):
-            o, t = divmod(k, PACK)
+            codes, scales = x_ops[k]
             bank = psum.tile([P, N], F32, name="scores", tag=f"bank{(0, 1, 2, 7)[k % 4]}")
-            cols = slice(t * P, (t + 1) * P)
-            nc.tensor.matmul_mx(bank[:], lhsT=x_codes[o][:, cols].bitcast(E4M3), lhsT_scale=x_scales[o][:, cols],
+            nc.tensor.matmul_mx(bank[:], lhsT=codes.bitcast(E4M3), lhsT_scale=scales,
                                 rhs=wd_codes[:].bitcast(E4M3), rhs_scale=wd_scales[:], start=True, stop=True)
-            ya = work.tile([P, N], F32, name="ya", tag="ya") if k < TILES - 1 else keep.tile([P, N], F32, name="ya_last", tag="late0", align_bytes=64)
+            ya = keep.tile([P, N], F32, name=f"ya{k}", tag=f"after_ya{k}", align_bytes=64)
             nc.vector.tensor_tensor(ya[:], bank[:], signed[k], ALU.mult)
             margin[k] = work.tile([P, N], F32, name="margin", tag="margin")
-            nc.scalar.activation(margin[k][:], ya[:], ACT.Relu, bias=1.0, scale=-1.0)
+            nc.scalar.activation(margin[k][:], ya[:], ACT.Relu, bias=1.0, scale=1.0)
 
         def weigh(k):
-            h = work.tile([P, N], BF16, name="h", tag="h") if k < TILES - 1 else keep.tile([P, N], BF16, name="h_last", tag="late1", align_bytes=64)
-            nc.vector.scalar_tensor_tensor(h[:], margin[k][:], neg_wt[:, k : k + 1], signed[k], ALU.mult, ALU.mult)
+            h = keep.tile([P, N], BF16, name=f"h{k}", tag=f"after_h{k}", align_bytes=64)
+            weight = wt_first[:, k // 2, k % 2 : k % 2 + 1] if k < PACK else wt_second[:, k - PACK : k - PACK + 1]
+            nc.vector.scalar_tensor_tensor(h[:], margin[k][:], weight, signed[k], ALU.mult, ALU.mult)
             words = h[:].bitcast(F32).rearrange("r (s u) -> r u s", u=2)
             bank = psum.tile([P, 2, P], F32, name="h_turn", tag=f"bank{3 + k % 2}")
             for u in range(2):
                 nc.tensor.transpose(bank[:, u, :], words[:, u, :], ident[:])
-            if k % 2 == 0:
-                h_words[k // 2] = work.tile([P, 2, P, 2], F32, name="h_words", tag="h_words", bufs=2, align_bytes=64)
-            nc.scalar.copy(h_words[k // 2][:, k % 2], bank[:].rearrange("s u r -> s r u"))
+            h_bank[k] = bank
 
-        def quantise_h(k, count):
-            codes = work.tile([P, count * P], U32, name="h_codes", tag="h_codes", bufs=2, align_bytes=64)
-            scales = work.tile([P, count * P], U8, name="h_scales", tag="h_scales", bufs=2, align_bytes=64)
-            words = h_words[k // 2][:, k % 2 : k % 2 + count].rearrange("s t r u -> s (t r u)")
-            nc.vector.quantize_mx(codes[:].bitcast(E5M2), scales[:], words.bitcast(BF16))
-            for i in range(count):
-                h_ops[k + i] = codes[:, i * P : (i + 1) * P], scales[:, i * P : (i + 1) * P]
+        def regroup(k):
+            bank = h_bank[k]
+            if k < PACK:
+                half, e = divmod(k, 2)
+                if half == 0:
+                    h_words[e] = keep.tile([P, 2, P, 2], F32, name=f"h_words{e}", align_bytes=64)
+                nc.scalar.copy(h_words[e][:, :, half * HALF : (half + 1) * HALF, :].rearrange("s c m u -> s m c u"),
+                               bank[:].rearrange("s u (m c) -> s m c u", c=2))
+            else:
+                if k != 5:
+                    h_words[k] = keep.tile([P, 2 if k == 4 else 1, P, 2], F32, name=f"h_words{k}", align_bytes=64)
+                nc.scalar.copy(h_words[4][:, 1] if k == 5 else h_words[k][:, 0], bank[:].rearrange("s u r -> s r u"))
 
-        def gradient(k):
+        def quantise_h(first, tiles):
+            codes = keep.tile([P, len(tiles) * P], U32, name=f"h_codes{first}", align_bytes=64)
+            scales = keep.tile([P, len(tiles) * P], U8, name=f"h_scales{first}", align_bytes=64)
+            nc.vector.quantize_mx(codes[:].bitcast(E5M2), scales[:], h_words[first][:].rearrange("s t r u -> s (t r u)").bitcast(BF16))
+            for i, k in enumerate(tiles):
+                h_ops[k] = codes[:, i * P : (i + 1) * P], scales[:, i * P : (i + 1) * P]
+
+        def gradient(k, slot):
             o, t = divmod(k, PACK)
             codes, scales = h_ops[k]
-            bank = psum.tile([P, D], F32, name="grad", tag=f"bank{5 + k % 2}")
-            nc.tensor.matmul_mx(bank[:], lhsT=codes.bitcast(E5M2), lhsT_scale=scales,
-                                rhs=wn_codes[:].bitcast(E4M3), rhs_scale=wn_scales[:], start=True, stop=True)
-            pieces = 2 if k == TILES - 1 else 1
-            for i in range(pieces):
-                cols = slice(i * D // pieces, (i + 1) * D // pieces)
-                nc.scalar.copy(grad_rows[o][:, t, cols], bank[:, cols])
+            bank = psum.tile([P, 2, P, 2], F32, name="grad", tag=f"bank{5 + slot}")
+            nc.tensor.matmul_mx(bank[:].rearrange("r u p e -> r (u p e)"), lhsT=codes.bitcast(E5M2), lhsT_scale=scales,
+                                rhs=wn["codes"][:].bitcast(E4M3), rhs_scale=wn_scales[:], start=True, stop=True)
+            rows = grad_rows[o][:, t, :].rearrange("r (p u e) -> r p u e", u=2, e=2)
+            cuts = (0, HALF, P) if k == TILES - 1 else (0, P)
+            for a, b in zip(cuts, cuts[1:]):
+                nc.scalar.copy(rows[:, a:b], bank[:, :, a:b, :].rearrange("r u p e -> r p u e"))
             nc.sync.dma_start(out_rows[o, :, t, :], grad_rows[o][:, t, :])
 
         out_scales = keep.tile([P, PASSES, D], U8, name="out_scales", align_bytes=64)
@@ -178,12 +203,12 @@ def tile_attend_gsqh_pl_x_ts_kernel(tc, xT, wT, y, wt, ts, offs, out_0, out_1, o
             words_out = out_1[o].rearrange("p d l -> p (d l)").bitcast(I32)
             half = D // 2
             last = o == PASSES - 1
-            woven = [keep.tile([P, half, PACK], BF16, name=f"woven{o}{c}", tag=f"woven{c}" if last else f"late{c}", align_bytes=64)
+            woven = [keep.tile([P, half, PACK], BF16, name=f"woven{o}{c}", tag=f"woven{c}" if last else ("after_ya7", "after_h7")[c], align_bytes=64)
                      for c in range(2)]
             if last:
                 weave(nc.vector.tensor_copy, woven[0], o, 0, 0, half)
-                weave(nc.scalar.copy, woven[1], o, half, half + half // 2, D)
-                weave(nc.vector.tensor_copy, woven[1], o, half, half, half + half // 2)
+                weave(nc.scalar.copy, woven[1], o, half, D - D // 4, D)
+                weave(nc.vector.tensor_copy, woven[1], o, half, half, D - D // 4)
             else:
                 for c in range(2):
                     weave(nc.vector.tensor_copy, woven[c], o, c * half, c * half, (c + 1) * half)
@@ -207,31 +232,52 @@ def tile_attend_gsqh_pl_x_ts_kernel(tc, xT, wT, y, wt, ts, offs, out_0, out_1, o
         gather_w(2)
         gather_w(3)
         nc.vector.quantize_mx(wd_codes[:].bitcast(E4M3), wd_scales[:], w_listed[:].rearrange("p n j -> p (n j)"))
-        deal_x(0, x_first[0][:], 0, nc.scalar.copy)
-        deal_x(0, x_first[1][:, :, :P], P // 2, nc.vector.tensor_copy)
-        deal_x(0, x_first[1][:, :, P:], 3 * P // 4, nc.scalar.copy)
-        quantise_x(0, 0, PACK)
+        first_x(0, (nc.scalar.copy, nc.vector.tensor_copy))
+        first_x(1, (nc.scalar.copy, nc.scalar.copy))
         sign_scales(0)
-        for k in range(TILES):
-            score(k)
-            if k == 0:
-                turn_w(1)
-            if k % 2 == 1 and k + 1 < TILES:
-                sign_scales(k + 1)
-            weigh(k)
-            if k == 1:
-                nc.vector.quantize_mx(wn_codes[:].bitcast(E4M3), wn_scales[:], w_turned[:].rearrange("s p u e t -> s (p u e t)"))
-            if k >= TILES - 2:
-                quantise_h(k, 1)
-                gradient(k)
-            elif k % 2 == 1:
-                quantise_h(k - 1, 2)
-                gradient(k - 1)
-                gradient(k)
-            if k in (1, 2):
-                deal_x(1, x_second[:, :, (k - 1) * PASS // 2 : k * PASS // 2], (k - 1) * P // 2, nc.scalar.copy)
-            if k == 2:
-                quantise_x(1, 0, PACK)
+        score(0)
+        score(1)
+        turn_w(1)
+        sign_scales(1)
+        weigh(0)
+        score(2)
+        weigh(1)
+        score(3)
+        second_x()
+        regroup(0)
+        regroup(1)
+        weigh(2)
+        quantise_turned()
+        sign_scales(2)
+        weigh(3)
+        score(4)
+        regroup(2)
+        quantise_h(0, (0, 2))
+        score(5)
+        regroup(3)
+        quantise_h(1, (1, 3))
+        weigh(4)
+        sign_scales(3)
+        weigh(5)
+        score(6)
+        regroup(4)
+        score(7)
+        regroup(5)
+        quantise_h(4, (4, 5))
+        weigh(6)
+        regroup(6)
+        weigh(7)
+        regroup(7)
+        quantise_h(6, (6,))
+        quantise_h(7, (7,))
+        gradient(0, 0)
+        gradient(2, 1)
+        gradient(1, 0)
+        gradient(3, 1)
+        gradient(4, 0)
+        gradient(5, 1)
+        gradient(6, 0)
+        gradient(7, 1)
         for o in range(PASSES):
             planes(o)
         store_scales()

@@ -142,7 +142,7 @@ def tile_attend_gsqh_pl_x_ts_kernel(tc, xT, wT, y, wt, ts, offs, out_0, out_1, o
 
         def score(k):
             codes, scales = x_ops[k]
-            bank = psum.tile([P, N], F32, name="scores", tag=f"bank{(0, 1, 2, 7)[k % 4]}")
+            bank = psum.tile([P, N], F32, name="scores", tag=f"bank{(0, 1, 2)[k % 3]}")
             nc.tensor.matmul_mx(bank[:], lhsT=codes.bitcast(E4M3), lhsT_scale=scales,
                                 rhs=wd_codes[:].bitcast(E4M3), rhs_scale=wd_scales[:], start=True, stop=True)
             ya = keep.tile([P, N], F32, name=f"ya{k}", tag=f"after_ya{k}", align_bytes=64)
@@ -153,8 +153,11 @@ def tile_attend_gsqh_pl_x_ts_kernel(tc, xT, wT, y, wt, ts, offs, out_0, out_1, o
         def weigh(k):
             h = keep.tile([P, N], BF16, name=f"h{k}", tag=f"after_h{k}", align_bytes=64)
             weight = wt_first[:, k // 2, k % 2 : k % 2 + 1] if k < PACK else wt_second[:, k - PACK : k - PACK + 1]
-            nc.vector.scalar_tensor_tensor(h[:], margin[k][:], weight, signed[k], ALU.mult, ALU.mult)
-            words = h[:].bitcast(F32).rearrange("r (s u) -> r u s", u=2)
+            for u in range(2):
+                nc.vector.scalar_tensor_tensor(h[:].rearrange("r (u s e) -> r u s e", u=2, e=2)[:, u],
+                                               margin[k][:].rearrange("r (s u e) -> r u s e", u=2, e=2)[:, u], weight,
+                                               signed[k].rearrange("r (s u e) -> r u s e", u=2, e=2)[:, u], ALU.mult, ALU.mult)
+            words = h[:].bitcast(F32).rearrange("r (u s) -> r u s", u=2)
             bank = psum.tile([P, 2, P], F32, name="h_turn", tag=f"bank{3 + k % 2}")
             for u in range(2):
                 nc.tensor.transpose(bank[:, u, :], words[:, u, :], ident[:])
@@ -169,9 +172,8 @@ def tile_attend_gsqh_pl_x_ts_kernel(tc, xT, wT, y, wt, ts, offs, out_0, out_1, o
                 nc.scalar.copy(h_words[e][:, :, half * HALF : (half + 1) * HALF, :].rearrange("s c m u -> s m c u"),
                                bank[:].rearrange("s u (m c) -> s m c u", c=2))
             else:
-                if k != 5:
-                    h_words[k] = keep.tile([P, 2 if k == 4 else 1, P, 2], F32, name=f"h_words{k}", align_bytes=64)
-                nc.scalar.copy(h_words[4][:, 1] if k == 5 else h_words[k][:, 0], bank[:].rearrange("s u r -> s r u"))
+                h_words[k] = keep.tile([P, 1, P, 2], F32, name=f"h_words{k}", align_bytes=64)
+                nc.scalar.copy(h_words[k][:, 0], bank[:].rearrange("s u r -> s r u"))
 
         def quantise_h(first, tiles):
             codes = keep.tile([P, len(tiles) * P], U32, name=f"h_codes{first}", align_bytes=64)
@@ -183,7 +185,7 @@ def tile_attend_gsqh_pl_x_ts_kernel(tc, xT, wT, y, wt, ts, offs, out_0, out_1, o
         def gradient(k, slot):
             o, t = divmod(k, PACK)
             codes, scales = h_ops[k]
-            bank = psum.tile([P, 2, P, 2], F32, name="grad", tag=f"bank{5 + slot}")
+            bank = psum.tile([P, 2, P, 2], F32, name="grad", tag=f"bank{(5, 6, 7)[slot % 3]}")
             nc.tensor.matmul_mx(bank[:].rearrange("r u p e -> r (u p e)"), lhsT=codes.bitcast(E5M2), lhsT_scale=scales,
                                 rhs=wn["codes"][:].bitcast(E4M3), rhs_scale=wn_scales[:], start=True, stop=True)
             rows = grad_rows[o][:, t, :].rearrange("r (p u e) -> r p u e", u=2, e=2)
@@ -242,42 +244,43 @@ def tile_attend_gsqh_pl_x_ts_kernel(tc, xT, wT, y, wt, ts, offs, out_0, out_1, o
         weigh(0)
         score(2)
         weigh(1)
+        quantise_turned()
         score(3)
+        weigh(2)
         second_x()
         regroup(0)
         regroup(1)
-        weigh(2)
-        quantise_turned()
-        sign_scales(2)
-        weigh(3)
-        score(4)
         regroup(2)
-        quantise_h(0, (0, 2))
-        score(5)
+        weigh(3)
         regroup(3)
-        quantise_h(1, (1, 3))
-        weigh(4)
+        sign_scales(2)
+        quantise_h(0, (0, 2))
+        score(4)
         sign_scales(3)
-        weigh(5)
+        quantise_h(1, (1, 3))
+        score(5)
+        weigh(4)
         score(6)
-        regroup(4)
+        weigh(5)
         score(7)
-        regroup(5)
-        quantise_h(4, (4, 5))
         weigh(6)
-        regroup(6)
         weigh(7)
-        regroup(7)
+        regroup(4)
+        quantise_h(4, (4,))
+        regroup(5)
+        quantise_h(5, (5,))
+        regroup(6)
         quantise_h(6, (6,))
+        regroup(7)
         quantise_h(7, (7,))
         gradient(0, 0)
         gradient(2, 1)
-        gradient(1, 0)
-        gradient(3, 1)
-        gradient(4, 0)
-        gradient(5, 1)
-        gradient(6, 0)
-        gradient(7, 1)
+        gradient(1, 2)
+        gradient(3, 3)
+        gradient(4, 4)
+        gradient(5, 5)
+        gradient(6, 6)
+        gradient(7, 7)
         for o in range(PASSES):
             planes(o)
         store_scales()

@@ -29,7 +29,8 @@ def tile_attend_gsqh_pl_x_ts_kernel(tc, xT, wT, y, wt, ts, offs, out_0, out_1, o
     nc = tc.nc
     with ExitStack() as ctx:
         keep = ctx.enter_context(tc.tile_pool(name="keep", bufs=1))
-        work = ctx.enter_context(tc.tile_pool(name="work", bufs=3))
+        work = ctx.enter_context(tc.tile_pool(name="work", bufs=4))
+        shared = ctx.enter_context(tc.tile_pool(name="shared", bufs=1))
         psum = ctx.enter_context(tc.psum_pool(name="psum", bufs=1))
 
         offsets = keep.tile([P, N // 16], U16, name="offsets")
@@ -43,7 +44,8 @@ def tile_attend_gsqh_pl_x_ts_kernel(tc, xT, wT, y, wt, ts, offs, out_0, out_1, o
         x_rows = xT[0].rearrange("(p j) r -> p j r", j=PACK)
         y_first = y[0, :PASS].rearrange("(h m e) n -> h m e n", m=P, e=2)
         y_second = y[0, PASS:].rearrange("(p c e) n -> c p e n", c=2, e=2)
-        x_raw = [keep.tile([P, PACK, 2 * P], F32, name=f"x_raw{i}", align_bytes=64) for i in range(TILES // 2)]
+        x_raw = [shared.tile([P, PACK, 2 * P], F32, name="x_raw0", offset=2048, align_bytes=64)]
+        x_raw += [keep.tile([P, PACK, 2 * P], F32, name=f"x_raw{i}", align_bytes=64) for i in range(1, TILES // 2)]
         y_pair = [keep.tile([P, 2, N], F32, name=f"y_pair{i}") for i in range(TILES // 2)]
         wt_first = keep.tile([P, 2, 2], F32, name="wt_first")
         wt_second = keep.tile([P, PACK], F32, name="wt_second")
@@ -99,14 +101,13 @@ def tile_attend_gsqh_pl_x_ts_kernel(tc, xT, wT, y, wt, ts, offs, out_0, out_1, o
                 nc.tensor.transpose(bank[:, t * P : (t + 1) * P], w_words[:, u, t, :], ident[:])
             pairs = bank[:].bitcast(BF16).rearrange("s (t p e) -> s p e t", t=PACK, e=2)
             turned[u] = keep.tile([P, P, 2, PACK], BF16, name=f"w_turned{u}", tag=("turned", "x_raw1")[u], align_bytes=64)
-            for i in range(2):
-                nc.scalar.copy(turned[u][:, i * HALF : (i + 1) * HALF], pairs[:, i * HALF : (i + 1) * HALF])
+            nc.scalar.copy(turned[u][:], pairs)
 
-        def quantise_turned():
-            wn["codes"] = keep.tile([P, D], U32, name="wn_codes", tag="after_ya1", align_bytes=64)
-            for u in range(2):
-                cols = slice(u * D // 2, (u + 1) * D // 2)
-                nc.vector.quantize_mx(wn["codes"][:, cols].bitcast(E4M3), wn_scales[:, cols], turned[u][:].rearrange("s p e t -> s (p e t)"))
+        def quantise_turned(u):
+            if u == 0:
+                wn["codes"] = shared.tile([P, D], U32, name="wn_codes", offset=4096, align_bytes=64)
+            cols = slice(u * D // 2, (u + 1) * D // 2)
+            nc.vector.quantize_mx(wn["codes"][:, cols].bitcast(E4M3), wn_scales[:, cols], turned[u][:].rearrange("s p e t -> s (p e t)"))
 
         x_ops, signed, margin, h_bank, h_words, h_ops = {}, {}, {}, {}, {}, {}
 
@@ -118,7 +119,10 @@ def tile_attend_gsqh_pl_x_ts_kernel(tc, xT, wT, y, wt, ts, offs, out_0, out_1, o
                 x_ops[first + i] = codes[:, i * P : (i + 1) * P], scales[:, i * P : (i + 1) * P]
 
         def first_x(h, copies):
-            woven = keep.tile([P, 2, P, PACK], BF16, name=f"x_half{h}", tag=("w_plane3", "x_raw0")[h], align_bytes=64)
+            if h == 0:
+                woven = keep.tile([P, 2, P, PACK], BF16, name="x_half0", tag="w_plane3", align_bytes=64)
+            else:
+                woven = shared.tile([P, 2, P, PACK], BF16, name="x_half1", offset=2048, align_bytes=64)
             for i, copy in enumerate(copies):
                 copy(woven[:, :, i * HALF : (i + 1) * HALF, :].rearrange("p e m j -> p m j e"),
                      x_raw[h][:, :, i * P : (i + 1) * P].rearrange("p j (m e) -> p m j e", e=2))
@@ -135,8 +139,10 @@ def tile_attend_gsqh_pl_x_ts_kernel(tc, xT, wT, y, wt, ts, offs, out_0, out_1, o
         out_rows = out_0[0].rearrange("(o p t) d -> o p t d", p=P, t=PACK)
 
         def sign_scales(i):
-            tag = ("w_plane3", "x_raw0", "after_ya0", "h_words0")[i]
-            pair = keep.tile([P, 2, N], F32, name=f"signed{i}", tag=tag, align_bytes=64)
+            if i % 2 == 0:
+                pair = keep.tile([P, 2, N], F32, name=f"signed{i}", tag="w_plane3", align_bytes=64)
+            else:
+                pair = shared.tile([P, 2, N], F32, name=f"signed{i}", offset=0, align_bytes=64)
             nc.vector.tensor_tensor(pair[:], y_pair[i][:], neg_ts[:].to_broadcast([P, 2, N]), ALU.mult)
             signed[2 * i], signed[2 * i + 1] = pair[:, 0, :], pair[:, 1, :]
 
@@ -153,11 +159,15 @@ def tile_attend_gsqh_pl_x_ts_kernel(tc, xT, wT, y, wt, ts, offs, out_0, out_1, o
         def weigh(k):
             h = keep.tile([P, N], BF16, name=f"h{k}", tag=f"after_h{k}", align_bytes=64)
             weight = wt_first[:, k // 2, k % 2 : k % 2 + 1] if k < PACK else wt_second[:, k - PACK : k - PACK + 1]
-            for u in range(2):
-                nc.vector.scalar_tensor_tensor(h[:].rearrange("r (u s e) -> r u s e", u=2, e=2)[:, u],
-                                               margin[k][:].rearrange("r (s u e) -> r u s e", u=2, e=2)[:, u], weight,
-                                               signed[k].rearrange("r (s u e) -> r u s e", u=2, e=2)[:, u], ALU.mult, ALU.mult)
-            words = h[:].bitcast(F32).rearrange("r (u s) -> r u s", u=2)
+            if k == TILES - 1:
+                for u in range(2):
+                    nc.vector.scalar_tensor_tensor(h[:].rearrange("r (u s e) -> r u s e", u=2, e=2)[:, u],
+                                                   margin[k][:].rearrange("r (s u e) -> r u s e", u=2, e=2)[:, u], weight,
+                                                   signed[k].rearrange("r (s u e) -> r u s e", u=2, e=2)[:, u], ALU.mult, ALU.mult)
+                words = h[:].bitcast(F32).rearrange("r (u s) -> r u s", u=2)
+            else:
+                nc.vector.scalar_tensor_tensor(h[:], margin[k][:], weight, signed[k], ALU.mult, ALU.mult)
+                words = h[:].bitcast(F32).rearrange("r (s u) -> r u s", u=2)
             bank = psum.tile([P, 2, P], F32, name="h_turn", tag=f"bank{3 + k % 2}")
             for u in range(2):
                 nc.tensor.transpose(bank[:, u, :], words[:, u, :], ident[:])
@@ -235,6 +245,7 @@ def tile_attend_gsqh_pl_x_ts_kernel(tc, xT, wT, y, wt, ts, offs, out_0, out_1, o
         gather_w(3)
         nc.vector.quantize_mx(wd_codes[:].bitcast(E4M3), wd_scales[:], w_listed[:].rearrange("p n j -> p (n j)"))
         first_x(0, (nc.scalar.copy, nc.vector.tensor_copy))
+        quantise_turned(0)
         first_x(1, (nc.scalar.copy, nc.scalar.copy))
         sign_scales(0)
         score(0)
@@ -244,20 +255,20 @@ def tile_attend_gsqh_pl_x_ts_kernel(tc, xT, wT, y, wt, ts, offs, out_0, out_1, o
         weigh(0)
         score(2)
         weigh(1)
-        quantise_turned()
         score(3)
         weigh(2)
         second_x()
+        weigh(3)
+        sign_scales(2)
+        score(4)
+        quantise_turned(1)
         regroup(0)
         regroup(1)
         regroup(2)
-        weigh(3)
         regroup(3)
-        sign_scales(2)
         quantise_h(0, (0, 2))
-        score(4)
-        sign_scales(3)
         quantise_h(1, (1, 3))
+        sign_scales(3)
         score(5)
         weigh(4)
         score(6)

@@ -44,7 +44,7 @@ def tile_attend_gsqh_pl_x_ts_kernel(tc, xT, wT, y, wt, ts, offs, out_0, out_1, o
         x_rows = xT[0].rearrange("(p j) r -> p j r", j=PACK)
         y_first = y[0, :PASS].rearrange("(h m e) n -> h m e n", m=P, e=2)
         y_second = y[0, PASS:].rearrange("(p c e) n -> c p e n", c=2, e=2)
-        x_raw = [shared.tile([P, PACK, 2 * P], F32, name="x_raw0", offset=2048, align_bytes=64)]
+        x_raw = [shared.tile([P, PACK, 2 * P], F32, name="x_raw0", offset=4096, align_bytes=64)]
         x_raw += [keep.tile([P, PACK, 2 * P], F32, name=f"x_raw{i}", align_bytes=64) for i in range(1, TILES // 2)]
         y_pair = [keep.tile([P, 2, N], F32, name=f"y_pair{i}") for i in range(TILES // 2)]
         wt_first = keep.tile([P, 2, 2], F32, name="wt_first")
@@ -78,12 +78,12 @@ def tile_attend_gsqh_pl_x_ts_kernel(tc, xT, wT, y, wt, ts, offs, out_0, out_1, o
         for c in range(PACK):
             nc.tensor.transpose(ts_turn[:, c, :], ts_listed[:, c * P : (c + 1) * P], ident[:])
         ts_col = keep.tile([P, PACK], F32, name="ts_col")
-        nc.scalar.copy(ts_col[:], ts_turn[:, :, 0])
-        ts_all = psum.tile([P, N], F32, name="ts_all", tag="bank7")
-        neg_ts = keep.tile([P, 1, N], F32, name="neg_ts")
+        nc.scalar.activation(ts_col[:], ts_turn[:, :, 0], ACT.Copy, scale=-1.0)
+        ts_bank = psum.tile([P, 1, N], F32, name="ts_bank", tag="bank7")
+        neg_ts = keep.tile([P, N], F32, name="neg_ts")
         for c in range(PACK):
-            nc.tensor.transpose(ts_all[:, c * P : (c + 1) * P], ts_col[:, c : c + 1].to_broadcast([P, P]), ident[:])
-        nc.scalar.activation(neg_ts[:, 0, :], ts_all[:], ACT.Copy, scale=-1.0)
+            nc.tensor.transpose(ts_bank[:, 0, c * P : (c + 1) * P], ts_col[:, c : c + 1].to_broadcast([P, P]), ident[:])
+        nc.scalar.copy(neg_ts[:], ts_bank[:, 0, :])
 
         w_listed = keep.tile([P, N, PACK], BF16, name="w_listed", tag="ts_row", align_bytes=64)
         w_words = w_listed[:].rearrange("p n j -> p (n j)").bitcast(F32).rearrange("p (s t u) -> p u t s", t=PACK, u=2)
@@ -105,7 +105,7 @@ def tile_attend_gsqh_pl_x_ts_kernel(tc, xT, wT, y, wt, ts, offs, out_0, out_1, o
 
         def quantise_turned(u):
             if u == 0:
-                wn["codes"] = shared.tile([P, D], U32, name="wn_codes", offset=4096, align_bytes=64)
+                wn["codes"] = shared.tile([P, D], U32, name="wn_codes", offset=7168, align_bytes=64)
             cols = slice(u * D // 2, (u + 1) * D // 2)
             nc.vector.quantize_mx(wn["codes"][:, cols].bitcast(E4M3), wn_scales[:, cols], turned[u][:].rearrange("s p e t -> s (p e t)"))
 
@@ -122,7 +122,7 @@ def tile_attend_gsqh_pl_x_ts_kernel(tc, xT, wT, y, wt, ts, offs, out_0, out_1, o
             if h == 0:
                 woven = keep.tile([P, 2, P, PACK], BF16, name="x_half0", tag="w_plane3", align_bytes=64)
             else:
-                woven = shared.tile([P, 2, P, PACK], BF16, name="x_half1", offset=2048, align_bytes=64)
+                woven = shared.tile([P, 2, P, PACK], BF16, name="x_half1", offset=3072, align_bytes=64)
             for i, copy in enumerate(copies):
                 copy(woven[:, :, i * HALF : (i + 1) * HALF, :].rearrange("p e m j -> p m j e"),
                      x_raw[h][:, :, i * P : (i + 1) * P].rearrange("p j (m e) -> p m j e", e=2))
@@ -139,16 +139,25 @@ def tile_attend_gsqh_pl_x_ts_kernel(tc, xT, wT, y, wt, ts, offs, out_0, out_1, o
         out_rows = out_0[0].rearrange("(o p t) d -> o p t d", p=P, t=PACK)
 
         def sign_scales(i):
-            if i % 2 == 0:
-                pair = keep.tile([P, 2, N], F32, name=f"signed{i}", tag="w_plane3", align_bytes=64)
+            if i == 0:
+                pair = keep.tile([P, 2, N], F32, name="signed0", tag="w_plane3", align_bytes=64)
+                nc.vector.tensor_tensor(pair[:], y_pair[0][:], ts_bank[:].to_broadcast([P, 2, N]), ALU.mult)
+                signed[0], signed[1] = pair[:, 0, :], pair[:, 1, :]
+                return
+            place = {2: 2048, 3: 4096, 5: 3072, 6: 5120}
+            if i in place:
+                one = shared.tile([P, N], F32, name=f"signed{i}", offset=place[i], align_bytes=64)
             else:
-                pair = shared.tile([P, 2, N], F32, name=f"signed{i}", offset=0, align_bytes=64)
-            nc.vector.tensor_tensor(pair[:], y_pair[i][:], neg_ts[:].to_broadcast([P, 2, N]), ALU.mult)
-            signed[2 * i], signed[2 * i + 1] = pair[:, 0, :], pair[:, 1, :]
+                one = keep.tile([P, N], F32, name=f"signed{i}", tag={4: "w_plane3", 7: "h_words1"}[i], align_bytes=64)
+            if i in (3, 5, 7,):
+                nc.gpsimd.tensor_tensor(one[:], y_pair[i // 2][:, i % 2, :], neg_ts[:], ALU.mult)
+            else:
+                nc.vector.tensor_tensor(one[:], y_pair[i // 2][:, i % 2, :], ts_bank[:, 0, :], ALU.mult)
+            signed[i] = one[:]
 
         def score(k):
             codes, scales = x_ops[k]
-            bank = psum.tile([P, N], F32, name="scores", tag=f"bank{(0, 1, 2)[k % 3]}")
+            bank = psum.tile([P, N], F32, name="scores", tag=f"bank{(0, 1)[k % 2]}")
             nc.tensor.matmul_mx(bank[:], lhsT=codes.bitcast(E4M3), lhsT_scale=scales,
                                 rhs=wd_codes[:].bitcast(E4M3), rhs_scale=wd_scales[:], start=True, stop=True)
             ya = keep.tile([P, N], F32, name=f"ya{k}", tag=f"after_ya{k}", align_bytes=64)
@@ -195,7 +204,7 @@ def tile_attend_gsqh_pl_x_ts_kernel(tc, xT, wT, y, wt, ts, offs, out_0, out_1, o
         def gradient(k, slot):
             o, t = divmod(k, PACK)
             codes, scales = h_ops[k]
-            bank = psum.tile([P, 2, P, 2], F32, name="grad", tag=f"bank{(5, 6, 7)[slot % 3]}")
+            bank = psum.tile([P, 2, P, 2], F32, name="grad", tag=f"bank{(5, 6, 2)[slot % 3]}")
             nc.tensor.matmul_mx(bank[:].rearrange("r u p e -> r (u p e)"), lhsT=codes.bitcast(E5M2), lhsT_scale=scales,
                                 rhs=wn["codes"][:].bitcast(E4M3), rhs_scale=wn_scales[:], start=True, stop=True)
             rows = grad_rows[o][:, t, :].rearrange("r (p u e) -> r p u e", u=2, e=2)
@@ -251,7 +260,8 @@ def tile_attend_gsqh_pl_x_ts_kernel(tc, xT, wT, y, wt, ts, offs, out_0, out_1, o
         score(0)
         score(1)
         turn_w(1)
-        sign_scales(1)
+        sign_scales(2)
+        sign_scales(3)
         weigh(0)
         score(2)
         weigh(1)
@@ -259,21 +269,23 @@ def tile_attend_gsqh_pl_x_ts_kernel(tc, xT, wT, y, wt, ts, offs, out_0, out_1, o
         weigh(2)
         second_x()
         weigh(3)
-        sign_scales(2)
-        score(4)
+        sign_scales(4)
+        sign_scales(5)
         quantise_turned(1)
+        sign_scales(6)
+        score(4)
         regroup(0)
         regroup(1)
         regroup(2)
         regroup(3)
         quantise_h(0, (0, 2))
         quantise_h(1, (1, 3))
-        sign_scales(3)
+        sign_scales(7)
         score(5)
-        weigh(4)
         score(6)
-        weigh(5)
+        weigh(4)
         score(7)
+        weigh(5)
         weigh(6)
         weigh(7)
         regroup(4)

@@ -18,20 +18,36 @@ ALU = mybir.AluOpType
 ACT = mybir.ActivationFunctionType
 
 P = 128
+HALF = P // 2
 PACK = 4
 PASS = P * PACK
 PASSES = R // PASS
 TILES = PASSES * PACK
-HALF = P // 2
+LAST = TILES - 1
+PAIRS = TILES // 2
+
+SCORE_BANKS = ("bank0", "bank1")
+TURN_BANKS = ("bank3", "bank4")
+GRADIENT_BANKS = ("bank5", "bank6", "bank2")
+TS_BANK = "bank7"
+
+KIB = 1024
+SHARED = {"x_raw0": 4 * KIB, "wn_codes": 7 * KIB, "x_half1": 3 * KIB,
+          "signed2": 2 * KIB, "signed3": 4 * KIB, "signed5": 3 * KIB, "signed6": 5 * KIB}
+
+SCALAR_WEAVES = D // 4
 
 
 def tile_attend_gsqh_pl_x_ts_kernel(tc, xT, wT, y, wt, ts, offs, out_0, out_1, out_2):
     nc = tc.nc
     with ExitStack() as ctx:
         keep = ctx.enter_context(tc.tile_pool(name="keep", bufs=1))
-        work = ctx.enter_context(tc.tile_pool(name="work", bufs=4))
+        hinges = ctx.enter_context(tc.tile_pool(name="hinges", bufs=PACK))
         shared = ctx.enter_context(tc.tile_pool(name="shared", bufs=1))
         psum = ctx.enter_context(tc.psum_pool(name="psum", bufs=1))
+
+        def shared_tile(name, shape, dtype):
+            return shared.tile(shape, dtype, name=name, offset=SHARED[name], align_bytes=64)
 
         offsets = keep.tile([P, N // 16], U16, name="offsets")
         ts_row = keep.tile([P, T], F32, name="ts_row", align_bytes=64)
@@ -40,180 +56,157 @@ def tile_attend_gsqh_pl_x_ts_kernel(tc, xT, wT, y, wt, ts, offs, out_0, out_1, o
         make_identity(nc, ident[:])
 
         w_rows = wT.rearrange("(p j) c -> j p c", j=PACK)
-        w_plane = [keep.tile([P, T], F32, name=f"w_plane{j}", align_bytes=64) for j in range(PACK)]
+        w_table = [keep.tile([P, T], F32, name=f"w_table{j}", align_bytes=64) for j in range(PACK)]
         x_rows = xT[0].rearrange("(p j) r -> p j r", j=PACK)
-        y_first = y[0, :PASS].rearrange("(h m e) n -> h m e n", m=P, e=2)
+        y_first = y[0, :PASS].rearrange("(a m e) n -> a m e n", m=P, e=2)
         y_second = y[0, PASS:].rearrange("(p c e) n -> c p e n", c=2, e=2)
-        x_raw = [shared.tile([P, PACK, 2 * P], F32, name="x_raw0", offset=4096, align_bytes=64)]
-        x_raw += [keep.tile([P, PACK, 2 * P], F32, name=f"x_raw{i}", align_bytes=64) for i in range(1, TILES // 2)]
-        y_pair = [keep.tile([P, 2, N], F32, name=f"y_pair{i}") for i in range(TILES // 2)]
+        x_raw = [shared_tile("x_raw0", [P, PACK, 2 * P], F32)]
+        x_raw += [keep.tile([P, PACK, 2 * P], F32, name=f"x_raw{i}", align_bytes=64) for i in range(1, PAIRS)]
+        y_pair = [keep.tile([P, 2, N], F32, name=f"y_pair{i}") for i in range(PAIRS)]
         wt_first = keep.tile([P, 2, 2], F32, name="wt_first")
         wt_second = keep.tile([P, PACK], F32, name="wt_second")
 
-        def load_x(i):
-            nc.sync.dma_start(x_raw[i][:], x_rows[:, :, i * 2 * P : (i + 1) * 2 * P])
-
-        def load_y(i):
-            nc.sync.dma_start(y_pair[i][:], y_first[i] if i < 2 else y_second[i - 2])
-
-        nc.scalar.dma_start(wt_first[:], wt[0, :PASS].rearrange("(h m e) one -> m h (e one)", m=P, e=2))
+        nc.scalar.dma_start(wt_first[:], wt[0, :PASS].rearrange("(a m e) one -> m a (e one)", m=P, e=2))
         nc.scalar.dma_start(wt_second[:], wt[0, PASS:].rearrange("(p t) one -> p (t one)", t=PACK))
         for j in range(PACK):
-            nc.sync.dma_start(w_plane[j][:], w_rows[j])
+            nc.sync.dma_start(w_table[j][:], w_rows[j])
             if j == 0:
                 nc.sync.dma_start(offsets[:], offs)
                 nc.sync.dma_start(ts_row[0:1, :], ts[0:1, :])
-        load_x(0)
-        load_x(1)
-        load_y(0)
-        load_y(1)
-        load_x(2)
-        load_x(3)
-        load_y(2)
-        load_y(3)
+        for o, y_rows in enumerate((y_first, y_second)):
+            for i in (2 * o, 2 * o + 1):
+                nc.sync.dma_start(x_raw[i][:], x_rows[:, :, i * 2 * P : (i + 1) * 2 * P])
+            for i in range(2):
+                nc.sync.dma_start(y_pair[2 * o + i][:], y_rows[i])
 
         ts_listed = keep.tile([P, N], F32, name="ts_listed")
         nc.vector.tensor_copy(ts_listed[:], ts_row[:].indirect(offsets[:]))
-        ts_turn = psum.tile([P, PACK, P], F32, name="ts_turn", tag="bank4")
+        ts_turn = psum.tile([P, PACK, P], F32, name="ts_turn", tag=TURN_BANKS[1])
         for c in range(PACK):
             nc.tensor.transpose(ts_turn[:, c, :], ts_listed[:, c * P : (c + 1) * P], ident[:])
-        ts_col = keep.tile([P, PACK], F32, name="ts_col")
-        nc.scalar.activation(ts_col[:], ts_turn[:, :, 0], ACT.Copy, scale=-1.0)
-        ts_bank = psum.tile([P, 1, N], F32, name="ts_bank", tag="bank7")
+        neg_ts_col = keep.tile([P, PACK], F32, name="neg_ts_col")
+        nc.scalar.activation(neg_ts_col[:], ts_turn[:, :, 0], ACT.Copy, scale=-1.0)
+        neg_ts_bank = psum.tile([P, 1, N], F32, name="neg_ts_bank", tag=TS_BANK)
         neg_ts = keep.tile([P, N], F32, name="neg_ts")
         for c in range(PACK):
-            nc.tensor.transpose(ts_bank[:, 0, c * P : (c + 1) * P], ts_col[:, c : c + 1].to_broadcast([P, P]), ident[:])
-        nc.scalar.copy(neg_ts[:], ts_bank[:, 0, :])
+            nc.tensor.transpose(neg_ts_bank[:, 0, c * P : (c + 1) * P], neg_ts_col[:, c : c + 1].to_broadcast([P, P]), ident[:])
+        nc.scalar.copy(neg_ts[:], neg_ts_bank[:, 0, :])
 
         w_listed = keep.tile([P, N, PACK], BF16, name="w_listed", tag="ts_row", align_bytes=64)
         w_words = w_listed[:].rearrange("p n j -> p (n j)").bitcast(F32).rearrange("p (s t u) -> p u t s", t=PACK, u=2)
         wd_codes = keep.tile([P, N], U32, name="wd_codes", align_bytes=64)
         wd_scales = keep.tile([P, N], U8, name="wd_scales", align_bytes=64)
-        turned, wn = {}, {}
         wn_scales = keep.tile([P, D], U8, name="wn_scales", align_bytes=64)
+        w_turned = {}
 
         def gather_w(j):
-            nc.vector.tensor_copy(w_listed[:, :, j], w_plane[j][:].indirect(offsets[:]))
+            nc.vector.tensor_copy(w_listed[:, :, j], w_table[j][:].indirect(offsets[:]))
 
-        def turn_w(u):
-            bank = psum.tile([P, PACK * P], F32, name=f"w_turn{u}", tag=f"bank{6 - u}")
+        def turn_w(u, tag):
+            bank = psum.tile([P, PACK * P], F32, name=f"w_turn{u}", tag=GRADIENT_BANKS[1 - u])
             for t in range(PACK):
                 nc.tensor.transpose(bank[:, t * P : (t + 1) * P], w_words[:, u, t, :], ident[:])
-            pairs = bank[:].bitcast(BF16).rearrange("s (t p e) -> s p e t", t=PACK, e=2)
-            turned[u] = keep.tile([P, P, 2, PACK], BF16, name=f"w_turned{u}", tag=("turned", "x_raw1")[u], align_bytes=64)
-            nc.scalar.copy(turned[u][:], pairs)
+            w_turned[u] = keep.tile([P, P, 2, PACK], BF16, name=f"w_turned{u}", tag=tag, align_bytes=64)
+            nc.scalar.copy(w_turned[u][:], bank[:].bitcast(BF16).rearrange("s (t p e) -> s p e t", t=PACK, e=2))
 
         def quantise_turned(u):
-            if u == 0:
-                wn["codes"] = shared.tile([P, D], U32, name="wn_codes", offset=7168, align_bytes=64)
             cols = slice(u * D // 2, (u + 1) * D // 2)
-            nc.vector.quantize_mx(wn["codes"][:, cols].bitcast(E4M3), wn_scales[:, cols], turned[u][:].rearrange("s p e t -> s (p e t)"))
+            nc.vector.quantize_mx(wn_codes[:, cols].bitcast(E4M3), wn_scales[:, cols],
+                                  w_turned[u][:].rearrange("s p e t -> s (p e t)"))
 
-        x_ops, signed, margin, h_bank, h_words, h_ops = {}, {}, {}, {}, {}, {}
+        x_ops, signed, hinge, h_bank, h_words, h_ops = {}, {}, {}, {}, {}, {}
 
-        def quantise_x(first, count, woven):
+        def quantise_x(first, count, rounded):
             codes = keep.tile([P, count * P], U32, name=f"x_codes{first}", align_bytes=64)
             scales = keep.tile([P, count * P], U8, name=f"x_scales{first}", align_bytes=64)
-            nc.vector.quantize_mx(codes[:].bitcast(E4M3), scales[:], woven)
+            nc.vector.quantize_mx(codes[:].bitcast(E4M3), scales[:], rounded)
             for i in range(count):
                 x_ops[first + i] = codes[:, i * P : (i + 1) * P], scales[:, i * P : (i + 1) * P]
 
-        def first_x(h, copies):
-            if h == 0:
-                woven = keep.tile([P, 2, P, PACK], BF16, name="x_half0", tag="w_plane3", align_bytes=64)
-            else:
-                woven = shared.tile([P, 2, P, PACK], BF16, name="x_half1", offset=3072, align_bytes=64)
+        def first_x(a, rounded, copies):
             for i, copy in enumerate(copies):
-                copy(woven[:, :, i * HALF : (i + 1) * HALF, :].rearrange("p e m j -> p m j e"),
-                     x_raw[h][:, :, i * P : (i + 1) * P].rearrange("p j (m e) -> p m j e", e=2))
-            quantise_x(2 * h, 2, woven[:].rearrange("p e m j -> p (e m j)"))
+                copy(rounded[:, :, i * HALF : (i + 1) * HALF, :].rearrange("p e m j -> p m j e"),
+                     x_raw[a][:, :, i * P : (i + 1) * P].rearrange("p j (m e) -> p m j e", e=2))
+            quantise_x(2 * a, 2, rounded[:].rearrange("p e m j -> p (e m j)"))
 
         def second_x():
-            woven = keep.tile([P, PACK, P, PACK], BF16, name="x_dealt", tag="after_ya0", align_bytes=64)
+            rounded = keep.tile([P, PACK, P, PACK], BF16, name="x_second", tag="neg_ya0", align_bytes=64)
             for i in range(PACK):
-                (nc.scalar.copy, nc.scalar.copy, nc.scalar.copy, nc.scalar.copy)[i](woven[:, :, i * P // PACK : (i + 1) * P // PACK, :].rearrange("p t m j -> p m j t"),
+                nc.scalar.copy(rounded[:, :, i * P // PACK : (i + 1) * P // PACK, :].rearrange("p t m j -> p m j t"),
                                x_raw[2 + i // 2][:, :, i % 2 * P : (i % 2 + 1) * P].rearrange("p j (m t) -> p m j t", t=PACK))
-            quantise_x(PACK, PACK, woven[:].rearrange("p t m j -> p (t m j)"))
+            quantise_x(PACK, PACK, rounded[:].rearrange("p t m j -> p (t m j)"))
 
-        grad_rows = [keep.tile([P, PACK, D], F32, name=f"grad_rows{o}") for o in range(PASSES)]
-        out_rows = out_0[0].rearrange("(o p t) d -> o p t d", p=P, t=PACK)
+        def sign_first_pair():
+            pair = keep.tile([P, 2, N], F32, name="signed_pair", tag="w_table3", align_bytes=64)
+            nc.vector.tensor_tensor(pair[:], y_pair[0][:], neg_ts_bank[:].to_broadcast([P, 2, N]), ALU.mult)
+            signed[0], signed[1] = pair[:, 0, :], pair[:, 1, :]
 
-        def sign_scales(i):
-            if i == 0:
-                pair = keep.tile([P, 2, N], F32, name="signed0", tag="w_plane3", align_bytes=64)
-                nc.vector.tensor_tensor(pair[:], y_pair[0][:], ts_bank[:].to_broadcast([P, 2, N]), ALU.mult)
-                signed[0], signed[1] = pair[:, 0, :], pair[:, 1, :]
-                return
-            place = {2: 2048, 3: 4096, 5: 3072, 6: 5120}
-            if i in place:
-                one = shared.tile([P, N], F32, name=f"signed{i}", offset=place[i], align_bytes=64)
+        def sign(k, tile):
+            if k % 2 == 1:
+                nc.gpsimd.tensor_tensor(tile[:], y_pair[k // 2][:, 1, :], neg_ts[:], ALU.mult)
             else:
-                one = keep.tile([P, N], F32, name=f"signed{i}", tag={4: "w_plane3", 7: "h_words1"}[i], align_bytes=64)
-            if i in (3, 5, 7,):
-                nc.gpsimd.tensor_tensor(one[:], y_pair[i // 2][:, i % 2, :], neg_ts[:], ALU.mult)
-            else:
-                nc.vector.tensor_tensor(one[:], y_pair[i // 2][:, i % 2, :], ts_bank[:, 0, :], ALU.mult)
-            signed[i] = one[:]
+                nc.vector.tensor_tensor(tile[:], y_pair[k // 2][:, 0, :], neg_ts_bank[:, 0, :], ALU.mult)
+            signed[k] = tile[:]
 
         def score(k):
             codes, scales = x_ops[k]
-            bank = psum.tile([P, N], F32, name="scores", tag=f"bank{(0, 1)[k % 2]}")
+            bank = psum.tile([P, N], F32, name="scores", tag=SCORE_BANKS[k % 2])
             nc.tensor.matmul_mx(bank[:], lhsT=codes.bitcast(E4M3), lhsT_scale=scales,
                                 rhs=wd_codes[:].bitcast(E4M3), rhs_scale=wd_scales[:], start=True, stop=True)
-            ya = keep.tile([P, N], F32, name=f"ya{k}", tag=f"after_ya{k}", align_bytes=64)
-            nc.vector.tensor_tensor(ya[:], bank[:], signed[k], ALU.mult)
-            margin[k] = work.tile([P, N], F32, name="margin", tag="margin")
-            nc.scalar.activation(margin[k][:], ya[:], ACT.Relu, bias=1.0, scale=1.0)
+            neg_ya = keep.tile([P, N], F32, name=f"neg_ya{k}", align_bytes=64)
+            nc.vector.tensor_tensor(neg_ya[:], bank[:], signed[k], ALU.mult)
+            hinge[k] = hinges.tile([P, N], F32, name="hinge")
+            nc.scalar.activation(hinge[k][:], neg_ya[:], ACT.Relu, bias=1.0, scale=1.0)
 
         def weigh(k):
-            h = keep.tile([P, N], BF16, name=f"h{k}", tag=f"after_h{k}", align_bytes=64)
+            h = keep.tile([P, N], BF16, name=f"h{k}", align_bytes=64)
             weight = wt_first[:, k // 2, k % 2 : k % 2 + 1] if k < PACK else wt_second[:, k - PACK : k - PACK + 1]
-            if k == TILES - 1:
+            if k == LAST:
                 for u in range(2):
                     nc.vector.scalar_tensor_tensor(h[:].rearrange("r (u s e) -> r u s e", u=2, e=2)[:, u],
-                                                   margin[k][:].rearrange("r (s u e) -> r u s e", u=2, e=2)[:, u], weight,
+                                                   hinge[k][:].rearrange("r (s u e) -> r u s e", u=2, e=2)[:, u], weight,
                                                    signed[k].rearrange("r (s u e) -> r u s e", u=2, e=2)[:, u], ALU.mult, ALU.mult)
                 words = h[:].bitcast(F32).rearrange("r (u s) -> r u s", u=2)
             else:
-                nc.vector.scalar_tensor_tensor(h[:], margin[k][:], weight, signed[k], ALU.mult, ALU.mult)
+                nc.vector.scalar_tensor_tensor(h[:], hinge[k][:], weight, signed[k], ALU.mult, ALU.mult)
                 words = h[:].bitcast(F32).rearrange("r (s u) -> r u s", u=2)
-            bank = psum.tile([P, 2, P], F32, name="h_turn", tag=f"bank{3 + k % 2}")
+            h_bank[k] = psum.tile([P, 2, P], F32, name="h_turn", tag=TURN_BANKS[k % 2])
             for u in range(2):
-                nc.tensor.transpose(bank[:, u, :], words[:, u, :], ident[:])
-            h_bank[k] = bank
+                nc.tensor.transpose(h_bank[k][:, u, :], words[:, u, :], ident[:])
 
-        def regroup(k):
-            bank = h_bank[k]
-            if k < PACK:
-                half, e = divmod(k, 2)
-                if half == 0:
-                    h_words[e] = keep.tile([P, 2, P, 2], F32, name=f"h_words{e}", align_bytes=64)
-                nc.scalar.copy(h_words[e][:, :, half * HALF : (half + 1) * HALF, :].rearrange("s c m u -> s m c u"),
-                               bank[:].rearrange("s u (m c) -> s m c u", c=2))
-            else:
-                h_words[k] = keep.tile([P, 1, P, 2], F32, name=f"h_words{k}", align_bytes=64)
-                nc.scalar.copy(h_words[k][:, 0], bank[:].rearrange("s u r -> s r u"))
+        def regroup_first(k):
+            a, e = divmod(k, 2)
+            if a == 0:
+                h_words[e] = keep.tile([P, 2, P, 2], F32, name=f"h_words{e}", align_bytes=64)
+            nc.scalar.copy(h_words[e][:, :, a * HALF : (a + 1) * HALF, :].rearrange("s c i u -> s i c u"),
+                           h_bank[k][:].rearrange("s u (i c) -> s i c u", c=2))
 
-        def quantise_h(first, tiles):
-            codes = keep.tile([P, len(tiles) * P], U32, name=f"h_codes{first}", align_bytes=64)
-            scales = keep.tile([P, len(tiles) * P], U8, name=f"h_scales{first}", align_bytes=64)
-            nc.vector.quantize_mx(codes[:].bitcast(E5M2), scales[:], h_words[first][:].rearrange("s t r u -> s (t r u)").bitcast(BF16))
-            for i, k in enumerate(tiles):
-                h_ops[k] = codes[:, i * P : (i + 1) * P], scales[:, i * P : (i + 1) * P]
+        def regroup_second(k):
+            h_words[k] = keep.tile([P, 1, P, 2], F32, name=f"h_words{k}", align_bytes=64)
+            nc.scalar.copy(h_words[k][:, 0], h_bank[k][:].rearrange("s u r -> s r u"))
 
-        def gradient(k, slot):
-            o, t = divmod(k, PACK)
-            codes, scales = h_ops[k]
-            bank = psum.tile([P, 2, P, 2], F32, name="grad", tag=f"bank{(5, 6, 2)[slot % 3]}")
-            nc.tensor.matmul_mx(bank[:].rearrange("r u p e -> r (u p e)"), lhsT=codes.bitcast(E5M2), lhsT_scale=scales,
-                                rhs=wn["codes"][:].bitcast(E4M3), rhs_scale=wn_scales[:], start=True, stop=True)
-            rows = grad_rows[o][:, t, :].rearrange("r (p u e) -> r p u e", u=2, e=2)
-            cuts = (0, HALF, P) if k == TILES - 1 else (0, P)
-            for a, b in zip(cuts, cuts[1:]):
-                nc.scalar.copy(rows[:, a:b], bank[:, :, a:b, :].rearrange("r u p e -> r p u e"))
-            nc.sync.dma_start(out_rows[o, :, t, :], grad_rows[o][:, t, :])
+        def quantise_h(group, places):
+            codes = keep.tile([P, len(places) * P], U32, name=f"h_codes{group}", align_bytes=64)
+            scales = keep.tile([P, len(places) * P], U8, name=f"h_scales{group}", align_bytes=64)
+            nc.vector.quantize_mx(codes[:].bitcast(E5M2), scales[:],
+                                  h_words[group][:].rearrange("s i r u -> s (i r u)").bitcast(BF16))
+            for i, place in enumerate(places):
+                h_ops[place] = codes[:, i * P : (i + 1) * P], scales[:, i * P : (i + 1) * P]
 
+        grad_rows = [keep.tile([P, PACK, D], F32, name=f"grad_rows{o}") for o in range(PASSES)]
+        out_rows = out_0[0].rearrange("(o p t) d -> o p t d", p=P, t=PACK)
         out_scales = keep.tile([P, PASSES, D], U8, name="out_scales", align_bytes=64)
+
+        def gradient(o, t, tag):
+            codes, scales = h_ops[o, t]
+            bank = psum.tile([P, 2, P, 2], F32, name="grad", tag=tag)
+            nc.tensor.matmul_mx(bank[:].rearrange("r u p e -> r (u p e)"), lhsT=codes.bitcast(E5M2), lhsT_scale=scales,
+                                rhs=wn_codes[:].bitcast(E4M3), rhs_scale=wn_scales[:], start=True, stop=True)
+            rows = grad_rows[o][:, t, :].rearrange("r (p u e) -> r p u e", u=2, e=2)
+            cuts = (0, HALF, P) if (o, t) == (PASSES - 1, PACK - 1) else (0, P)
+            for start, stop in zip(cuts, cuts[1:]):
+                nc.scalar.copy(rows[:, start:stop], bank[:, :, start:stop, :].rearrange("r u p e -> r p u e"))
+            nc.sync.dma_start(out_rows[o, :, t, :], grad_rows[o][:, t, :])
 
         def weave(copy, woven, o, first, start, stop):
             copy(woven[:, start - first : stop - first, :].rearrange("p (c i) t -> p c t i", i=4),
@@ -224,15 +217,12 @@ def tile_attend_gsqh_pl_x_ts_kernel(tc, xT, wT, y, wt, ts, offs, out_0, out_1, o
             words_out = out_1[o].rearrange("p d l -> p (d l)").bitcast(I32)
             half = D // 2
             last = o == PASSES - 1
-            woven = [keep.tile([P, half, PACK], BF16, name=f"woven{o}{c}", tag=f"woven{c}" if last else ("after_ya7", "after_h7")[c], align_bytes=64)
-                     for c in range(2)]
+            tags = ("woven0", "woven1") if last else (f"neg_ya{LAST}", f"h{LAST}")
+            woven = [keep.tile([P, half, PACK], BF16, name=f"woven{o}{c}", tag=tags[c], align_bytes=64) for c in range(2)]
+            weave(nc.vector.tensor_copy, woven[0], o, 0, 0, half)
             if last:
-                weave(nc.vector.tensor_copy, woven[0], o, 0, 0, half)
-                weave(nc.scalar.copy, woven[1], o, half, D - D // 4, D)
-                weave(nc.vector.tensor_copy, woven[1], o, half, half, D - D // 4)
-            else:
-                for c in range(2):
-                    weave(nc.vector.tensor_copy, woven[c], o, c * half, c * half, (c + 1) * half)
+                weave(nc.scalar.copy, woven[1], o, half, D - SCALAR_WEAVES, D)
+            weave(nc.vector.tensor_copy, woven[1], o, half, half, D - SCALAR_WEAVES if last else D)
             for c in range(2):
                 cols = slice(c * half, (c + 1) * half)
                 nc.vector.quantize_mx(codes[:, cols].bitcast(E4M3), out_scales[:, o, cols], woven[c][:].rearrange("p d t -> p (d t)"))
@@ -241,69 +231,58 @@ def tile_attend_gsqh_pl_x_ts_kernel(tc, xT, wT, y, wt, ts, offs, out_0, out_1, o
             if not last:
                 nc.sync.dma_start(words_out, codes[:].bitcast(I32))
 
-        def store_scales():
-            for q in range(4):
-                queue = nc.scalar if q % 2 == 0 else nc.sync
-                queue.dma_start(out_2[:, 4 * q : 4 * q + 4, :].rearrange("o i d -> i o d").bitcast(I32),
-                                out_scales[32 * q : 32 * q + 4].bitcast(I32))
-
         gather_w(0)
         gather_w(1)
-        turn_w(0)
+        turn_w(0, "w_turned0")
         gather_w(2)
         gather_w(3)
         nc.vector.quantize_mx(wd_codes[:].bitcast(E4M3), wd_scales[:], w_listed[:].rearrange("p n j -> p (n j)"))
-        first_x(0, (nc.scalar.copy, nc.vector.tensor_copy))
+        x_half0 = keep.tile([P, 2, P, PACK], BF16, name="x_half0", tag="w_table3", align_bytes=64)
+        first_x(0, x_half0, (nc.scalar.copy, nc.vector.tensor_copy))
+        wn_codes = shared_tile("wn_codes", [P, D], U32)
         quantise_turned(0)
-        first_x(1, (nc.scalar.copy, nc.scalar.copy))
-        sign_scales(0)
+        first_x(1, shared_tile("x_half1", [P, 2, P, PACK], BF16), (nc.scalar.copy, nc.scalar.copy))
+
+        sign_first_pair()
         score(0)
         score(1)
-        turn_w(1)
-        sign_scales(2)
-        sign_scales(3)
-        weigh(0)
-        score(2)
-        weigh(1)
-        score(3)
-        weigh(2)
-        second_x()
-        weigh(3)
-        sign_scales(4)
-        sign_scales(5)
+        turn_w(1, "x_raw1")
+        for k in (2, 3):
+            sign(k, shared_tile(f"signed{k}", [P, N], F32))
+        for k in range(PACK):
+            weigh(k)
+            if k + 2 < PACK:
+                score(k + 2)
+            if k + 2 == PACK:
+                second_x()
+
+        sign(4, keep.tile([P, N], F32, name="signed4", tag="w_table3", align_bytes=64))
+        sign(5, shared_tile("signed5", [P, N], F32))
         quantise_turned(1)
-        sign_scales(6)
+        sign(6, shared_tile("signed6", [P, N], F32))
         score(4)
-        regroup(0)
-        regroup(1)
-        regroup(2)
-        regroup(3)
-        quantise_h(0, (0, 2))
-        quantise_h(1, (1, 3))
-        sign_scales(7)
+        for k in range(PACK):
+            regroup_first(k)
+        quantise_h(0, ((0, 0), (0, 2)))
+        sign(7, keep.tile([P, N], F32, name="signed7", tag="h_words0", align_bytes=64))
         score(5)
         score(6)
+        quantise_h(1, ((0, 1), (0, 3)))
+
         weigh(4)
-        score(7)
-        weigh(5)
-        weigh(6)
-        weigh(7)
-        regroup(4)
-        quantise_h(4, (4,))
-        regroup(5)
-        quantise_h(5, (5,))
-        regroup(6)
-        quantise_h(6, (6,))
-        regroup(7)
-        quantise_h(7, (7,))
-        gradient(0, 0)
-        gradient(2, 1)
-        gradient(1, 2)
-        gradient(3, 3)
-        gradient(4, 4)
-        gradient(5, 5)
-        gradient(6, 6)
-        gradient(7, 7)
+        score(LAST)
+        for k in range(PACK + 1, TILES):
+            weigh(k)
+        for t in range(PACK):
+            regroup_second(PACK + t)
+            quantise_h(PACK + t, ((1, t),))
+        places = [(0, 0), (0, 2), (0, 1), (0, 3)] + [(1, t) for t in range(PACK)]
+        for i, (o, t) in enumerate(places):
+            gradient(o, t, GRADIENT_BANKS[i % len(GRADIENT_BANKS)])
         for o in range(PASSES):
             planes(o)
-        store_scales()
+
+        for q in range(4):
+            queue = nc.scalar if q % 2 == 0 else nc.sync
+            queue.dma_start(out_2[:, 4 * q : 4 * q + 4, :].rearrange("o i d -> i o d").bitcast(I32),
+                            out_scales[32 * q : 32 * q + 4].bitcast(I32))

@@ -26,43 +26,37 @@ TILES = PASSES * PACK
 LAST = TILES - 1
 PAIRS = TILES // 2
 
-SCORE_BANKS = ("bank0", "bank1")
+SCORE_BANKS = ("bank0", "bank1", "bank2")
 TURN_BANKS = ("bank3", "bank4")
 GRADIENT_BANKS = ("bank5", "bank6", "bank2")
 TS_BANK = "bank7"
-
-KIB = 1024
-SHARED = {"x_raw0": 4 * KIB, "wn_codes": 7 * KIB, "x_half1": 3 * KIB,
-          "signed2": 2 * KIB, "signed3": 4 * KIB, "signed5": 3 * KIB, "signed6": 5 * KIB}
-
-SCALAR_WEAVES = D // 4
 
 
 def tile_attend_gsqh_pl_x_ts_kernel(tc, xT, wT, y, wt, ts, offs, out_0, out_1, out_2):
     nc = tc.nc
     with ExitStack() as ctx:
         keep = ctx.enter_context(tc.tile_pool(name="keep", bufs=1))
-        hinges = ctx.enter_context(tc.tile_pool(name="hinges", bufs=PACK))
         shared = ctx.enter_context(tc.tile_pool(name="shared", bufs=1))
         psum = ctx.enter_context(tc.psum_pool(name="psum", bufs=1))
 
-        def shared_tile(name, shape, dtype):
-            return shared.tile(shape, dtype, name=name, offset=SHARED[name], align_bytes=64)
+        def tile(name, shape, dtype, on=None):
+            if isinstance(on, int):
+                return shared.tile(shape, dtype, name=name, offset=on * 1024, align_bytes=64)
+            return keep.tile(shape, dtype, name=name, tag=on or name, align_bytes=64)
 
         offsets = keep.tile([P, N // 16], U16, name="offsets")
-        ts_row = keep.tile([P, T], F32, name="ts_row", align_bytes=64)
+        ts_row = tile("ts_row", [P, T], F32)
         nc.vector.memset(ts_row[:], 0.0)
         ident = keep.tile([P, P], F32, name="ident")
         make_identity(nc, ident[:])
 
         w_rows = wT.rearrange("(p j) c -> j p c", j=PACK)
-        w_table = [keep.tile([P, T], F32, name=f"w_table{j}", align_bytes=64) for j in range(PACK)]
+        w_table = [tile(f"w_table{j}", [P, T], F32) for j in range(PACK)]
         x_rows = xT[0].rearrange("(p j) r -> p j r", j=PACK)
         y_first = y[0, :PASS].rearrange("(a m e) n -> a m e n", m=P, e=2)
         y_second = y[0, PASS:].rearrange("(p c e) n -> c p e n", c=2, e=2)
-        x_raw = [shared_tile("x_raw0", [P, PACK, 2 * P], F32)]
-        x_raw += [keep.tile([P, PACK, 2 * P], F32, name=f"x_raw{i}", align_bytes=64) for i in range(1, PAIRS)]
-        y_pair = [keep.tile([P, 2, N], F32, name=f"y_pair{i}") for i in range(PAIRS)]
+        x_raw = [tile(f"x_raw{i}", [P, PACK, 2 * P], F32) for i in range(PAIRS)]
+        y_pair = [tile(f"y_pair{i}", [P, 2, N], F32) for i in range(PAIRS)]
         wt_first = keep.tile([P, 2, 2], F32, name="wt_first")
         wt_second = keep.tile([P, PACK], F32, name="wt_second")
 
@@ -73,214 +67,318 @@ def tile_attend_gsqh_pl_x_ts_kernel(tc, xT, wT, y, wt, ts, offs, out_0, out_1, o
             if j == 0:
                 nc.sync.dma_start(offsets[:], offs)
                 nc.sync.dma_start(ts_row[0:1, :], ts[0:1, :])
-        for o, y_rows in enumerate((y_first, y_second)):
-            for i in (2 * o, 2 * o + 1):
-                nc.sync.dma_start(x_raw[i][:], x_rows[:, :, i * 2 * P : (i + 1) * 2 * P])
-            for i in range(2):
-                nc.sync.dma_start(y_pair[2 * o + i][:], y_rows[i])
 
-        ts_listed = keep.tile([P, N], F32, name="ts_listed")
-        nc.vector.tensor_copy(ts_listed[:], ts_row[:].indirect(offsets[:]))
-        ts_turn = psum.tile([P, PACK, P], F32, name="ts_turn", tag=TURN_BANKS[1])
-        for c in range(PACK):
-            nc.tensor.transpose(ts_turn[:, c, :], ts_listed[:, c * P : (c + 1) * P], ident[:])
-        neg_ts_col = keep.tile([P, PACK], F32, name="neg_ts_col")
-        nc.scalar.activation(neg_ts_col[:], ts_turn[:, :, 0], ACT.Copy, scale=-1.0)
+        def load_x(i):
+            nc.sync.dma_start(x_raw[i][:], x_rows[:, :, i * 2 * P : (i + 1) * 2 * P])
+
+        def load_y(i):
+            nc.sync.dma_start(y_pair[i][:], (y_first, y_second)[i // 2][i % 2])
+
+        load_x(0)
+        load_y(0)
+        load_x(1)
+        load_y(1)
+        load_x(2)
+        load_x(3)
+        load_y(2)
+        load_y(3)
+
         neg_ts_bank = psum.tile([P, 1, N], F32, name="neg_ts_bank", tag=TS_BANK)
-        neg_ts = keep.tile([P, N], F32, name="neg_ts")
-        for c in range(PACK):
-            nc.tensor.transpose(neg_ts_bank[:, 0, c * P : (c + 1) * P], neg_ts_col[:, c : c + 1].to_broadcast([P, P]), ident[:])
-        nc.scalar.copy(neg_ts[:], neg_ts_bank[:, 0, :])
+        neg_ts = tile("neg_ts", [P, 1, N], F32)
 
-        w_listed = keep.tile([P, N, PACK], BF16, name="w_listed", tag="ts_row", align_bytes=64)
+        def spread_ts():
+            ts_listed = tile("ts_listed", [P, N], F32)
+            nc.vector.tensor_copy(ts_listed[:], ts_row[:].indirect(offsets[:]))
+            ts_turn = psum.tile([P, PACK, P], F32, name="ts_turn", tag=TURN_BANKS[1])
+            for c in range(PACK):
+                nc.tensor.transpose(ts_turn[:, c, :], ts_listed[:, c * P : (c + 1) * P], ident[:])
+            neg_ts_col = tile("neg_ts_col", [P, PACK], F32)
+            nc.scalar.activation(neg_ts_col[:], ts_turn[:, :, 0], ACT.Copy, scale=-1.0)
+            for c in range(PACK):
+                nc.tensor.transpose(neg_ts_bank[:, 0, c * P : (c + 1) * P], neg_ts_col[:, c : c + 1].to_broadcast([P, P]), ident[:])
+            nc.scalar.copy(neg_ts[:], neg_ts_bank[:])
+
+        def weight(first, second, k):
+            return first[:, k // 2, k % 2 : k % 2 + 1] if k < PACK else second[:, k - PACK : k - PACK + 1]
+
+        w_listed = tile("w_listed", [P, N, PACK], BF16)
         w_words = w_listed[:].rearrange("p n j -> p (n j)").bitcast(F32).rearrange("p (s t u) -> p u t s", t=PACK, u=2)
-        wd_codes = keep.tile([P, N], U32, name="wd_codes", align_bytes=64)
-        wd_scales = keep.tile([P, N], U8, name="wd_scales", align_bytes=64)
-        wn_scales = keep.tile([P, D], U8, name="wn_scales", align_bytes=64)
-        w_turned = {}
+        wd_codes = tile("wd_codes", [P, N], U32)
+        wd_scales = tile("wd_scales", [P, N], U8)
+        wn_scales = tile("wn_scales", [P, D], U8)
+        w_bank, w_turned, wn = {}, {}, {}
 
         def gather_w(j):
             nc.vector.tensor_copy(w_listed[:, :, j], w_table[j][:].indirect(offsets[:]))
 
-        def turn_w(u, tag):
-            bank = psum.tile([P, PACK * P], F32, name=f"w_turn{u}", tag=GRADIENT_BANKS[1 - u])
-            for t in range(PACK):
-                nc.tensor.transpose(bank[:, t * P : (t + 1) * P], w_words[:, u, t, :], ident[:])
-            w_turned[u] = keep.tile([P, P, 2, PACK], BF16, name=f"w_turned{u}", tag=tag, align_bytes=64)
-            nc.scalar.copy(w_turned[u][:], bank[:].bitcast(BF16).rearrange("s (t p e) -> s p e t", t=PACK, e=2))
+        def quantise_w():
+            nc.vector.quantize_mx(wd_codes[:].bitcast(E4M3), wd_scales[:], w_listed[:].rearrange("p n j -> p (n j)"))
 
-        def quantise_turned(u):
+        def turn_w(u, bank=None):
+            w_bank[u] = psum.tile([P, PACK * P], F32, name=f"w_turn{u}", tag=bank or GRADIENT_BANKS[1 - u])
+            for t in range(PACK):
+                nc.tensor.transpose(w_bank[u][:, t * P : (t + 1) * P], w_words[:, u, t, :], ident[:])
+
+        def copy_w(u, on=None):
+            w_turned[u] = tile(f"w_turned{u}", [P, P, 2, PACK], BF16, on)
+            nc.scalar.copy(w_turned[u][:], w_bank[u][:].bitcast(BF16).rearrange("s (t p e) -> s p e t", t=PACK, e=2))
+
+        def quantise_turned(u, on=None):
+            if u == 0:
+                wn["codes"] = tile("wn_codes", [P, D], U32, on)
             cols = slice(u * D // 2, (u + 1) * D // 2)
-            nc.vector.quantize_mx(wn_codes[:, cols].bitcast(E4M3), wn_scales[:, cols],
+            nc.vector.quantize_mx(wn["codes"][:, cols].bitcast(E4M3), wn_scales[:, cols],
                                   w_turned[u][:].rearrange("s p e t -> s (p e t)"))
 
-        x_ops, signed, hinge, h_bank, h_words, h_ops = {}, {}, {}, {}, {}, {}
+        x_round, x_ops, signed, scores, neg_ya, hinge, h, h_bank, h_words, h_ops, g_bank = ({} for i in range(11))
 
-        def quantise_x(first, count, rounded):
-            codes = keep.tile([P, count * P], U32, name=f"x_codes{first}", align_bytes=64)
-            scales = keep.tile([P, count * P], U8, name=f"x_scales{first}", align_bytes=64)
-            nc.vector.quantize_mx(codes[:].bitcast(E4M3), scales[:], rounded)
+        def round_first(a, i, copy, on=None):
+            if a not in x_round:
+                x_round[a] = tile(f"x_half{a}", [P, 2, P, PACK], BF16, on)
+            copy(x_round[a][:, :, i * HALF : (i + 1) * HALF, :].rearrange("p e m j -> p m j e"),
+                 x_raw[a][:, :, i * P : (i + 1) * P].rearrange("p j (m e) -> p m j e", e=2))
+
+        def round_tile(k, copy, on=None):
+            rounded = tile(f"x_tile{k}", [P, P, PACK], BF16, on)
+            copy(rounded[:].rearrange("p (c i) j -> p c j i", i=2),
+                 x_raw[k // 2][:].rearrange("p j (c i e) -> p e c j i", i=2, e=2)[:, k % 2])
+            x_round["tile", k] = rounded
+
+        def quantise_tile(k):
+            codes = tile(f"x_codes{k}", [P, P], U32)
+            scales = tile(f"x_scales{k}", [P, P], U8)
+            nc.vector.quantize_mx(codes[:].bitcast(E4M3), scales[:], x_round["tile", k][:].rearrange("p m j -> p (m j)"))
+            x_ops[k] = codes[:], scales[:]
+
+        def round_second(i, copy, on=None):
+            if 2 not in x_round:
+                x_round[2] = tile("x_second", [P, PACK, P, PACK], BF16, on)
+            copy(x_round[2][:, :, i * P // PACK : (i + 1) * P // PACK, :].rearrange("p t m j -> p m j t"),
+                 x_raw[2 + i // 2][:, :, i % 2 * P : (i % 2 + 1) * P].rearrange("p j (m t) -> p m j t", t=PACK))
+
+        def quantise_x(a, on=None):
+            first, count = 2 * a, 2 if a < 2 else PACK
+            codes = tile(f"x_codes{first}", [P, count * P], U32, on)
+            scales = tile(f"x_scales{first}", [P, count * P], U8)
+            nc.vector.quantize_mx(codes[:].bitcast(E4M3), scales[:], x_round[a][:].rearrange("p e m j -> p (e m j)"))
             for i in range(count):
                 x_ops[first + i] = codes[:, i * P : (i + 1) * P], scales[:, i * P : (i + 1) * P]
 
-        def first_x(a, rounded, copies):
-            for i, copy in enumerate(copies):
-                copy(rounded[:, :, i * HALF : (i + 1) * HALF, :].rearrange("p e m j -> p m j e"),
-                     x_raw[a][:, :, i * P : (i + 1) * P].rearrange("p j (m e) -> p m j e", e=2))
-            quantise_x(2 * a, 2, rounded[:].rearrange("p e m j -> p (e m j)"))
+        def sign_pair(i, on=None):
+            pair = tile(f"signed_pair{i}", [P, 2, N], F32, on)
+            nc.vector.tensor_tensor(pair[:], y_pair[i][:], neg_ts_bank[:].to_broadcast([P, 2, N]), ALU.mult)
+            signed[2 * i], signed[2 * i + 1] = pair[:, 0, :], pair[:, 1, :]
 
-        def second_x():
-            rounded = keep.tile([P, PACK, P, PACK], BF16, name="x_second", tag="neg_ya0", align_bytes=64)
-            for i in range(PACK):
-                nc.scalar.copy(rounded[:, :, i * P // PACK : (i + 1) * P // PACK, :].rearrange("p t m j -> p m j t"),
-                               x_raw[2 + i // 2][:, :, i % 2 * P : (i % 2 + 1) * P].rearrange("p j (m t) -> p m j t", t=PACK))
-            quantise_x(PACK, PACK, rounded[:].rearrange("p t m j -> p (t m j)"))
+        def sign_pair_aside(i, on=None, cut=0):
+            pair = tile(f"signed_pair{i}", [P, 2, N], F32, on)
+            nc.gpsimd.tensor_tensor(pair[:, :, cut:], y_pair[i][:, :, cut:], neg_ts[:, :, cut:].to_broadcast([P, 2, N - cut]), ALU.mult)
+            if cut:
+                nc.vector.tensor_tensor(pair[:, :, :cut], y_pair[i][:, :, :cut], neg_ts_bank[:, :, :cut].to_broadcast([P, 2, cut]), ALU.mult)
+            signed[2 * i], signed[2 * i + 1] = pair[:, 0, :], pair[:, 1, :]
 
-        def sign_first_pair():
-            pair = keep.tile([P, 2, N], F32, name="signed_pair", tag="w_table3", align_bytes=64)
-            nc.vector.tensor_tensor(pair[:], y_pair[0][:], neg_ts_bank[:].to_broadcast([P, 2, N]), ALU.mult)
-            signed[0], signed[1] = pair[:, 0, :], pair[:, 1, :]
+        def sign(k, on=None):
+            signed[k] = tile(f"signed{k}", [P, N], F32, on)[:]
+            nc.vector.tensor_tensor(signed[k], y_pair[k // 2][:, k % 2, :], neg_ts_bank[:, 0, :], ALU.mult)
 
-        def sign(k, tile):
-            if k % 2 == 1:
-                nc.gpsimd.tensor_tensor(tile[:], y_pair[k // 2][:, 1, :], neg_ts[:], ALU.mult)
-            else:
-                nc.vector.tensor_tensor(tile[:], y_pair[k // 2][:, 0, :], neg_ts_bank[:, 0, :], ALU.mult)
-            signed[k] = tile[:]
+        def sign_aside(k, on=None):
+            signed[k] = tile(f"signed{k}", [P, N], F32, on)[:]
+            nc.gpsimd.tensor_tensor(signed[k], y_pair[k // 2][:, k % 2, :], neg_ts[:, 0, :], ALU.mult)
 
         def score(k):
             codes, scales = x_ops[k]
-            bank = psum.tile([P, N], F32, name="scores", tag=SCORE_BANKS[k % 2])
-            nc.tensor.matmul_mx(bank[:], lhsT=codes.bitcast(E4M3), lhsT_scale=scales,
+            scores[k] = psum.tile([P, N], F32, name="scores", tag=SCORE_BANKS[k % 3])
+            nc.tensor.matmul_mx(scores[k][:], lhsT=codes.bitcast(E4M3), lhsT_scale=scales,
                                 rhs=wd_codes[:].bitcast(E4M3), rhs_scale=wd_scales[:], start=True, stop=True)
-            neg_ya = keep.tile([P, N], F32, name=f"neg_ya{k}", align_bytes=64)
-            nc.vector.tensor_tensor(neg_ya[:], bank[:], signed[k], ALU.mult)
-            hinge[k] = hinges.tile([P, N], F32, name="hinge")
-            nc.scalar.activation(hinge[k][:], neg_ya[:], ACT.Relu, bias=1.0, scale=1.0)
 
-        def weigh(k):
-            h = keep.tile([P, N], BF16, name=f"h{k}", align_bytes=64)
-            weight = wt_first[:, k // 2, k % 2 : k % 2 + 1] if k < PACK else wt_second[:, k - PACK : k - PACK + 1]
+        def margin(k, on=None):
+            neg_ya[k] = tile(f"neg_ya{k}", [P, N], F32, on)
+            nc.vector.tensor_tensor(neg_ya[k][:], scores[k][:], signed[k], ALU.mult)
+
+        def clip(k, on=None):
+            hinge[k] = tile(f"hinge{k}", [P, N], F32, on)
+            nc.scalar.activation(hinge[k][:], neg_ya[k][:], ACT.Relu, bias=1.0, scale=1.0)
+
+        def weigh(k, on=None):
+            h[k] = tile(f"h{k}", [P, N], BF16, on)
+            factor = weight(wt_first, wt_second, k)
             if k == LAST:
                 for u in range(2):
-                    nc.vector.scalar_tensor_tensor(h[:].rearrange("r (u s e) -> r u s e", u=2, e=2)[:, u],
-                                                   hinge[k][:].rearrange("r (s u e) -> r u s e", u=2, e=2)[:, u], weight,
+                    nc.vector.scalar_tensor_tensor(h[k][:].rearrange("r (u s e) -> r u s e", u=2, e=2)[:, u],
+                                                   hinge[k][:].rearrange("r (s u e) -> r u s e", u=2, e=2)[:, u], factor,
                                                    signed[k].rearrange("r (s u e) -> r u s e", u=2, e=2)[:, u], ALU.mult, ALU.mult)
-                words = h[:].bitcast(F32).rearrange("r (u s) -> r u s", u=2)
             else:
-                nc.vector.scalar_tensor_tensor(h[:], hinge[k][:], weight, signed[k], ALU.mult, ALU.mult)
-                words = h[:].bitcast(F32).rearrange("r (s u) -> r u s", u=2)
+                nc.vector.scalar_tensor_tensor(h[k][:], hinge[k][:], factor, signed[k], ALU.mult, ALU.mult)
+
+        def turn_h(k):
+            words = h[k][:].bitcast(F32).rearrange("r (u s) -> r u s" if k == LAST else "r (s u) -> r u s", u=2)
             h_bank[k] = psum.tile([P, 2, P], F32, name="h_turn", tag=TURN_BANKS[k % 2])
             for u in range(2):
                 nc.tensor.transpose(h_bank[k][:, u, :], words[:, u, :], ident[:])
 
-        def regroup_first(k):
-            a, e = divmod(k, 2)
-            if a == 0:
-                h_words[e] = keep.tile([P, 2, P, 2], F32, name=f"h_words{e}", align_bytes=64)
-            nc.scalar.copy(h_words[e][:, :, a * HALF : (a + 1) * HALF, :].rearrange("s c i u -> s i c u"),
-                           h_bank[k][:].rearrange("s u (i c) -> s i c u", c=2))
+        def regroup(k, on=None, copy=nc.scalar.copy):
+            if k < PACK:
+                a, e = divmod(k, 2)
+                if a == 0:
+                    h_words[e] = tile(f"h_words{e}", [P, 2, P, 2], F32, on)
+                copy(h_words[e][:, :, a * HALF : (a + 1) * HALF, :].rearrange("s c i u -> s i c u"),
+                     h_bank[k][:].rearrange("s u (i c) -> s i c u", c=2))
+            else:
+                h_words[k] = tile(f"h_words{k}", [P, 1, P, 2], F32, on)
+                copy(h_words[k][:, 0], h_bank[k][:].rearrange("s u r -> s r u"))
 
-        def regroup_second(k):
-            h_words[k] = keep.tile([P, 1, P, 2], F32, name=f"h_words{k}", align_bytes=64)
-            nc.scalar.copy(h_words[k][:, 0], h_bank[k][:].rearrange("s u r -> s r u"))
-
-        def quantise_h(group, places):
-            codes = keep.tile([P, len(places) * P], U32, name=f"h_codes{group}", align_bytes=64)
-            scales = keep.tile([P, len(places) * P], U8, name=f"h_scales{group}", align_bytes=64)
+        def quantise_h(group, on=None):
+            places = ((0, group), (0, group + 2)) if group < 2 else ((1, group - PACK),)
+            codes = tile(f"h_codes{group}", [P, len(places) * P], U32, on)
+            scales = tile(f"h_scales{group}", [P, len(places) * P], U8)
             nc.vector.quantize_mx(codes[:].bitcast(E5M2), scales[:],
                                   h_words[group][:].rearrange("s i r u -> s (i r u)").bitcast(BF16))
             for i, place in enumerate(places):
                 h_ops[place] = codes[:, i * P : (i + 1) * P], scales[:, i * P : (i + 1) * P]
 
-        grad_rows = [keep.tile([P, PACK, D], F32, name=f"grad_rows{o}") for o in range(PASSES)]
+        grad_rows = [tile(f"grad_rows{o}", [P, PACK, D], F32) for o in range(PASSES)]
         out_rows = out_0[0].rearrange("(o p t) d -> o p t d", p=P, t=PACK)
-        out_scales = keep.tile([P, PASSES, D], U8, name="out_scales", align_bytes=64)
+        out_scales = tile("out_scales", [P, PASSES, D], U8)
+        woven, out_codes = {}, {}
 
-        def gradient(o, t, tag):
+        def gradient(o, t, bank=None):
             codes, scales = h_ops[o, t]
-            bank = psum.tile([P, 2, P, 2], F32, name="grad", tag=tag)
-            nc.tensor.matmul_mx(bank[:].rearrange("r u p e -> r (u p e)"), lhsT=codes.bitcast(E5M2), lhsT_scale=scales,
-                                rhs=wn_codes[:].bitcast(E4M3), rhs_scale=wn_scales[:], start=True, stop=True)
+            g_bank[o, t] = psum.tile([P, 2, P, 2], F32, name="grad", tag=bank or GRADIENT_BANKS[len(g_bank) % len(GRADIENT_BANKS)])
+            nc.tensor.matmul_mx(g_bank[o, t][:].rearrange("r u p e -> r (u p e)"), lhsT=codes.bitcast(E5M2), lhsT_scale=scales,
+                                rhs=wn["codes"][:].bitcast(E4M3), rhs_scale=wn_scales[:], start=True, stop=True)
+
+        def empty(o, t, cuts=(0, P), copy=nc.scalar.copy):
             rows = grad_rows[o][:, t, :].rearrange("r (p u e) -> r p u e", u=2, e=2)
-            cuts = (0, HALF, P) if (o, t) == (PASSES - 1, PACK - 1) else (0, P)
             for start, stop in zip(cuts, cuts[1:]):
-                nc.scalar.copy(rows[:, start:stop], bank[:, :, start:stop, :].rearrange("r u p e -> r p u e"))
+                copy(rows[:, start:stop], g_bank[o, t][:, :, start:stop, :].rearrange("r u p e -> r p u e"))
             nc.sync.dma_start(out_rows[o, :, t, :], grad_rows[o][:, t, :])
 
-        def weave(copy, woven, o, first, start, stop):
-            copy(woven[:, start - first : stop - first, :].rearrange("p (c i) t -> p c t i", i=4),
-                 grad_rows[o][:, :, start:stop].rearrange("p t (c i) -> p c t i", i=4))
+        def weave(copy, o, c, start=0, stop=D // 2, on=None):
+            if (o, c) not in woven:
+                woven[o, c] = tile(f"woven{o}{c}", [P, D // 2, PACK], BF16, on)
+            first = c * D // 2
+            copy(woven[o, c][:, start:stop, :].rearrange("p (c i) t -> p c t i", i=4),
+                 grad_rows[o][:, :, first + start : first + stop].rearrange("p t (c i) -> p c t i", i=4))
 
-        def planes(o):
-            codes = keep.tile([P, D], U32, name=f"out_codes{o}", align_bytes=64)
-            words_out = out_1[o].rearrange("p d l -> p (d l)").bitcast(I32)
-            half = D // 2
-            last = o == PASSES - 1
-            tags = ("woven0", "woven1") if last else (f"neg_ya{LAST}", f"h{LAST}")
-            woven = [keep.tile([P, half, PACK], BF16, name=f"woven{o}{c}", tag=tags[c], align_bytes=64) for c in range(2)]
-            weave(nc.vector.tensor_copy, woven[0], o, 0, 0, half)
-            if last:
-                weave(nc.scalar.copy, woven[1], o, half, D - SCALAR_WEAVES, D)
-            weave(nc.vector.tensor_copy, woven[1], o, half, half, D - SCALAR_WEAVES if last else D)
-            for c in range(2):
-                cols = slice(c * half, (c + 1) * half)
-                nc.vector.quantize_mx(codes[:, cols].bitcast(E4M3), out_scales[:, o, cols], woven[c][:].rearrange("p d t -> p (d t)"))
-                if last:
-                    nc.sync.dma_start(words_out[:, cols], codes[:, cols].bitcast(I32))
-            if not last:
-                nc.sync.dma_start(words_out, codes[:].bitcast(I32))
+        def quantise_out(o, c):
+            if o not in out_codes:
+                out_codes[o] = tile(f"out_codes{o}", [P, D], U32)
+            cols = slice(c * D // 2, (c + 1) * D // 2)
+            nc.vector.quantize_mx(out_codes[o][:, cols].bitcast(E4M3), out_scales[:, o, cols], woven[o, c][:].rearrange("p d t -> p (d t)"))
 
+        def store_words(o, start, stop):
+            nc.sync.dma_start(out_1[o].rearrange("p d l -> p (d l)").bitcast(I32)[:, start:stop], out_codes[o][:, start:stop].bitcast(I32))
+
+        on_vector, on_scalar = nc.vector.tensor_copy, nc.scalar.copy
         gather_w(0)
+        spread_ts()
         gather_w(1)
-        turn_w(0, "w_turned0")
+        turn_w(0)
+        copy_w(0)
         gather_w(2)
         gather_w(3)
-        nc.vector.quantize_mx(wd_codes[:].bitcast(E4M3), wd_scales[:], w_listed[:].rearrange("p n j -> p (n j)"))
-        x_half0 = keep.tile([P, 2, P, PACK], BF16, name="x_half0", tag="w_table3", align_bytes=64)
-        first_x(0, x_half0, (nc.scalar.copy, nc.vector.tensor_copy))
-        wn_codes = shared_tile("wn_codes", [P, D], U32)
-        quantise_turned(0)
-        first_x(1, shared_tile("x_half1", [P, 2, P, PACK], BF16), (nc.scalar.copy, nc.scalar.copy))
-
-        sign_first_pair()
+        round_tile(0,on_vector,"w_table2")
+        round_tile(1,on_scalar,"neg_ts_col")
+        quantise_w()
+        quantise_tile(0)
+        quantise_tile(1)
+        turn_w(1)
         score(0)
         score(1)
-        turn_w(1, "x_raw1")
-        for k in (2, 3):
-            sign(k, shared_tile(f"signed{k}", [P, N], F32))
-        for k in range(PACK):
-            weigh(k)
-            if k + 2 < PACK:
-                score(k + 2)
-            if k + 2 == PACK:
-                second_x()
-
-        sign(4, keep.tile([P, N], F32, name="signed4", tag="w_table3", align_bytes=64))
-        sign(5, shared_tile("signed5", [P, N], F32))
+        sign_pair(0,"w_table3")
+        copy_w(1)
+        quantise_turned(0,"x_raw0")
+        margin(0)
+        margin(1)
+        round_first(1,0,on_scalar,"neg_ts_col")
+        round_first(1,1,on_scalar)
+        clip(0)
+        clip(1)
+        sign_pair(1,"w_turned0")
+        quantise_x(1)
+        score(2)
+        score(3)
+        weigh(0)
+        turn_h(0)
+        weigh(1)
+        turn_h(1)
+        margin(2)
+        round_second(0,on_scalar,"neg_ya1")
+        round_second(1,on_scalar)
+        round_second(2,on_scalar)
+        clip(2,1)
+        round_second(3,on_vector)
         quantise_turned(1)
-        sign(6, shared_tile("signed6", [P, N], F32))
+        quantise_x(2)
         score(4)
-        for k in range(PACK):
-            regroup_first(k)
-        quantise_h(0, ((0, 0), (0, 2)))
-        sign(7, keep.tile([P, N], F32, name="signed7", tag="h_words0", align_bytes=64))
+        regroup(0)
+        regroup(1)
+        weigh(2)
+        turn_h(2)
         score(5)
+        regroup(2)
+        sign_pair_aside(3,2)
+        sign_pair(2,"neg_ya1")
+        margin(3,0)
         score(6)
-        quantise_h(1, ((0, 1), (0, 3)))
-
+        margin(4)
+        score(7)
+        margin(5)
+        clip(3)
+        clip(4)
+        clip(5)
+        quantise_h(0)
+        gradient(0,0,"bank5")
+        gradient(0,2,"bank6")
+        margin(6)
+        weigh(3)
+        turn_h(3)
+        margin(7)
         weigh(4)
-        score(LAST)
-        for k in range(PACK + 1, TILES):
-            weigh(k)
-        for t in range(PACK):
-            regroup_second(PACK + t)
-            quantise_h(PACK + t, ((1, t),))
-        places = [(0, 0), (0, 2), (0, 1), (0, 3)] + [(1, t) for t in range(PACK)]
-        for i, (o, t) in enumerate(places):
-            gradient(o, t, GRADIENT_BANKS[i % len(GRADIENT_BANKS)])
-        for o in range(PASSES):
-            planes(o)
+        turn_h(4)
+        clip(6)
+        empty(0,0)
+        regroup(3)
+        clip(7)
+        empty(0,2)
+        regroup(4)
+        weigh(5)
+        turn_h(5)
+        quantise_h(1)
+        gradient(0,1,"bank7")
+        gradient(0,3,"bank5")
+        weigh(6)
+        turn_h(6)
+        regroup(5)
+        empty(0,1)
+        weigh(7)
+        turn_h(7)
+        quantise_h(4)
+        gradient(1,0,"bank2")
+        regroup(6)
+        regroup(7)
+        quantise_h(5)
+        gradient(1,1,"bank0")
+        empty(0,3,(0,P),on_vector)
+        quantise_h(6)
+        gradient(1,2,"bank1")
+        quantise_h(7)
+        gradient(1,3,"bank6")
+        empty(1,0)
+        empty(1,1)
+        weave(on_vector,0,0)
+        weave(on_vector,0,1)
+        quantise_out(0,0)
+        quantise_out(0,1)
+        empty(1,2)
+        store_words(0,0,D)
+        empty(1,3,(0,HALF,P))
+        weave(on_vector,1,0)
+        weave(on_scalar,1,1,128,256)
+        weave(on_vector,1,1,0,128)
+        quantise_out(1,0)
+        store_words(1,0,256)
+        quantise_out(1,1)
+        store_words(1,256,512)
 
         for q in range(4):
             queue = nc.scalar if q % 2 == 0 else nc.sync

@@ -30,6 +30,7 @@ SCORE_BANKS = ("bank0", "bank1", "bank2")
 TURN_BANKS = ("bank3", "bank4")
 GRADIENT_BANKS = ("bank5", "bank6", "bank2")
 TS_BANK = "bank7"
+SORTED = 6
 
 
 def tile_attend_gsqh_pl_x_ts_kernel(tc, xT, wT, y, wt, ts, offs, out_0, out_1, out_2):
@@ -51,7 +52,7 @@ def tile_attend_gsqh_pl_x_ts_kernel(tc, xT, wT, y, wt, ts, offs, out_0, out_1, o
         make_identity(nc, ident[:])
 
         w_rows = wT.rearrange("(p j) c -> j p c", j=PACK)
-        w_table = [tile(f"w_table{j}", [P, T], F32) for j in range(PACK)]
+        w_table = [tile(f"w_table{j}", [P, T], F32, 12 if j == PACK - 1 else None) for j in range(PACK)]
         x_rows = xT[0].rearrange("(p j) r -> p j r", j=PACK)
         y_first = y[0, :PASS].rearrange("(a m e) n -> a m e n", m=P, e=2)
         y_second = y[0, PASS:].rearrange("(p c e) n -> c p e n", c=2, e=2)
@@ -80,8 +81,8 @@ def tile_attend_gsqh_pl_x_ts_kernel(tc, xT, wT, y, wt, ts, offs, out_0, out_1, o
         load_y(1)
         load_x(2)
         load_x(3)
-        load_y(2)
         load_y(3)
+        load_y(2)
 
         neg_ts_bank = psum.tile([P, 1, N], F32, name="neg_ts_bank", tag=TS_BANK)
         neg_ts = tile("neg_ts", [P, 1, N], F32)
@@ -118,6 +119,13 @@ def tile_attend_gsqh_pl_x_ts_kernel(tc, xT, wT, y, wt, ts, offs, out_0, out_1, o
             w_bank[u] = psum.tile([P, PACK * P], F32, name=f"w_turn{u}", tag=bank or GRADIENT_BANKS[1 - u])
             for t in range(PACK):
                 nc.tensor.transpose(w_bank[u][:, t * P : (t + 1) * P], w_words[:, u, t, :], ident[:])
+
+        def deal_and_turn_w(u, on):
+            dealt = tile(f"w_dealt{u}", [P, PACK, P], F32, on)
+            nc.scalar.copy(dealt[:].rearrange("p t s -> p s t"), w_words[:, u].rearrange("p t s -> p s t"))
+            w_bank[u] = psum.tile([P, PACK * P], F32, name=f"w_turn{u}", tag=GRADIENT_BANKS[1 - u])
+            for t in range(PACK):
+                nc.tensor.transpose(w_bank[u][:, t * P : (t + 1) * P], dealt[:, t, :], ident[:])
 
         def copy_w(u, on=None):
             w_turned[u] = tile(f"w_turned{u}", [P, P, 2, PACK], BF16, on)
@@ -164,6 +172,12 @@ def tile_attend_gsqh_pl_x_ts_kernel(tc, xT, wT, y, wt, ts, offs, out_0, out_1, o
             for i in range(count):
                 x_ops[first + i] = codes[:, i * P : (i + 1) * P], scales[:, i * P : (i + 1) * P]
 
+        def by_words(slots):
+            return slots.rearrange("r (s u e) -> r u s e", u=2, e=2)
+
+        def as_laid(slots):
+            return slots.rearrange("r (u s e) -> r u s e", u=2, e=2)
+
         def sign_pair(i, on=None):
             pair = tile(f"signed_pair{i}", [P, 2, N], F32, on)
             nc.vector.tensor_tensor(pair[:], y_pair[i][:], neg_ts_bank[:].to_broadcast([P, 2, N]), ALU.mult)
@@ -178,7 +192,7 @@ def tile_attend_gsqh_pl_x_ts_kernel(tc, xT, wT, y, wt, ts, offs, out_0, out_1, o
 
         def sign(k, on=None):
             signed[k] = tile(f"signed{k}", [P, N], F32, on)[:]
-            nc.vector.tensor_tensor(signed[k], y_pair[k // 2][:, k % 2, :], neg_ts_bank[:, 0, :], ALU.mult)
+            nc.vector.tensor_tensor(as_laid(signed[k]), by_words(y_pair[k // 2][:, k % 2, :]), by_words(neg_ts_bank[:, 0, :]), ALU.mult)
 
         def sign_aside(k, on=None):
             signed[k] = tile(f"signed{k}", [P, N], F32, on)[:]
@@ -192,7 +206,10 @@ def tile_attend_gsqh_pl_x_ts_kernel(tc, xT, wT, y, wt, ts, offs, out_0, out_1, o
 
         def margin(k, on=None):
             neg_ya[k] = tile(f"neg_ya{k}", [P, N], F32, on)
-            nc.vector.tensor_tensor(neg_ya[k][:], scores[k][:], signed[k], ALU.mult)
+            if k < SORTED:
+                nc.vector.tensor_tensor(as_laid(neg_ya[k][:]), by_words(scores[k][:]), as_laid(signed[k]), ALU.mult)
+            else:
+                nc.vector.tensor_tensor(neg_ya[k][:], scores[k][:], signed[k], ALU.mult)
 
         def clip(k, on=None):
             hinge[k] = tile(f"hinge{k}", [P, N], F32, on)
@@ -210,7 +227,7 @@ def tile_attend_gsqh_pl_x_ts_kernel(tc, xT, wT, y, wt, ts, offs, out_0, out_1, o
                 nc.vector.scalar_tensor_tensor(h[k][:], hinge[k][:], factor, signed[k], ALU.mult, ALU.mult)
 
         def turn_h(k):
-            words = h[k][:].bitcast(F32).rearrange("r (u s) -> r u s" if k == LAST else "r (s u) -> r u s", u=2)
+            words = h[k][:].bitcast(F32).rearrange("r (u s) -> r u s" if k == LAST or k < SORTED else "r (s u) -> r u s", u=2)
             h_bank[k] = psum.tile([P, 2, P], F32, name="h_turn", tag=TURN_BANKS[k % 2])
             for u in range(2):
                 nc.tensor.transpose(h_bank[k][:, u, :], words[:, u, :], ident[:])
@@ -268,12 +285,15 @@ def tile_attend_gsqh_pl_x_ts_kernel(tc, xT, wT, y, wt, ts, offs, out_0, out_1, o
         def store_words(o, start, stop):
             nc.sync.dma_start(out_1[o].rearrange("p d l -> p (d l)").bitcast(I32)[:, start:stop], out_codes[o][:, start:stop].bitcast(I32))
 
+        def on_gpsimd(out, in_):
+            nc.gpsimd.tensor_scalar(out, in_, 1.0, 0.0, ALU.mult, ALU.add)
+
         on_vector, on_scalar = nc.vector.tensor_copy, nc.scalar.copy
         gather_w(0)
         spread_ts()
         gather_w(1)
         turn_w(0)
-        copy_w(0)
+        copy_w(0,21)
         gather_w(2)
         gather_w(3)
         round_tile(0,on_vector,"w_table2")
@@ -281,19 +301,20 @@ def tile_attend_gsqh_pl_x_ts_kernel(tc, xT, wT, y, wt, ts, offs, out_0, out_1, o
         quantise_w()
         quantise_tile(0)
         quantise_tile(1)
-        turn_w(1)
         score(0)
         score(1)
-        sign_pair(0,"w_table3")
-        copy_w(1)
+        sign(0,12)
+        sign(1,14)
+        deal_and_turn_w(1,"w_table2")
         quantise_turned(0,"x_raw0")
         margin(0)
-        margin(1)
+        margin(1,8)
         round_first(1,0,on_scalar,"neg_ts_col")
         round_first(1,1,on_scalar)
         clip(0)
         clip(1)
-        sign_pair(1,"w_turned0")
+        sign(2,20)
+        sign(3,22)
         quantise_x(1)
         score(2)
         score(3)
@@ -302,70 +323,72 @@ def tile_attend_gsqh_pl_x_ts_kernel(tc, xT, wT, y, wt, ts, offs, out_0, out_1, o
         weigh(1)
         turn_h(1)
         margin(2)
-        round_second(0,on_scalar,"neg_ya1")
+        copy_w(1,"neg_ya0")
+        round_second(0,on_scalar,5)
         round_second(1,on_scalar)
         round_second(2,on_scalar)
-        clip(2,1)
+        clip(2)
         round_second(3,on_vector)
+        margin(3)
         quantise_turned(1)
         quantise_x(2)
         score(4)
+        clip(3,1)
         regroup(0)
         regroup(1)
         weigh(2)
         turn_h(2)
+        weigh(3)
+        turn_h(3)
         score(5)
-        regroup(2)
-        sign_pair_aside(3,2)
-        sign_pair(2,"neg_ya1")
-        margin(3,0)
         score(6)
+        regroup(2)
+        regroup(3)
+        sign(4,20)
+        sign_pair_aside(3,2,64)
+        sign(5,22)
         margin(4)
         score(7)
         margin(5)
-        clip(3)
         clip(4)
         clip(5)
         quantise_h(0)
         gradient(0,0,"bank5")
         gradient(0,2,"bank6")
-        margin(6)
-        weigh(3)
-        turn_h(3)
-        margin(7)
-        weigh(4)
-        turn_h(4)
-        clip(6)
-        empty(0,0)
-        regroup(3)
-        clip(7)
-        empty(0,2)
-        regroup(4)
-        weigh(5)
-        turn_h(5)
         quantise_h(1)
         gradient(0,1,"bank7")
+        margin(6)
+        weigh(4)
+        turn_h(4)
+        margin(7)
+        weigh(5)
+        turn_h(5)
+        empty(0,0)
         gradient(0,3,"bank5")
-        weigh(6)
-        turn_h(6)
+        clip(6)
+        empty(0,2)
+        clip(7)
+        regroup(4)
         regroup(5)
         empty(0,1)
+        weigh(6)
+        turn_h(6)
         weigh(7)
-        turn_h(7)
         quantise_h(4)
+        turn_h(7)
         gradient(1,0,"bank2")
-        regroup(6)
-        regroup(7)
         quantise_h(5)
         gradient(1,1,"bank0")
         empty(0,3,(0,P),on_vector)
+        regroup(6)
+        regroup(7)
         quantise_h(6)
         gradient(1,2,"bank1")
+        weave(on_vector,0,0)
         quantise_h(7)
         gradient(1,3,"bank6")
         empty(1,0)
         empty(1,1)
-        weave(on_vector,0,0)
         weave(on_vector,0,1)
         quantise_out(0,0)
         quantise_out(0,1)

@@ -30,7 +30,7 @@ SCORE_BANKS = ("bank0", "bank1", "bank2")
 TURN_BANKS = ("bank3", "bank4")
 GRADIENT_BANKS = ("bank5", "bank6", "bank2")
 TS_BANK = "bank7"
-SORTED = 6
+SORTED = (4, 5)
 
 
 def tile_attend_gsqh_pl_x_ts_kernel(tc, xT, wT, y, wt, ts, offs, out_0, out_1, out_2):
@@ -127,9 +127,10 @@ def tile_attend_gsqh_pl_x_ts_kernel(tc, xT, wT, y, wt, ts, offs, out_0, out_1, o
             for t in range(PACK):
                 nc.tensor.transpose(w_bank[u][:, t * P : (t + 1) * P], dealt[:, t, :], ident[:])
 
-        def copy_w(u, on=None):
-            w_turned[u] = tile(f"w_turned{u}", [P, P, 2, PACK], BF16, on)
-            nc.scalar.copy(w_turned[u][:], w_bank[u][:].bitcast(BF16).rearrange("s (t p e) -> s p e t", t=PACK, e=2))
+        def copy_w(u, on=None, start=0, stop=P):
+            if u not in w_turned:
+                w_turned[u] = tile(f"w_turned{u}", [P, P, 2, PACK], BF16, on)
+            nc.scalar.copy(w_turned[u][:, start:stop], w_bank[u][:].bitcast(BF16).rearrange("s (t p e) -> s p e t", t=PACK, e=2)[:, start:stop])
 
         def quantise_turned(u, on=None):
             if u == 0:
@@ -158,11 +159,18 @@ def tile_attend_gsqh_pl_x_ts_kernel(tc, xT, wT, y, wt, ts, offs, out_0, out_1, o
             nc.vector.quantize_mx(codes[:].bitcast(E4M3), scales[:], x_round["tile", k][:].rearrange("p m j -> p (m j)"))
             x_ops[k] = codes[:], scales[:]
 
+        def round_half(a, copy, on=None):
+            x_round[a] = tile(f"x_half{a}", [P, 2, P, PACK], BF16, on)
+            copy(x_round[a][:].rearrange("p e m j -> p m j e"), x_raw[a][:].rearrange("p j (m e) -> p m j e", e=2))
+
         def round_second(i, copy, on=None):
             if 2 not in x_round:
                 x_round[2] = tile("x_second", [P, PACK, P, PACK], BF16, on)
             copy(x_round[2][:, :, i * P // PACK : (i + 1) * P // PACK, :].rearrange("p t m j -> p m j t"),
                  x_raw[2 + i // 2][:, :, i % 2 * P : (i % 2 + 1) * P].rearrange("p j (m t) -> p m j t", t=PACK))
+
+        def round_last(copy):
+            copy(x_round[2][:, :, HALF:, :].rearrange("p t m j -> p m j t"), x_raw[3][:].rearrange("p j (m t) -> p m j t", t=PACK))
 
         def quantise_x(a, on=None):
             first, count = 2 * a, 2 if a < 2 else PACK
@@ -192,11 +200,16 @@ def tile_attend_gsqh_pl_x_ts_kernel(tc, xT, wT, y, wt, ts, offs, out_0, out_1, o
 
         def sign(k, on=None):
             signed[k] = tile(f"signed{k}", [P, N], F32, on)[:]
-            nc.vector.tensor_tensor(as_laid(signed[k]), by_words(y_pair[k // 2][:, k % 2, :]), by_words(neg_ts_bank[:, 0, :]), ALU.mult)
+            if k in SORTED:
+                nc.vector.tensor_tensor(as_laid(signed[k]), by_words(y_pair[k // 2][:, k % 2, :]), by_words(neg_ts_bank[:, 0, :]), ALU.mult)
+            else:
+                nc.vector.tensor_tensor(signed[k], y_pair[k // 2][:, k % 2, :], neg_ts_bank[:, 0, :], ALU.mult)
 
-        def sign_aside(k, on=None):
+        def sign_aside(k, on=None, cut=0):
             signed[k] = tile(f"signed{k}", [P, N], F32, on)[:]
-            nc.gpsimd.tensor_tensor(signed[k], y_pair[k // 2][:, k % 2, :], neg_ts[:, 0, :], ALU.mult)
+            nc.gpsimd.tensor_tensor(signed[k][:, cut:], y_pair[k // 2][:, k % 2, cut:], neg_ts[:, 0, cut:], ALU.mult)
+            if cut:
+                nc.vector.tensor_tensor(signed[k][:, :cut], y_pair[k // 2][:, k % 2, :cut], neg_ts_bank[:, 0, :cut], ALU.mult)
 
         def score(k):
             codes, scales = x_ops[k]
@@ -204,9 +217,16 @@ def tile_attend_gsqh_pl_x_ts_kernel(tc, xT, wT, y, wt, ts, offs, out_0, out_1, o
             nc.tensor.matmul_mx(scores[k][:], lhsT=codes.bitcast(E4M3), lhsT_scale=scales,
                                 rhs=wd_codes[:].bitcast(E4M3), rhs_scale=wd_scales[:], start=True, stop=True)
 
+        def keep_warm(k, passes=2):
+            codes, scales = x_ops[k]
+            bank = psum.tile([P, N], F32, name="unread", tag=SCORE_BANKS[k % 3])
+            for i in range(passes):
+                nc.tensor.matmul_mx(bank[:], lhsT=codes.bitcast(E4M3), lhsT_scale=scales,
+                                    rhs=wd_codes[:].bitcast(E4M3), rhs_scale=wd_scales[:], start=True, stop=True)
+
         def margin(k, on=None):
             neg_ya[k] = tile(f"neg_ya{k}", [P, N], F32, on)
-            if k < SORTED:
+            if k in SORTED:
                 nc.vector.tensor_tensor(as_laid(neg_ya[k][:]), by_words(scores[k][:]), as_laid(signed[k]), ALU.mult)
             else:
                 nc.vector.tensor_tensor(neg_ya[k][:], scores[k][:], signed[k], ALU.mult)
@@ -226,9 +246,9 @@ def tile_attend_gsqh_pl_x_ts_kernel(tc, xT, wT, y, wt, ts, offs, out_0, out_1, o
             else:
                 nc.vector.scalar_tensor_tensor(h[k][:], hinge[k][:], factor, signed[k], ALU.mult, ALU.mult)
 
-        def turn_h(k):
-            words = h[k][:].bitcast(F32).rearrange("r (u s) -> r u s" if k == LAST or k < SORTED else "r (s u) -> r u s", u=2)
-            h_bank[k] = psum.tile([P, 2, P], F32, name="h_turn", tag=TURN_BANKS[k % 2])
+        def turn_h(k, bank=None):
+            words = h[k][:].bitcast(F32).rearrange("r (u s) -> r u s" if k == LAST or k in SORTED else "r (s u) -> r u s", u=2)
+            h_bank[k] = psum.tile([P, 2, P], F32, name="h_turn", tag=bank or TURN_BANKS[k % 2])
             for u in range(2):
                 nc.tensor.transpose(h_bank[k][:, u, :], words[:, u, :], ident[:])
 
@@ -293,28 +313,28 @@ def tile_attend_gsqh_pl_x_ts_kernel(tc, xT, wT, y, wt, ts, offs, out_0, out_1, o
         spread_ts()
         gather_w(1)
         turn_w(0)
-        copy_w(0,21)
+        copy_w(0)
         gather_w(2)
         gather_w(3)
-        round_tile(0,on_vector,"w_table2")
-        round_tile(1,on_scalar,"neg_ts_col")
+        round_half(0,on_vector,"w_table2")
         quantise_w()
-        quantise_tile(0)
-        quantise_tile(1)
+        quantise_x(0)
+        quantise_turned(0,"x_raw0")
+        deal_and_turn_w(1,None)
         score(0)
         score(1)
         sign(0,12)
-        sign(1,14)
-        deal_and_turn_w(1,"w_table2")
-        quantise_turned(0,"x_raw0")
+        sign_aside(1,"w_turned0",128)
+        copy_w(1,None,0,HALF)
         margin(0)
         margin(1,8)
-        round_first(1,0,on_scalar,"neg_ts_col")
+        round_first(1,0,on_scalar,"w_dealt1")
         round_first(1,1,on_scalar)
         clip(0)
         clip(1)
-        sign(2,20)
-        sign(3,22)
+        copy_w(1,None,HALF,P)
+        sign(2,"x_codes0")
+        sign_aside(3)
         quantise_x(1)
         score(2)
         score(3)
@@ -323,7 +343,6 @@ def tile_attend_gsqh_pl_x_ts_kernel(tc, xT, wT, y, wt, ts, offs, out_0, out_1, o
         weigh(1)
         turn_h(1)
         margin(2)
-        copy_w(1,"neg_ya0")
         round_second(0,on_scalar,5)
         round_second(1,on_scalar)
         round_second(2,on_scalar)
@@ -344,9 +363,9 @@ def tile_attend_gsqh_pl_x_ts_kernel(tc, xT, wT, y, wt, ts, offs, out_0, out_1, o
         score(6)
         regroup(2)
         regroup(3)
-        sign(4,20)
+        sign(4,"hinge2")
         sign_pair_aside(3,2,64)
-        sign(5,22)
+        sign(5,"signed3")
         margin(4)
         score(7)
         margin(5)
@@ -360,9 +379,11 @@ def tile_attend_gsqh_pl_x_ts_kernel(tc, xT, wT, y, wt, ts, offs, out_0, out_1, o
         margin(6)
         weigh(4)
         turn_h(4)
+        keep_warm(6)
         margin(7)
         weigh(5)
         turn_h(5)
+        keep_warm(7)
         empty(0,0)
         gradient(0,3,"bank5")
         clip(6)
@@ -379,7 +400,7 @@ def tile_attend_gsqh_pl_x_ts_kernel(tc, xT, wT, y, wt, ts, offs, out_0, out_1, o
         gradient(1,0,"bank2")
         quantise_h(5)
         gradient(1,1,"bank0")
-        empty(0,3,(0,P),on_vector)
+        empty(0,3)
         regroup(6)
         regroup(7)
         quantise_h(6)

@@ -85,7 +85,7 @@ def tile_attend_gsqh_pl_x_ts_kernel(tc, xT, wT, y, wt, ts, offs, out_0, out_1, o
         load_y(2)
 
         neg_ts_bank = psum.tile([P, 1, N], F32, name="neg_ts_bank", tag=TS_BANK)
-        neg_ts = tile("neg_ts", [P, 1, N], F32)
+        neg_ts = tile("neg_ts", [P, 2, N], F32)
 
         def spread_ts():
             ts_listed = tile("ts_listed", [P, N], F32)
@@ -97,7 +97,7 @@ def tile_attend_gsqh_pl_x_ts_kernel(tc, xT, wT, y, wt, ts, offs, out_0, out_1, o
             nc.scalar.activation(neg_ts_col[:], ts_turn[:, :, 0], ACT.Copy, scale=-1.0)
             for c in range(PACK):
                 nc.tensor.transpose(neg_ts_bank[:, 0, c * P : (c + 1) * P], neg_ts_col[:, c : c + 1].to_broadcast([P, P]), ident[:])
-            nc.scalar.copy(neg_ts[:], neg_ts_bank[:])
+            nc.scalar.copy(neg_ts[:], neg_ts_bank[:].to_broadcast([P, 2, N]))
 
         def weight(first, second, k):
             return first[:, k // 2, k % 2 : k % 2 + 1] if k < PACK else second[:, k - PACK : k - PACK + 1]
@@ -193,9 +193,9 @@ def tile_attend_gsqh_pl_x_ts_kernel(tc, xT, wT, y, wt, ts, offs, out_0, out_1, o
 
         def sign_pair_aside(i, on=None, cut=0):
             pair = tile(f"signed_pair{i}", [P, 2, N], F32, on)
-            nc.gpsimd.tensor_tensor(pair[:, :, cut:], y_pair[i][:, :, cut:], neg_ts[:, :, cut:].to_broadcast([P, 2, N - cut]), ALU.mult)
-            if cut:
-                nc.vector.tensor_tensor(pair[:, :, :cut], y_pair[i][:, :, :cut], neg_ts_bank[:, :, :cut].to_broadcast([P, 2, cut]), ALU.mult)
+            flat = [part[:].rearrange("r k n -> r (k n)")[:, cut:] for part in (pair, y_pair[i], neg_ts)]
+            nc.gpsimd.tensor_tensor(*flat, ALU.mult)
+            nc.vector.tensor_tensor(pair[:, 0, :cut], y_pair[i][:, 0, :cut], neg_ts_bank[:, 0, :cut], ALU.mult)
             signed[2 * i], signed[2 * i + 1] = pair[:, 0, :], pair[:, 1, :]
 
         def sign(k, on=None):
@@ -364,7 +364,7 @@ def tile_attend_gsqh_pl_x_ts_kernel(tc, xT, wT, y, wt, ts, offs, out_0, out_1, o
         regroup(2)
         regroup(3)
         sign(4,"hinge2")
-        sign_pair_aside(3,2,64)
+        sign_pair_aside(3,2,128)
         sign(5,"signed3")
         margin(4)
         score(7)

@@ -28,21 +28,30 @@ PAIRS = TILES // 2
 
 SCORE_BANKS = ("bank0", "bank1", "bank2")
 TURN_BANKS = ("bank3", "bank4")
-GRADIENT_BANKS = ("bank5", "bank6", "bank2")
+COLUMN_BANKS = ("bank6", "bank5")
 TS_BANK = "bank7"
+
 SORTED = (4, 5)
+
+KIB = 1024
+SHARED = {"w_table3": 12, "signed0": 12, "margin1": 8, "x_second": 5, "hinge3": 1, "signed_last": 2,
+          "margin0": 26, "x_codes2": 26, "w_turned1": 27}
+
+VECTOR_SHARE = N // 4
+SCALAR_WEAVES = D // 4
 
 
 def tile_attend_gsqh_pl_x_ts_kernel(tc, xT, wT, y, wt, ts, offs, out_0, out_1, out_2):
     nc = tc.nc
+    on_vector, on_scalar = nc.vector.tensor_copy, nc.scalar.copy
     with ExitStack() as ctx:
         keep = ctx.enter_context(tc.tile_pool(name="keep", bufs=1))
         shared = ctx.enter_context(tc.tile_pool(name="shared", bufs=1))
         psum = ctx.enter_context(tc.psum_pool(name="psum", bufs=1))
 
         def tile(name, shape, dtype, on=None):
-            if isinstance(on, int):
-                return shared.tile(shape, dtype, name=name, offset=on * 1024, align_bytes=64)
+            if name in SHARED:
+                return shared.tile(shape, dtype, name=name, offset=SHARED[name] * KIB, align_bytes=64)
             return keep.tile(shape, dtype, name=name, tag=on or name, align_bytes=64)
 
         offsets = keep.tile([P, N // 16], U16, name="offsets")
@@ -52,7 +61,7 @@ def tile_attend_gsqh_pl_x_ts_kernel(tc, xT, wT, y, wt, ts, offs, out_0, out_1, o
         make_identity(nc, ident[:])
 
         w_rows = wT.rearrange("(p j) c -> j p c", j=PACK)
-        w_table = [tile(f"w_table{j}", [P, T], F32, 12 if j == PACK - 1 else None) for j in range(PACK)]
+        w_table = [tile(f"w_table{j}", [P, T], F32) for j in range(PACK)]
         x_rows = xT[0].rearrange("(p j) r -> p j r", j=PACK)
         y_first = y[0, :PASS].rearrange("(a m e) n -> a m e n", m=P, e=2)
         y_second = y[0, PASS:].rearrange("(p c e) n -> c p e n", c=2, e=2)
@@ -68,21 +77,13 @@ def tile_attend_gsqh_pl_x_ts_kernel(tc, xT, wT, y, wt, ts, offs, out_0, out_1, o
             if j == 0:
                 nc.sync.dma_start(offsets[:], offs)
                 nc.sync.dma_start(ts_row[0:1, :], ts[0:1, :])
-
-        def load_x(i):
+        for i in range(2):
             nc.sync.dma_start(x_raw[i][:], x_rows[:, :, i * 2 * P : (i + 1) * 2 * P])
-
-        def load_y(i):
-            nc.sync.dma_start(y_pair[i][:], (y_first, y_second)[i // 2][i % 2])
-
-        load_x(0)
-        load_y(0)
-        load_x(1)
-        load_y(1)
-        load_x(2)
-        load_x(3)
-        load_y(3)
-        load_y(2)
+            nc.sync.dma_start(y_pair[i][:], y_first[i])
+        for i in range(2, PAIRS):
+            nc.sync.dma_start(x_raw[i][:], x_rows[:, :, i * 2 * P : (i + 1) * 2 * P])
+        for i in range(2):
+            nc.sync.dma_start(y_pair[2 + i][:], y_second[i])
 
         neg_ts_bank = psum.tile([P, 1, N], F32, name="neg_ts_bank", tag=TS_BANK)
         neg_ts = tile("neg_ts", [P, 2, N], F32)
@@ -99,173 +100,120 @@ def tile_attend_gsqh_pl_x_ts_kernel(tc, xT, wT, y, wt, ts, offs, out_0, out_1, o
                 nc.tensor.transpose(neg_ts_bank[:, 0, c * P : (c + 1) * P], neg_ts_col[:, c : c + 1].to_broadcast([P, P]), ident[:])
             nc.scalar.copy(neg_ts[:], neg_ts_bank[:].to_broadcast([P, 2, N]))
 
-        def weight(first, second, k):
-            return first[:, k // 2, k % 2 : k % 2 + 1] if k < PACK else second[:, k - PACK : k - PACK + 1]
-
         w_listed = tile("w_listed", [P, N, PACK], BF16)
         w_words = w_listed[:].rearrange("p n j -> p (n j)").bitcast(F32).rearrange("p (s t u) -> p u t s", t=PACK, u=2)
         wd_codes = tile("wd_codes", [P, N], U32)
         wd_scales = tile("wd_scales", [P, N], U8)
         wn_scales = tile("wn_scales", [P, D], U8)
-        w_bank, w_turned, wn = {}, {}, {}
+        w_bank, w_turned = {}, {}
 
         def gather_w(j):
             nc.vector.tensor_copy(w_listed[:, :, j], w_table[j][:].indirect(offsets[:]))
 
-        def quantise_w():
-            nc.vector.quantize_mx(wd_codes[:].bitcast(E4M3), wd_scales[:], w_listed[:].rearrange("p n j -> p (n j)"))
-
-        def turn_w(u, bank=None):
-            w_bank[u] = psum.tile([P, PACK * P], F32, name=f"w_turn{u}", tag=bank or GRADIENT_BANKS[1 - u])
+        def turn_w(u, words):
+            w_bank[u] = psum.tile([P, PACK * P], F32, name=f"w_turn{u}", tag=COLUMN_BANKS[u])
             for t in range(PACK):
-                nc.tensor.transpose(w_bank[u][:, t * P : (t + 1) * P], w_words[:, u, t, :], ident[:])
+                nc.tensor.transpose(w_bank[u][:, t * P : (t + 1) * P], words[:, t, :], ident[:])
 
-        def deal_and_turn_w(u, on):
-            dealt = tile(f"w_dealt{u}", [P, PACK, P], F32, on)
-            nc.scalar.copy(dealt[:].rearrange("p t s -> p s t"), w_words[:, u].rearrange("p t s -> p s t"))
-            w_bank[u] = psum.tile([P, PACK * P], F32, name=f"w_turn{u}", tag=GRADIENT_BANKS[1 - u])
-            for t in range(PACK):
-                nc.tensor.transpose(w_bank[u][:, t * P : (t + 1) * P], dealt[:, t, :], ident[:])
+        def copy_w(u):
+            w_turned[u] = tile(f"w_turned{u}", [P, P, 2, PACK], BF16)
+            nc.scalar.copy(w_turned[u][:], w_bank[u][:].bitcast(BF16).rearrange("s (t p e) -> s p e t", t=PACK, e=2))
 
-        def copy_w(u, on=None, start=0, stop=P):
-            if u not in w_turned:
-                w_turned[u] = tile(f"w_turned{u}", [P, P, 2, PACK], BF16, on)
-            nc.scalar.copy(w_turned[u][:, start:stop], w_bank[u][:].bitcast(BF16).rearrange("s (t p e) -> s p e t", t=PACK, e=2)[:, start:stop])
-
-        def quantise_turned(u, on=None):
-            if u == 0:
-                wn["codes"] = tile("wn_codes", [P, D], U32, on)
+        def quantise_turned(u):
             cols = slice(u * D // 2, (u + 1) * D // 2)
-            nc.vector.quantize_mx(wn["codes"][:, cols].bitcast(E4M3), wn_scales[:, cols],
+            nc.vector.quantize_mx(wn_codes[:, cols].bitcast(E4M3), wn_scales[:, cols],
                                   w_turned[u][:].rearrange("s p e t -> s (p e t)"))
 
-        x_round, x_ops, signed, scores, neg_ya, hinge, h, h_bank, h_words, h_ops, g_bank = ({} for i in range(11))
+        x_ops, signed, scores, margin, hinge, h, h_bank, h_words, h_ops, g_bank = ({} for i in range(10))
 
-        def round_first(a, i, copy, on=None):
-            if a not in x_round:
-                x_round[a] = tile(f"x_half{a}", [P, 2, P, PACK], BF16, on)
-            copy(x_round[a][:, :, i * HALF : (i + 1) * HALF, :].rearrange("p e m j -> p m j e"),
-                 x_raw[a][:, :, i * P : (i + 1) * P].rearrange("p j (m e) -> p m j e", e=2))
+        def round_x(copy, rounded, raw, start, stop, first):
+            count = rounded.shape[1]
+            copy(rounded[:, :, first : first + (stop - start) // count, :].rearrange("p e m j -> p m j e"),
+                 raw[:, :, start:stop].rearrange("p j (m e) -> p m j e", e=count))
 
-        def round_tile(k, copy, on=None):
-            rounded = tile(f"x_tile{k}", [P, P, PACK], BF16, on)
-            copy(rounded[:].rearrange("p (c i) j -> p c j i", i=2),
-                 x_raw[k // 2][:].rearrange("p j (c i e) -> p e c j i", i=2, e=2)[:, k % 2])
-            x_round["tile", k] = rounded
-
-        def quantise_tile(k):
-            codes = tile(f"x_codes{k}", [P, P], U32)
-            scales = tile(f"x_scales{k}", [P, P], U8)
-            nc.vector.quantize_mx(codes[:].bitcast(E4M3), scales[:], x_round["tile", k][:].rearrange("p m j -> p (m j)"))
-            x_ops[k] = codes[:], scales[:]
-
-        def round_half(a, copy, on=None):
-            x_round[a] = tile(f"x_half{a}", [P, 2, P, PACK], BF16, on)
-            copy(x_round[a][:].rearrange("p e m j -> p m j e"), x_raw[a][:].rearrange("p j (m e) -> p m j e", e=2))
-
-        def round_second(i, copy, on=None):
-            if 2 not in x_round:
-                x_round[2] = tile("x_second", [P, PACK, P, PACK], BF16, on)
-            copy(x_round[2][:, :, i * P // PACK : (i + 1) * P // PACK, :].rearrange("p t m j -> p m j t"),
-                 x_raw[2 + i // 2][:, :, i % 2 * P : (i % 2 + 1) * P].rearrange("p j (m t) -> p m j t", t=PACK))
-
-        def round_last(copy):
-            copy(x_round[2][:, :, HALF:, :].rearrange("p t m j -> p m j t"), x_raw[3][:].rearrange("p j (m t) -> p m j t", t=PACK))
-
-        def quantise_x(a, on=None):
-            first, count = 2 * a, 2 if a < 2 else PACK
-            codes = tile(f"x_codes{first}", [P, count * P], U32, on)
+        def quantise_x(first, rounded):
+            count = rounded.shape[1]
+            codes = tile(f"x_codes{first}", [P, count * P], U32)
             scales = tile(f"x_scales{first}", [P, count * P], U8)
-            nc.vector.quantize_mx(codes[:].bitcast(E4M3), scales[:], x_round[a][:].rearrange("p e m j -> p (e m j)"))
+            nc.vector.quantize_mx(codes[:].bitcast(E4M3), scales[:], rounded[:].rearrange("p e m j -> p (e m j)"))
             for i in range(count):
                 x_ops[first + i] = codes[:, i * P : (i + 1) * P], scales[:, i * P : (i + 1) * P]
 
         def by_words(slots):
             return slots.rearrange("r (s u e) -> r u s e", u=2, e=2)
 
-        def as_laid(slots):
+        def as_sorted(slots):
             return slots.rearrange("r (u s e) -> r u s e", u=2, e=2)
-
-        def sign_pair(i, on=None):
-            pair = tile(f"signed_pair{i}", [P, 2, N], F32, on)
-            nc.vector.tensor_tensor(pair[:], y_pair[i][:], neg_ts_bank[:].to_broadcast([P, 2, N]), ALU.mult)
-            signed[2 * i], signed[2 * i + 1] = pair[:, 0, :], pair[:, 1, :]
-
-        def sign_pair_aside(i, on=None, cut=0):
-            pair = tile(f"signed_pair{i}", [P, 2, N], F32, on)
-            flat = [part[:].rearrange("r k n -> r (k n)")[:, cut:] for part in (pair, y_pair[i], neg_ts)]
-            nc.gpsimd.tensor_tensor(*flat, ALU.mult)
-            nc.vector.tensor_tensor(pair[:, 0, :cut], y_pair[i][:, 0, :cut], neg_ts_bank[:, 0, :cut], ALU.mult)
-            signed[2 * i], signed[2 * i + 1] = pair[:, 0, :], pair[:, 1, :]
 
         def sign(k, on=None):
             signed[k] = tile(f"signed{k}", [P, N], F32, on)[:]
+            labels, scale = y_pair[k // 2][:, k % 2, :], neg_ts_bank[:, 0, :]
             if k in SORTED:
-                nc.vector.tensor_tensor(as_laid(signed[k]), by_words(y_pair[k // 2][:, k % 2, :]), by_words(neg_ts_bank[:, 0, :]), ALU.mult)
+                nc.vector.tensor_tensor(as_sorted(signed[k]), by_words(labels), by_words(scale), ALU.mult)
             else:
-                nc.vector.tensor_tensor(signed[k], y_pair[k // 2][:, k % 2, :], neg_ts_bank[:, 0, :], ALU.mult)
+                nc.vector.tensor_tensor(signed[k], labels, scale, ALU.mult)
 
-        def sign_aside(k, on=None, cut=0):
-            signed[k] = tile(f"signed{k}", [P, N], F32, on)[:]
-            nc.gpsimd.tensor_tensor(signed[k][:, cut:], y_pair[k // 2][:, k % 2, cut:], neg_ts[:, 0, cut:], ALU.mult)
-            if cut:
-                nc.vector.tensor_tensor(signed[k][:, :cut], y_pair[k // 2][:, k % 2, :cut], neg_ts_bank[:, 0, :cut], ALU.mult)
+        def sign_aside(out, labels, share):
+            scale = neg_ts[:].rearrange("r k n -> r (k n)")
+            nc.gpsimd.tensor_tensor(out[:, share:], labels[:, share:], scale[:, share : out.shape[1]], ALU.mult)
+            if share:
+                nc.vector.tensor_tensor(out[:, :share], labels[:, :share], neg_ts_bank[:, 0, :share], ALU.mult)
 
-        def score(k):
+        def score_pass(k, bank):
             codes, scales = x_ops[k]
-            scores[k] = psum.tile([P, N], F32, name="scores", tag=SCORE_BANKS[k % 3])
-            nc.tensor.matmul_mx(scores[k][:], lhsT=codes.bitcast(E4M3), lhsT_scale=scales,
+            nc.tensor.matmul_mx(bank[:], lhsT=codes.bitcast(E4M3), lhsT_scale=scales,
                                 rhs=wd_codes[:].bitcast(E4M3), rhs_scale=wd_scales[:], start=True, stop=True)
 
-        def keep_warm(k, passes=2):
-            codes, scales = x_ops[k]
-            bank = psum.tile([P, N], F32, name="unread", tag=SCORE_BANKS[k % 3])
-            for i in range(passes):
-                nc.tensor.matmul_mx(bank[:], lhsT=codes.bitcast(E4M3), lhsT_scale=scales,
-                                    rhs=wd_codes[:].bitcast(E4M3), rhs_scale=wd_scales[:], start=True, stop=True)
+        def score(k):
+            scores[k] = psum.tile([P, N], F32, name="scores", tag=SCORE_BANKS[k % len(SCORE_BANKS)])
+            score_pass(k, scores[k])
 
-        def margin(k, on=None):
-            neg_ya[k] = tile(f"neg_ya{k}", [P, N], F32, on)
+        def keep_warm(k):
+            bank = psum.tile([P, N], F32, name="unread", tag=SCORE_BANKS[k % len(SCORE_BANKS)])
+            for i in range(2):
+                score_pass(k, bank)
+
+        def form_margin(k):
+            margin[k] = tile(f"margin{k}", [P, N], F32)
             if k in SORTED:
-                nc.vector.tensor_tensor(as_laid(neg_ya[k][:]), by_words(scores[k][:]), as_laid(signed[k]), ALU.mult)
+                nc.vector.tensor_tensor(as_sorted(margin[k][:]), by_words(scores[k][:]), as_sorted(signed[k]), ALU.mult)
             else:
-                nc.vector.tensor_tensor(neg_ya[k][:], scores[k][:], signed[k], ALU.mult)
+                nc.vector.tensor_tensor(margin[k][:], scores[k][:], signed[k], ALU.mult)
 
-        def clip(k, on=None):
-            hinge[k] = tile(f"hinge{k}", [P, N], F32, on)
-            nc.scalar.activation(hinge[k][:], neg_ya[k][:], ACT.Relu, bias=1.0, scale=1.0)
+        def clip(k):
+            hinge[k] = tile(f"hinge{k}", [P, N], F32)
+            nc.scalar.activation(hinge[k][:], margin[k][:], ACT.Relu, bias=1.0, scale=1.0)
 
-        def weigh(k, on=None):
-            h[k] = tile(f"h{k}", [P, N], BF16, on)
-            factor = weight(wt_first, wt_second, k)
+        def weigh(k):
+            h[k] = tile(f"h{k}", [P, N], BF16)
+            weight = wt_first[:, k // 2, k % 2 : k % 2 + 1] if k < PACK else wt_second[:, k - PACK : k - PACK + 1]
             if k == LAST:
                 for u in range(2):
-                    nc.vector.scalar_tensor_tensor(h[k][:].rearrange("r (u s e) -> r u s e", u=2, e=2)[:, u],
-                                                   hinge[k][:].rearrange("r (s u e) -> r u s e", u=2, e=2)[:, u], factor,
-                                                   signed[k].rearrange("r (s u e) -> r u s e", u=2, e=2)[:, u], ALU.mult, ALU.mult)
+                    nc.vector.scalar_tensor_tensor(as_sorted(h[k][:])[:, u], by_words(hinge[k][:])[:, u], weight,
+                                                   by_words(signed[k])[:, u], ALU.mult, ALU.mult)
             else:
-                nc.vector.scalar_tensor_tensor(h[k][:], hinge[k][:], factor, signed[k], ALU.mult, ALU.mult)
+                nc.vector.scalar_tensor_tensor(h[k][:], hinge[k][:], weight, signed[k], ALU.mult, ALU.mult)
 
-        def turn_h(k, bank=None):
-            words = h[k][:].bitcast(F32).rearrange("r (u s) -> r u s" if k == LAST or k in SORTED else "r (s u) -> r u s", u=2)
-            h_bank[k] = psum.tile([P, 2, P], F32, name="h_turn", tag=bank or TURN_BANKS[k % 2])
+        def turn_h(k):
+            words = h[k][:].bitcast(F32).rearrange("r (u s) -> r u s" if k in SORTED or k == LAST else "r (s u) -> r u s", u=2)
+            h_bank[k] = psum.tile([P, 2, P], F32, name="h_turn", tag=TURN_BANKS[k % 2])
             for u in range(2):
                 nc.tensor.transpose(h_bank[k][:, u, :], words[:, u, :], ident[:])
 
-        def regroup(k, on=None, copy=nc.scalar.copy):
+        def regroup(k):
             if k < PACK:
                 a, e = divmod(k, 2)
                 if a == 0:
-                    h_words[e] = tile(f"h_words{e}", [P, 2, P, 2], F32, on)
-                copy(h_words[e][:, :, a * HALF : (a + 1) * HALF, :].rearrange("s c i u -> s i c u"),
-                     h_bank[k][:].rearrange("s u (i c) -> s i c u", c=2))
+                    h_words[e] = tile(f"h_words{e}", [P, 2, P, 2], F32)
+                nc.scalar.copy(h_words[e][:, :, a * HALF : (a + 1) * HALF, :].rearrange("s c i u -> s i c u"),
+                               h_bank[k][:].rearrange("s u (i c) -> s i c u", c=2))
             else:
-                h_words[k] = tile(f"h_words{k}", [P, 1, P, 2], F32, on)
-                copy(h_words[k][:, 0], h_bank[k][:].rearrange("s u r -> s r u"))
+                h_words[k] = tile(f"h_words{k}", [P, 1, P, 2], F32)
+                nc.scalar.copy(h_words[k][:, 0], h_bank[k][:].rearrange("s u r -> s r u"))
 
-        def quantise_h(group, on=None):
+        def quantise_h(group):
             places = ((0, group), (0, group + 2)) if group < 2 else ((1, group - PACK),)
-            codes = tile(f"h_codes{group}", [P, len(places) * P], U32, on)
+            codes = tile(f"h_codes{group}", [P, len(places) * P], U32)
             scales = tile(f"h_scales{group}", [P, len(places) * P], U8)
             nc.vector.quantize_mx(codes[:].bitcast(E5M2), scales[:],
                                   h_words[group][:].rearrange("s i r u -> s (i r u)").bitcast(BF16))
@@ -275,154 +223,155 @@ def tile_attend_gsqh_pl_x_ts_kernel(tc, xT, wT, y, wt, ts, offs, out_0, out_1, o
         grad_rows = [tile(f"grad_rows{o}", [P, PACK, D], F32) for o in range(PASSES)]
         out_rows = out_0[0].rearrange("(o p t) d -> o p t d", p=P, t=PACK)
         out_scales = tile("out_scales", [P, PASSES, D], U8)
-        woven, out_codes = {}, {}
+        out_codes = [tile(f"out_codes{o}", [P, D], U32) for o in range(PASSES)]
+        woven = [[tile(f"woven{o}{c}", [P, D // 2, PACK], BF16) for c in range(2)] for o in range(PASSES)]
 
-        def gradient(o, t, bank=None):
+        def gradient(o, t, bank):
             codes, scales = h_ops[o, t]
-            g_bank[o, t] = psum.tile([P, 2, P, 2], F32, name="grad", tag=bank or GRADIENT_BANKS[len(g_bank) % len(GRADIENT_BANKS)])
+            g_bank[o, t] = psum.tile([P, 2, P, 2], F32, name="grad", tag=bank)
             nc.tensor.matmul_mx(g_bank[o, t][:].rearrange("r u p e -> r (u p e)"), lhsT=codes.bitcast(E5M2), lhsT_scale=scales,
-                                rhs=wn["codes"][:].bitcast(E4M3), rhs_scale=wn_scales[:], start=True, stop=True)
+                                rhs=wn_codes[:].bitcast(E4M3), rhs_scale=wn_scales[:], start=True, stop=True)
 
-        def empty(o, t, cuts=(0, P), copy=nc.scalar.copy):
+        def empty(o, t, cuts=(0, P)):
             rows = grad_rows[o][:, t, :].rearrange("r (p u e) -> r p u e", u=2, e=2)
             for start, stop in zip(cuts, cuts[1:]):
-                copy(rows[:, start:stop], g_bank[o, t][:, :, start:stop, :].rearrange("r u p e -> r p u e"))
+                nc.scalar.copy(rows[:, start:stop], g_bank[o, t][:, :, start:stop, :].rearrange("r u p e -> r p u e"))
             nc.sync.dma_start(out_rows[o, :, t, :], grad_rows[o][:, t, :])
 
-        def weave(copy, o, c, start=0, stop=D // 2, on=None):
-            if (o, c) not in woven:
-                woven[o, c] = tile(f"woven{o}{c}", [P, D // 2, PACK], BF16, on)
+        def weave(copy, o, c, start=0, stop=D // 2):
             first = c * D // 2
-            copy(woven[o, c][:, start:stop, :].rearrange("p (c i) t -> p c t i", i=4),
+            copy(woven[o][c][:, start:stop, :].rearrange("p (c i) t -> p c t i", i=4),
                  grad_rows[o][:, :, first + start : first + stop].rearrange("p t (c i) -> p c t i", i=4))
 
         def quantise_out(o, c):
-            if o not in out_codes:
-                out_codes[o] = tile(f"out_codes{o}", [P, D], U32)
             cols = slice(c * D // 2, (c + 1) * D // 2)
-            nc.vector.quantize_mx(out_codes[o][:, cols].bitcast(E4M3), out_scales[:, o, cols], woven[o, c][:].rearrange("p d t -> p (d t)"))
+            nc.vector.quantize_mx(out_codes[o][:, cols].bitcast(E4M3), out_scales[:, o, cols],
+                                  woven[o][c][:].rearrange("p d t -> p (d t)"))
 
-        def store_words(o, start, stop):
-            nc.sync.dma_start(out_1[o].rearrange("p d l -> p (d l)").bitcast(I32)[:, start:stop], out_codes[o][:, start:stop].bitcast(I32))
+        def store_words(o, cols):
+            nc.sync.dma_start(out_1[o].rearrange("p d l -> p (d l)").bitcast(I32)[:, cols], out_codes[o][:, cols].bitcast(I32))
 
-        def on_gpsimd(out, in_):
-            nc.gpsimd.tensor_scalar(out, in_, 1.0, 0.0, ALU.mult, ALU.add)
-
-        on_vector, on_scalar = nc.vector.tensor_copy, nc.scalar.copy
         gather_w(0)
         spread_ts()
         gather_w(1)
-        turn_w(0)
+        turn_w(0, w_words[:, 0])
         copy_w(0)
         gather_w(2)
         gather_w(3)
-        round_half(0,on_vector,"w_table2")
-        quantise_w()
-        quantise_x(0)
-        quantise_turned(0,"x_raw0")
-        deal_and_turn_w(1,None)
+        x_half0 = tile("x_half0", [P, 2, P, PACK], BF16, "w_table2")
+        round_x(on_vector, x_half0, x_raw[0], 0, 2 * P, 0)
+        nc.vector.quantize_mx(wd_codes[:].bitcast(E4M3), wd_scales[:], w_listed[:].rearrange("p n j -> p (n j)"))
+        quantise_x(0, x_half0)
+        wn_codes = tile("wn_codes", [P, D], U32, "x_raw0")
+        quantise_turned(0)
+        w_dealt = tile("w_dealt", [P, PACK, P], F32)
+        nc.scalar.copy(w_dealt[:].rearrange("p t s -> p s t"), w_words[:, 1].rearrange("p t s -> p s t"))
+        turn_w(1, w_dealt)
+
         score(0)
         score(1)
-        sign(0,12)
-        sign_aside(1,"w_turned0",128)
-        copy_w(1,None,0,HALF)
-        margin(0)
-        margin(1,8)
-        round_first(1,0,on_scalar,"w_dealt1")
-        round_first(1,1,on_scalar)
+        sign(0)
+        signed[1] = tile("signed1", [P, N], F32, "w_turned0")[:]
+        sign_aside(signed[1], y_pair[0][:, 1, :], VECTOR_SHARE)
+        form_margin(0)
+        form_margin(1)
+        x_half1 = tile("x_half1", [P, 2, P, PACK], BF16, "w_dealt")
+        for i in range(2):
+            round_x(on_scalar, x_half1, x_raw[1], i * P, (i + 1) * P, i * HALF)
         clip(0)
         clip(1)
-        copy_w(1,None,HALF,P)
-        sign(2,"x_codes0")
-        sign_aside(3)
-        quantise_x(1)
+        copy_w(1)
+        sign(2, "x_codes0")
+        signed[3] = tile("signed3", [P, N], F32)[:]
+        sign_aside(signed[3], y_pair[1][:, 1, :], 0)
+        quantise_x(2, x_half1)
         score(2)
         score(3)
-        weigh(0)
-        turn_h(0)
-        weigh(1)
-        turn_h(1)
-        margin(2)
-        round_second(0,on_scalar,5)
-        round_second(1,on_scalar)
-        round_second(2,on_scalar)
+        for k in range(2):
+            weigh(k)
+            turn_h(k)
+        form_margin(2)
+        x_second = tile("x_second", [P, PACK, P, PACK], BF16)
+        for i in range(2):
+            round_x(on_scalar, x_second, x_raw[2], i * P, (i + 1) * P, i * P // PACK)
         clip(2)
-        round_second(3,on_vector)
-        margin(3)
+        form_margin(3)
+        clip(3)
         quantise_turned(1)
-        quantise_x(2)
-        score(4)
-        clip(3,1)
+        round_x(on_vector, x_second, x_raw[3], 0, 2 * P, HALF)
         regroup(0)
         regroup(1)
         weigh(2)
         turn_h(2)
+        quantise_x(PACK, x_second)
+        score(4)
         weigh(3)
         turn_h(3)
         score(5)
         score(6)
         regroup(2)
         regroup(3)
-        sign(4,"hinge2")
-        sign_pair_aside(3,2,128)
-        sign(5,"signed3")
-        margin(4)
-        score(7)
-        margin(5)
+
+        sign(4, "hinge2")
+        signed_last = tile("signed_last", [P, 2 * N], F32)
+        sign_aside(signed_last[:], y_pair[3][:].rearrange("r k n -> r (k n)"), VECTOR_SHARE)
+        signed[6], signed[7] = signed_last[:, :N], signed_last[:, N:]
+        sign(5, "signed3")
+        form_margin(4)
+        score(LAST)
+        form_margin(5)
         clip(4)
         clip(5)
+
         quantise_h(0)
-        gradient(0,0,"bank5")
-        gradient(0,2,"bank6")
+        gradient(0, 0, COLUMN_BANKS[1])
+        gradient(0, 2, COLUMN_BANKS[0])
         quantise_h(1)
-        gradient(0,1,"bank7")
-        margin(6)
-        weigh(4)
-        turn_h(4)
-        keep_warm(6)
-        margin(7)
-        weigh(5)
-        turn_h(5)
-        keep_warm(7)
-        empty(0,0)
-        gradient(0,3,"bank5")
+        gradient(0, 1, TS_BANK)
+        for k in (6, 7):
+            form_margin(k)
+            weigh(k - 2)
+            turn_h(k - 2)
+            keep_warm(k)
+        empty(0, 0)
+        gradient(0, 3, COLUMN_BANKS[1])
         clip(6)
-        empty(0,2)
-        clip(7)
+        empty(0, 2)
+        clip(LAST)
         regroup(4)
         regroup(5)
-        empty(0,1)
+        empty(0, 1)
         weigh(6)
         turn_h(6)
-        weigh(7)
+        weigh(LAST)
         quantise_h(4)
-        turn_h(7)
-        gradient(1,0,"bank2")
+        turn_h(LAST)
+
+        gradient(1, 0, SCORE_BANKS[2])
         quantise_h(5)
-        gradient(1,1,"bank0")
-        empty(0,3)
+        gradient(1, 1, SCORE_BANKS[0])
+        empty(0, 3)
         regroup(6)
-        regroup(7)
+        regroup(LAST)
         quantise_h(6)
-        gradient(1,2,"bank1")
-        weave(on_vector,0,0)
-        quantise_h(7)
-        gradient(1,3,"bank6")
-        empty(1,0)
-        empty(1,1)
-        weave(on_vector,0,1)
-        quantise_out(0,0)
-        quantise_out(0,1)
-        empty(1,2)
-        store_words(0,0,D)
-        empty(1,3,(0,HALF,P))
-        weave(on_vector,1,0)
-        weave(on_scalar,1,1,128,256)
-        weave(on_vector,1,1,0,128)
-        quantise_out(1,0)
-        store_words(1,0,256)
-        quantise_out(1,1)
-        store_words(1,256,512)
+        gradient(1, 2, SCORE_BANKS[1])
+        weave(on_vector, 0, 0)
+        quantise_h(LAST)
+        gradient(1, 3, COLUMN_BANKS[0])
+        empty(1, 0)
+        empty(1, 1)
+        weave(on_vector, 0, 1)
+        for c in range(2):
+            quantise_out(0, c)
+        empty(1, 2)
+        store_words(0, slice(0, D))
+        empty(1, 3, (0, HALF, P))
+        weave(on_vector, 1, 0)
+        weave(on_scalar, 1, 1, D // 2 - SCALAR_WEAVES, D // 2)
+        weave(on_vector, 1, 1, 0, D // 2 - SCALAR_WEAVES)
+        for c in range(2):
+            quantise_out(1, c)
+            store_words(1, slice(c * D // 2, (c + 1) * D // 2))
 
         for q in range(4):
             queue = nc.scalar if q % 2 == 0 else nc.sync

@@ -168,11 +168,6 @@ def tile_attend_gsqh_pl_x_ts_kernel(tc, xT, wT, y, wt, ts, offs, out_0, out_1, o
             scores[k] = psum.tile([P, N], F32, name="scores", tag=SCORE_BANKS[k % len(SCORE_BANKS)])
             score_pass(k, scores[k])
 
-        def keep_warm(k):
-            bank = psum.tile([P, N], F32, name="unread", tag=SCORE_BANKS[k % len(SCORE_BANKS)])
-            for i in range(2):
-                score_pass(k, bank)
-
         def form_margin(k):
             margin[k] = tile(f"margin{k}", [P, N], F32)
             if k in SORTED:
@@ -332,7 +327,6 @@ def tile_attend_gsqh_pl_x_ts_kernel(tc, xT, wT, y, wt, ts, offs, out_0, out_1, o
             form_margin(k)
             weigh(k - 2)
             turn_h(k - 2)
-            keep_warm(k)
         empty(0, 0)
         gradient(0, 3, COLUMN_BANKS[1])
         clip(6)

@@ -322,13 +322,12 @@ def tile_attend_gsqh_pl_x_ts_kernel(tc, xT, wT, y, wt, ts, offs, out_0, out_1, o
         gradient(0, 0, COLUMN_BANKS[1])
         gradient(0, 2, COLUMN_BANKS[0])
         quantise_h(1)
-        gradient(0, 1, TS_BANK)
-        for k in (6, 7):
+        for k, t in ((6, 1), (7, 3)):
             form_margin(k)
             weigh(k - 2)
             turn_h(k - 2)
+            gradient(0, t, SCORE_BANKS[k % len(SCORE_BANKS)])
         empty(0, 0)
-        gradient(0, 3, COLUMN_BANKS[1])
         clip(6)
         empty(0, 2)
         clip(LAST)
@@ -343,12 +342,12 @@ def tile_attend_gsqh_pl_x_ts_kernel(tc, xT, wT, y, wt, ts, offs, out_0, out_1, o
 
         gradient(1, 0, SCORE_BANKS[2])
         quantise_h(5)
-        gradient(1, 1, SCORE_BANKS[0])
+        gradient(1, 1, TS_BANK)
         empty(0, 3)
         regroup(6)
         regroup(LAST)
         quantise_h(6)
-        gradient(1, 2, SCORE_BANKS[1])
+        gradient(1, 2, COLUMN_BANKS[1])
         weave(on_vector, 0, 0)
         quantise_h(LAST)
         gradient(1, 3, COLUMN_BANKS[0])

@@ -159,14 +159,18 @@ def tile_attend_gsqh_pl_x_ts_kernel(tc, xT, wT, y, wt, ts, offs, out_0, out_1, o
             if share:
                 nc.vector.tensor_tensor(out[:, :share], labels[:, :share], neg_ts_bank[:, 0, :share], ALU.mult)
 
-        def score_pass(k, bank):
+        def score_pass(k, bank, slots=N):
             codes, scales = x_ops[k]
-            nc.tensor.matmul_mx(bank[:], lhsT=codes.bitcast(E4M3), lhsT_scale=scales,
-                                rhs=wd_codes[:].bitcast(E4M3), rhs_scale=wd_scales[:], start=True, stop=True)
+            nc.tensor.matmul_mx(bank[:, :slots], lhsT=codes.bitcast(E4M3), lhsT_scale=scales,
+                                rhs=wd_codes[:, :slots].bitcast(E4M3), rhs_scale=wd_scales[:, :slots], start=True, stop=True)
 
         def score(k):
             scores[k] = psum.tile([P, N], F32, name="scores", tag=SCORE_BANKS[k % len(SCORE_BANKS)])
             score_pass(k, scores[k])
+
+        def keep_warm(k):
+            bank = psum.tile([P, N], F32, name="unread", tag=SCORE_BANKS[k % len(SCORE_BANKS)])
+            score_pass(k, bank, N if k == LAST else N // 2)
 
         def form_margin(k):
             margin[k] = tile(f"margin{k}", [P, N], F32)
@@ -326,6 +330,7 @@ def tile_attend_gsqh_pl_x_ts_kernel(tc, xT, wT, y, wt, ts, offs, out_0, out_1, o
             form_margin(k)
             weigh(k - 2)
             turn_h(k - 2)
+            keep_warm(k)
             gradient(0, t, SCORE_BANKS[k % len(SCORE_BANKS)])
         empty(0, 0)
         clip(6)

@@ -56,7 +56,7 @@ def tile_attend_gsqh_pl_x_ts_kernel(tc, xT, wT, y, wt, ts, offs, out_0, out_1, o
 
         offsets = keep.tile([P, N // 16], U16, name="offsets")
         ts_row = tile("ts_row", [P, T], F32)
-        nc.vector.memset(ts_row[:], 0.0)
+        nc.vector.memset(ts_row[: P - 1, :], 0.0)
         ident = keep.tile([P, P], F32, name="ident")
         make_identity(nc, ident[:])
 
@@ -70,13 +70,12 @@ def tile_attend_gsqh_pl_x_ts_kernel(tc, xT, wT, y, wt, ts, offs, out_0, out_1, o
         wt_first = keep.tile([P, 2, 2], F32, name="wt_first")
         wt_second = keep.tile([P, PACK], F32, name="wt_second")
 
+        nc.sync.dma_start(offsets[:], offs)
+        nc.scalar.dma_start(ts_row[P - 1 :, :], ts[0:1, :])
         nc.scalar.dma_start(wt_first[:], wt[0, :PASS].rearrange("(a m e) one -> m a (e one)", m=P, e=2))
         nc.scalar.dma_start(wt_second[:], wt[0, PASS:].rearrange("(p t) one -> p (t one)", t=PACK))
         for j in range(PACK):
             nc.sync.dma_start(w_table[j][:], w_rows[j])
-            if j == 0:
-                nc.sync.dma_start(offsets[:], offs)
-                nc.sync.dma_start(ts_row[0:1, :], ts[0:1, :])
         for i in range(2):
             nc.sync.dma_start(x_raw[i][:], x_rows[:, :, i * 2 * P : (i + 1) * 2 * P])
             nc.sync.dma_start(y_pair[i][:], y_first[i])
@@ -95,7 +94,7 @@ def tile_attend_gsqh_pl_x_ts_kernel(tc, xT, wT, y, wt, ts, offs, out_0, out_1, o
             for c in range(PACK):
                 nc.tensor.transpose(ts_turn[:, c, :], ts_listed[:, c * P : (c + 1) * P], ident[:])
             neg_ts_col = tile("neg_ts_col", [P, PACK], F32)
-            nc.scalar.activation(neg_ts_col[:], ts_turn[:, :, 0], ACT.Copy, scale=-1.0)
+            nc.scalar.activation(neg_ts_col[:], ts_turn[:, :, P - 1], ACT.Copy, scale=-1.0)
             for c in range(PACK):
                 nc.tensor.transpose(neg_ts_bank[:, 0, c * P : (c + 1) * P], neg_ts_col[:, c : c + 1].to_broadcast([P, P]), ident[:])
             nc.scalar.copy(neg_ts[:], neg_ts_bank[:].to_broadcast([P, 2, N]))
@@ -250,8 +249,8 @@ def tile_attend_gsqh_pl_x_ts_kernel(tc, xT, wT, y, wt, ts, offs, out_0, out_1, o
         def store_words(o, cols):
             nc.sync.dma_start(out_1[o].rearrange("p d l -> p (d l)").bitcast(I32)[:, cols], out_codes[o][:, cols].bitcast(I32))
 
-        gather_w(0)
         spread_ts()
+        gather_w(0)
         gather_w(1)
         turn_w(0, w_words[:, 0])
         copy_w(0)

@@ -70,19 +70,21 @@ def tile_attend_gsqh_pl_x_ts_kernel(tc, xT, wT, y, wt, ts, offs, out_0, out_1, o
         wt_first = keep.tile([P, 2, 2], F32, name="wt_first")
         wt_second = keep.tile([P, PACK], F32, name="wt_second")
 
-        nc.sync.dma_start(offsets[:], offs)
-        nc.scalar.dma_start(ts_row[P - 1 :, :], ts[0:1, :])
-        nc.scalar.dma_start(wt_first[:], wt[0, :PASS].rearrange("(a m e) one -> m a (e one)", m=P, e=2))
-        nc.scalar.dma_start(wt_second[:], wt[0, PASS:].rearrange("(p t) one -> p (t one)", t=PACK))
         for j in range(PACK):
             nc.sync.dma_start(w_table[j][:], w_rows[j])
+            if j == 0:
+                nc.sync.dma_start(offsets[:], offs)
+                nc.sync.dma_start(ts_row[P - 1 :, :], ts[0:1, :])
         for i in range(2):
             nc.sync.dma_start(x_raw[i][:], x_rows[:, :, i * 2 * P : (i + 1) * 2 * P])
             nc.sync.dma_start(y_pair[i][:], y_first[i])
+            if i == 1:
+                nc.sync.dma_start(wt_first[:], wt[0, :PASS].rearrange("(a m e) one -> m a (e one)", m=P, e=2))
         for i in range(2, PAIRS):
             nc.sync.dma_start(x_raw[i][:], x_rows[:, :, i * 2 * P : (i + 1) * 2 * P])
         for i in range(2):
             nc.sync.dma_start(y_pair[2 + i][:], y_second[i])
+        nc.sync.dma_start(wt_second[:], wt[0, PASS:].rearrange("(p t) one -> p (t one)", t=PACK))
 
         neg_ts_bank = psum.tile([P, 1, N], F32, name="neg_ts_bank", tag=TS_BANK)
         neg_ts = tile("neg_ts", [P, 2, N], F32)
@@ -249,8 +251,8 @@ def tile_attend_gsqh_pl_x_ts_kernel(tc, xT, wT, y, wt, ts, offs, out_0, out_1, o
         def store_words(o, cols):
             nc.sync.dma_start(out_1[o].rearrange("p d l -> p (d l)").bitcast(I32)[:, cols], out_codes[o][:, cols].bitcast(I32))
 
-        spread_ts()
         gather_w(0)
+        spread_ts()
         gather_w(1)
         turn_w(0, w_words[:, 0])
         copy_w(0)

@@ -34,7 +34,7 @@ TS_BANK = "bank7"
 SORTED = (4, 5)
 
 KIB = 1024
-SHARED = {"w_table3": 12, "signed0": 12, "margin1": 8, "x_second": 5, "hinge3": 1, "signed_last": 2,
+SHARED = {"w_table3": 12, "wn_codes": 12, "x_half0": 33, "signed0": 32, "signed1": 34, "margin1": 8, "x_second": 5, "hinge3": 1, "signed_last": 2,
           "margin0": 26, "x_codes2": 26, "w_turned1": 27}
 
 VECTOR_SHARE = N // 4
@@ -112,7 +112,7 @@ def tile_attend_gsqh_pl_x_ts_kernel(tc, xT, wT, y, wt, ts, offs, out_0, out_1, o
             nc.vector.tensor_copy(w_listed[:, :, j], w_table[j][:].indirect(offsets[:]))
 
         def turn_w(u, words):
-            w_bank[u] = psum.tile([P, PACK * P], F32, name=f"w_turn{u}", tag=COLUMN_BANKS[u])
+            w_bank[u] = psum.tile([P, PACK * P], F32, name=f"w_turn{u}", tag=(COLUMN_BANKS[0], SCORE_BANKS[0])[u])
             for t in range(PACK):
                 nc.tensor.transpose(w_bank[u][:, t * P : (t + 1) * P], words[:, t, :], ident[:])
 
@@ -166,7 +166,8 @@ def tile_attend_gsqh_pl_x_ts_kernel(tc, xT, wT, y, wt, ts, offs, out_0, out_1, o
                                 rhs=wd_codes[:, :slots].bitcast(E4M3), rhs_scale=wd_scales[:, :slots], start=True, stop=True)
 
         def score(k):
-            scores[k] = psum.tile([P, N], F32, name="scores", tag=SCORE_BANKS[k % len(SCORE_BANKS)])
+            bank = COLUMN_BANKS[1] if k == len(SCORE_BANKS) else SCORE_BANKS[k % len(SCORE_BANKS)]
+            scores[k] = psum.tile([P, N], F32, name="scores", tag=bank)
             score_pass(k, scores[k])
 
         def keep_warm(k):
@@ -258,24 +259,24 @@ def tile_attend_gsqh_pl_x_ts_kernel(tc, xT, wT, y, wt, ts, offs, out_0, out_1, o
         copy_w(0)
         gather_w(2)
         gather_w(3)
-        x_half0 = tile("x_half0", [P, 2, P, PACK], BF16, "w_table2")
-        round_x(on_vector, x_half0, x_raw[0], 0, 2 * P, 0)
+        x_half0 = tile("x_half0", [P, 2, P, PACK], BF16)
+        round_x(on_scalar, x_half0, x_raw[0], 0, 2 * P, 0)
+        wn_codes = tile("wn_codes", [P, D], U32)
+        quantise_turned(0)
         nc.vector.quantize_mx(wd_codes[:].bitcast(E4M3), wd_scales[:], w_listed[:].rearrange("p n j -> p (n j)"))
         quantise_x(0, x_half0)
-        wn_codes = tile("wn_codes", [P, D], U32, "x_raw0")
-        quantise_turned(0)
-        w_dealt = tile("w_dealt", [P, PACK, P], F32)
+        w_dealt = tile("w_dealt", [P, PACK, P], F32, "x_raw0")
         nc.scalar.copy(w_dealt[:].rearrange("p t s -> p s t"), w_words[:, 1].rearrange("p t s -> p s t"))
-        turn_w(1, w_dealt)
 
         score(0)
         score(1)
         sign(0)
-        signed[1] = tile("signed1", [P, N], F32, "w_turned0")[:]
+        signed[1] = tile("signed1", [P, N], F32)[:]
         sign_aside(signed[1], y_pair[0][:, 1, :], VECTOR_SHARE)
         form_margin(0)
+        turn_w(1, w_dealt)
         form_margin(1)
-        x_half1 = tile("x_half1", [P, 2, P, PACK], BF16, "w_dealt")
+        x_half1 = tile("x_half1", [P, 2, P, PACK], BF16)
         for i in range(2):
             round_x(on_scalar, x_half1, x_raw[1], i * P, (i + 1) * P, i * HALF)
         clip(0)

from contextlib import ExitStack

import concourse.mybir as mybir
from concourse.masks import make_identity

N, T, D, R = 512, 2048, 512, 1024
FLOPS = 2 * 2 * R * N * D

F32 = mybir.dt.float32
BF16 = mybir.dt.bfloat16
I32 = mybir.dt.int32
U32 = mybir.dt.uint32
U16 = mybir.dt.uint16
U8 = mybir.dt.uint8
E4M3 = mybir.dt.float8_e4m3fn_x4
E5M2 = mybir.dt.float8_e5m2_x4
ALU = mybir.AluOpType
ACT = mybir.ActivationFunctionType

P = 128
HALF = P // 2
PACK = 4
PASS = P * PACK
PASSES = R // PASS
TILES = PASSES * PACK
LAST = TILES - 1
PAIRS = TILES // 2

SCORE_BANKS = ("bank0", "bank1", "bank2")
TURN_BANKS = ("bank3", "bank4")
COLUMN_BANKS = ("bank6", "bank5")
TS_BANK = "bank7"

SORTED = (4, 5)

KIB = 1024
SHARED = {"w_table3": 12, "wn_codes": 12, "x_half0": 33, "signed0": 32, "signed1": 34, "margin1": 8, "x_second": 5, "hinge3": 1, "signed_last": 2,
          "margin0": 26, "x_codes2": 26, "w_turned1": 27}

VECTOR_SHARE = N // 4
SCALAR_WEAVES = D // 4


def tile_attend_gsqh_pl_x_ts_kernel(tc, xT, wT, y, wt, ts, offs, out_0, out_1, out_2):
    nc = tc.nc
    on_vector, on_scalar = nc.vector.tensor_copy, nc.scalar.copy
    with ExitStack() as ctx:
        keep = ctx.enter_context(tc.tile_pool(name="keep", bufs=1))
        shared = ctx.enter_context(tc.tile_pool(name="shared", bufs=1))
        psum = ctx.enter_context(tc.psum_pool(name="psum", bufs=1))

        def tile(name, shape, dtype, on=None):
            if name in SHARED:
                return shared.tile(shape, dtype, name=name, offset=SHARED[name] * KIB, align_bytes=64)
            return keep.tile(shape, dtype, name=name, tag=on or name, align_bytes=64)

        offsets = keep.tile([P, N // 16], U16, name="offsets")
        ts_row = tile("ts_row", [P, T], F32)
        nc.vector.memset(ts_row[: P - 1, :], 0.0)
        ident = keep.tile([P, P], F32, name="ident")
        make_identity(nc, ident[:])

        w_rows = wT.rearrange("(p j) c -> j p c", j=PACK)
        w_table = [tile(f"w_table{j}", [P, T], F32) for j in range(PACK)]
        x_rows = xT[0].rearrange("(p j) r -> p j r", j=PACK)
        y_first = y[0, :PASS].rearrange("(a m e) n -> a m e n", m=P, e=2)
        y_second = y[0, PASS:].rearrange("(p c e) n -> c p e n", c=2, e=2)
        x_raw = [tile(f"x_raw{i}", [P, PACK, 2 * P], F32) for i in range(PAIRS)]
        y_pair = [tile(f"y_pair{i}", [P, 2, N], F32) for i in range(PAIRS)]
        wt_first = keep.tile([P, 2, 2], F32, name="wt_first")
        wt_second = keep.tile([P, PACK], F32, name="wt_second")

        for j in range(PACK):
            nc.sync.dma_start(w_table[j][:], w_rows[j])
            if j == 0:
                nc.sync.dma_start(offsets[:], offs)
                nc.sync.dma_start(ts_row[P - 1 :, :], ts[0:1, :])
        for i in range(2):
            nc.sync.dma_start(x_raw[i][:], x_rows[:, :, i * 2 * P : (i + 1) * 2 * P])
            nc.sync.dma_start(y_pair[i][:], y_first[i])
            if i == 1:
                nc.sync.dma_start(wt_first[:], wt[0, :PASS].rearrange("(a m e) one -> m a (e one)", m=P, e=2))
        for i in range(2, PAIRS):
            nc.sync.dma_start(x_raw[i][:], x_rows[:, :, i * 2 * P : (i + 1) * 2 * P])
        for i in range(2):
            nc.sync.dma_start(y_pair[2 + i][:], y_second[i])
        nc.sync.dma_start(wt_second[:], wt[0, PASS:].rearrange("(p t) one -> p (t one)", t=PACK))

        neg_ts_bank = psum.tile([P, 1, N], F32, name="neg_ts_bank", tag=TS_BANK)
        neg_ts = tile("neg_ts", [P, 2, N], F32)

        def spread_ts():
            ts_listed = tile("ts_listed", [P, N], F32)
            nc.vector.tensor_copy(ts_listed[:], ts_row[:].indirect(offsets[:]))
            ts_turn = psum.tile([P, PACK, P], F32, name="ts_turn", tag=TURN_BANKS[1])
            for c in range(PACK):
                nc.tensor.transpose(ts_turn[:, c, :], ts_listed[:, c * P : (c + 1) * P], ident[:])
            neg_ts_col = tile("neg_ts_col", [P, PACK], F32)
            nc.scalar.activation(neg_ts_col[:], ts_turn[:, :, P - 1], ACT.Copy, scale=-1.0)
            for c in range(PACK):
                nc.tensor.transpose(neg_ts_bank[:, 0, c * P : (c + 1) * P], neg_ts_col[:, c : c + 1].to_broadcast([P, P]), ident[:])
            nc.scalar.copy(neg_ts[:], neg_ts_bank[:].to_broadcast([P, 2, N]))

        w_listed = tile("w_listed", [P, N, PACK], BF16)
        w_words = w_listed[:].rearrange("p n j -> p (n j)").bitcast(F32).rearrange("p (s t u) -> p u t s", t=PACK, u=2)
        wd_codes = tile("wd_codes", [P, N], U32)
        wd_scales = tile("wd_scales", [P, N], U8)
        wn_scales = tile("wn_scales", [P, D], U8)
        w_bank, w_turned = {}, {}

        def gather_w(j):
            nc.vector.tensor_copy(w_listed[:, :, j], w_table[j][:].indirect(offsets[:]))

        def turn_w(u, words):
            w_bank[u] = psum.tile([P, PACK * P], F32, name=f"w_turn{u}", tag=(COLUMN_BANKS[0], SCORE_BANKS[0])[u])
            for t in range(PACK):
                nc.tensor.transpose(w_bank[u][:, t * P : (t + 1) * P], words[:, t, :], ident[:])

        def copy_w(u):
            w_turned[u] = tile(f"w_turned{u}", [P, P, 2, PACK], BF16)
            nc.scalar.copy(w_turned[u][:], w_bank[u][:].bitcast(BF16).rearrange("s (t p e) -> s p e t", t=PACK, e=2))

        def quantise_turned(u):
            cols = slice(u * D // 2, (u + 1) * D // 2)
            nc.vector.quantize_mx(wn_codes[:, cols].bitcast(E4M3), wn_scales[:, cols],
                                  w_turned[u][:].rearrange("s p e t -> s (p e t)"))

        x_ops, signed, scores, margin, hinge, h, h_bank, h_words, h_ops, g_bank = ({} for i in range(10))

        def round_x(copy, rounded, raw, start, stop, first):
            count = rounded.shape[1]
            copy(rounded[:, :, first : first + (stop - start) // count, :].rearrange("p e m j -> p m j e"),
                 raw[:, :, start:stop].rearrange("p j (m e) -> p m j e", e=count))

        def quantise_x(first, rounded):
            count = rounded.shape[1]
            codes = tile(f"x_codes{first}", [P, count * P], U32)
            scales = tile(f"x_scales{first}", [P, count * P], U8)
            nc.vector.quantize_mx(codes[:].bitcast(E4M3), scales[:], rounded[:].rearrange("p e m j -> p (e m j)"))
            for i in range(count):
                x_ops[first + i] = codes[:, i * P : (i + 1) * P], scales[:, i * P : (i + 1) * P]

        def by_words(slots):
            return slots.rearrange("r (s u e) -> r u s e", u=2, e=2)

        def as_sorted(slots):
            return slots.rearrange("r (u s e) -> r u s e", u=2, e=2)

        def sign(k, on=None):
            signed[k] = tile(f"signed{k}", [P, N], F32, on)[:]
            labels, scale = y_pair[k // 2][:, k % 2, :], neg_ts_bank[:, 0, :]
            if k in SORTED:
                nc.vector.tensor_tensor(as_sorted(signed[k]), by_words(labels), by_words(scale), ALU.mult)
            else:
                nc.vector.tensor_tensor(signed[k], labels, scale, ALU.mult)

        def sign_aside(out, labels, share):
            scale = neg_ts[:].rearrange("r k n -> r (k n)")
            nc.gpsimd.tensor_tensor(out[:, share:], labels[:, share:], scale[:, share : out.shape[1]], ALU.mult)
            if share:
                nc.vector.tensor_tensor(out[:, :share], labels[:, :share], neg_ts_bank[:, 0, :share], ALU.mult)

        def score_pass(k, bank, slots=N):
            codes, scales = x_ops[k]
            nc.tensor.matmul_mx(bank[:, :slots], lhsT=codes.bitcast(E4M3), lhsT_scale=scales,
                                rhs=wd_codes[:, :slots].bitcast(E4M3), rhs_scale=wd_scales[:, :slots], start=True, stop=True)

        def score(k):
            bank = COLUMN_BANKS[1] if k == len(SCORE_BANKS) else SCORE_BANKS[k % len(SCORE_BANKS)]
            scores[k] = psum.tile([P, N], F32, name="scores", tag=bank)
            score_pass(k, scores[k])

        def keep_warm(k):
            bank = psum.tile([P, N], F32, name="unread", tag=SCORE_BANKS[k % len(SCORE_BANKS)])
            score_pass(k, bank, N if k == LAST else N // 2)

        def form_margin(k):
            margin[k] = tile(f"margin{k}", [P, N], F32)
            if k in SORTED:
                nc.vector.tensor_tensor(as_sorted(margin[k][:]), by_words(scores[k][:]), as_sorted(signed[k]), ALU.mult)
            else:
                nc.vector.tensor_tensor(margin[k][:], scores[k][:], signed[k], ALU.mult)

        def clip(k):
            hinge[k] = tile(f"hinge{k}", [P, N], F32)
            nc.scalar.activation(hinge[k][:], margin[k][:], ACT.Relu, bias=1.0, scale=1.0)

        def weigh(k):
            h[k] = tile(f"h{k}", [P, N], BF16)
            weight = wt_first[:, k // 2, k % 2 : k % 2 + 1] if k < PACK else wt_second[:, k - PACK : k - PACK + 1]
            if k == LAST:
                for u in range(2):
                    nc.vector.scalar_tensor_tensor(as_sorted(h[k][:])[:, u], by_words(hinge[k][:])[:, u], weight,
                                                   by_words(signed[k])[:, u], ALU.mult, ALU.mult)
            else:
                nc.vector.scalar_tensor_tensor(h[k][:], hinge[k][:], weight, signed[k], ALU.mult, ALU.mult)

        def turn_h(k):
            words = h[k][:].bitcast(F32).rearrange("r (u s) -> r u s" if k in SORTED or k == LAST else "r (s u) -> r u s", u=2)
            h_bank[k] = psum.tile([P, 2, P], F32, name="h_turn", tag=TURN_BANKS[k % 2])
            for u in range(2):
                nc.tensor.transpose(h_bank[k][:, u, :], words[:, u, :], ident[:])

        def regroup(k):
            if k < PACK:
                a, e = divmod(k, 2)
                if a == 0:
                    h_words[e] = tile(f"h_words{e}", [P, 2, P, 2], F32)
                nc.scalar.copy(h_words[e][:, :, a * HALF : (a + 1) * HALF, :].rearrange("s c i u -> s i c u"),
                               h_bank[k][:].rearrange("s u (i c) -> s i c u", c=2))
            else:
                h_words[k] = tile(f"h_words{k}", [P, 1, P, 2], F32)
                nc.scalar.copy(h_words[k][:, 0], h_bank[k][:].rearrange("s u r -> s r u"))

        def quantise_h(group):
            places = ((0, group), (0, group + 2)) if group < 2 else ((1, group - PACK),)
            codes = tile(f"h_codes{group}", [P, len(places) * P], U32)
            scales = tile(f"h_scales{group}", [P, len(places) * P], U8)
            nc.vector.quantize_mx(codes[:].bitcast(E5M2), scales[:],
                                  h_words[group][:].rearrange("s i r u -> s (i r u)").bitcast(BF16))
            for i, place in enumerate(places):
                h_ops[place] = codes[:, i * P : (i + 1) * P], scales[:, i * P : (i + 1) * P]

        grad_rows = [tile(f"grad_rows{o}", [P, PACK, D], F32) for o in range(PASSES)]
        out_rows = out_0[0].rearrange("(o p t) d -> o p t d", p=P, t=PACK)
        out_scales = tile("out_scales", [P, PASSES, D], U8)
        out_codes = [tile(f"out_codes{o}", [P, D], U32) for o in range(PASSES)]
        woven = [[tile(f"woven{o}{c}", [P, D // 2, PACK], BF16) for c in range(2)] for o in range(PASSES)]

        def gradient(o, t, bank):
            codes, scales = h_ops[o, t]
            g_bank[o, t] = psum.tile([P, 2, P, 2], F32, name="grad", tag=bank)
            nc.tensor.matmul_mx(g_bank[o, t][:].rearrange("r u p e -> r (u p e)"), lhsT=codes.bitcast(E5M2), lhsT_scale=scales,
                                rhs=wn_codes[:].bitcast(E4M3), rhs_scale=wn_scales[:], start=True, stop=True)

        def empty(o, t, cuts=(0, P)):
            rows = grad_rows[o][:, t, :].rearrange("r (p u e) -> r p u e", u=2, e=2)
            for start, stop in zip(cuts, cuts[1:]):
                nc.scalar.copy(rows[:, start:stop], g_bank[o, t][:, :, start:stop, :].rearrange("r u p e -> r p u e"))
            nc.sync.dma_start(out_rows[o, :, t, :], grad_rows[o][:, t, :])

        def weave(copy, o, c, start=0, stop=D // 2):
            first = c * D // 2
            copy(woven[o][c][:, start:stop, :].rearrange("p (c i) t -> p c t i", i=4),
                 grad_rows[o][:, :, first + start : first + stop].rearrange("p t (c i) -> p c t i", i=4))

        def quantise_out(o, c):
            cols = slice(c * D // 2, (c + 1) * D // 2)
            nc.vector.quantize_mx(out_codes[o][:, cols].bitcast(E4M3), out_scales[:, o, cols],
                                  woven[o][c][:].rearrange("p d t -> p (d t)"))

        def store_words(o, cols):
            nc.sync.dma_start(out_1[o].rearrange("p d l -> p (d l)").bitcast(I32)[:, cols], out_codes[o][:, cols].bitcast(I32))

        gather_w(0)
        spread_ts()
        gather_w(1)
        turn_w(0, w_words[:, 0])
        copy_w(0)
        gather_w(2)
        gather_w(3)
        x_half0 = tile("x_half0", [P, 2, P, PACK], BF16)
        round_x(on_scalar, x_half0, x_raw[0], 0, 2 * P, 0)
        wn_codes = tile("wn_codes", [P, D], U32)
        quantise_turned(0)
        nc.vector.quantize_mx(wd_codes[:].bitcast(E4M3), wd_scales[:], w_listed[:].rearrange("p n j -> p (n j)"))
        quantise_x(0, x_half0)
        w_dealt = tile("w_dealt", [P, PACK, P], F32, "x_raw0")
        nc.scalar.copy(w_dealt[:].rearrange("p t s -> p s t"), w_words[:, 1].rearrange("p t s -> p s t"))

        score(0)
        score(1)
        sign(0)
        signed[1] = tile("signed1", [P, N], F32)[:]
        sign_aside(signed[1], y_pair[0][:, 1, :], VECTOR_SHARE)
        form_margin(0)
        turn_w(1, w_dealt)
        form_margin(1)
        x_half1 = tile("x_half1", [P, 2, P, PACK], BF16)
        for i in range(2):
            round_x(on_scalar, x_half1, x_raw[1], i * P, (i + 1) * P, i * HALF)
        clip(0)
        clip(1)
        copy_w(1)
        sign(2, "x_codes0")
        signed[3] = tile("signed3", [P, N], F32)[:]
        sign_aside(signed[3], y_pair[1][:, 1, :], 0)
        quantise_x(2, x_half1)
        score(2)
        score(3)
        for k in range(2):
            weigh(k)
            turn_h(k)
        form_margin(2)
        x_second = tile("x_second", [P, PACK, P, PACK], BF16)
        for i in range(2):
            round_x(on_scalar, x_second, x_raw[2], i * P, (i + 1) * P, i * P // PACK)
        clip(2)
        form_margin(3)
        clip(3)
        quantise_turned(1)
        round_x(on_vector, x_second, x_raw[3], 0, 2 * P, HALF)
        regroup(0)
        regroup(1)
        weigh(2)
        turn_h(2)
        quantise_x(PACK, x_second)
        score(4)
        weigh(3)
        turn_h(3)
        score(5)
        score(6)
        regroup(2)
        regroup(3)

        sign(4, "hinge2")
        signed_last = tile("signed_last", [P, 2 * N], F32)
        sign_aside(signed_last[:], y_pair[3][:].rearrange("r k n -> r (k n)"), VECTOR_SHARE)
        signed[6], signed[7] = signed_last[:, :N], signed_last[:, N:]
        sign(5, "signed3")
        form_margin(4)
        score(LAST)
        form_margin(5)
        clip(4)
        clip(5)

        quantise_h(0)
        gradient(0, 0, COLUMN_BANKS[1])
        gradient(0, 2, COLUMN_BANKS[0])
        quantise_h(1)
        for k, t in ((6, 1), (7, 3)):
            form_margin(k)
            weigh(k - 2)
            turn_h(k - 2)
            keep_warm(k)
            gradient(0, t, SCORE_BANKS[k % len(SCORE_BANKS)])
        empty(0, 0)
        clip(6)
        empty(0, 2)
        clip(LAST)
        regroup(4)
        regroup(5)
        empty(0, 1)
        weigh(6)
        turn_h(6)
        weigh(LAST)
        quantise_h(4)
        turn_h(LAST)

        gradient(1, 0, SCORE_BANKS[2])
        quantise_h(5)
        gradient(1, 1, TS_BANK)
        empty(0, 3)
        regroup(6)
        regroup(LAST)
        quantise_h(6)
        gradient(1, 2, COLUMN_BANKS[1])
        weave(on_vector, 0, 0)
        quantise_h(LAST)
        gradient(1, 3, COLUMN_BANKS[0])
        empty(1, 0)
        empty(1, 1)
        weave(on_vector, 0, 1)
        for c in range(2):
            quantise_out(0, c)
        empty(1, 2)
        store_words(0, slice(0, D))
        empty(1, 3, (0, HALF, P))
        weave(on_vector, 1, 0)
        weave(on_scalar, 1, 1, D // 2 - SCALAR_WEAVES, D // 2)
        weave(on_vector, 1, 1, 0, D // 2 - SCALAR_WEAVES)
        for c in range(2):
            quantise_out(1, c)
            store_words(1, slice(c * D // 2, (c + 1) * D // 2))

        for q in range(4):
            queue = nc.scalar if q % 2 == 0 else nc.sync
            queue.dma_start(out_2[:, 4 * q : 4 * q + 4, :].rearrange("o i d -> i o d").bitcast(I32),
                            out_scales[32 * q : 32 * q + 4].bitcast(I32))
